import numpy as np, ml_dtypes
CORES = [13,21,141,149]
N = 4
BF = ml_dtypes.bfloat16
W, NB, L, E, T, LIM, HOP, STR = 2048, 512, 256, 128, 6, 4, 3, 8
def among(rng, m, *s):
    i = rng.integers(0, m.shape[1], (N, 8) + s)
    return m[np.arange(8).reshape((1, 8) + (1,) * len(s)), i]
def parts(rng):
    rate = np.array([0.3, 0.6, 0.8, 0.93])[(np.arange(W) >> 4) & 3]
    rec = np.where(rng.random((N, 8, 16, W)) < rate, 9, rng.integers(0, 4, (N, 8, 16, W)))
    ver = rng.integers(0, W // 64, (N, 8, 16, NB)) * 64 + rng.integers(0, 3, (N, 8, 1, NB)) * 16 + rng.integers(0, 16, (N, 8, 16, NB))
    hot = rng.integers(0, W // 64, (8, 24)) * 64 + 48 + rng.integers(0, 16, (8, 24)); hb = rng.integers(0, NB, (8, 48)); s = (N, 8, 16, NB)
    known = np.where(rng.random(s) < 0.5, among(rng, hot, 16, NB), rng.integers(0, W // 64, s) * 64 + 48 + rng.integers(0, 16, s))
    stub = W + np.where(rng.random(s) < 0.5, among(rng, hb, 16, NB), rng.integers(0, NB, s))
    edge = np.where(rng.random(s) < 0.4, known, stub)
    eff = rng.integers(0, 4, (N, 8, 16, E)) * rng.integers(0, 2, (N, 8, 16, E)); x = rng.integers(0, 4, (N, 8, 16, L))
    v = np.where(rng.random((N, 8, L)) < 0.5, among(rng, hot, L), rng.integers(0, W, (N, 8, L)))
    return rec, ver, edge, eff, x, v
def own(rng, a, g, dd, lo=0):
    rec, ver, edge, eff, x, v = a; i = np.arange(L)
    v[:, g] = i; edge[:, g, :, :L] = W + i
    ver[:, g, :, :L] = STR * i + (np.arange(16)[:, None] + rng.integers(0, STR)) % STR
    far = np.argsort(rng.random((N, 16 - lo, L, STR)), axis=1) < dd.reshape(N, 1, L, -1); xx = x[:, g][:, :, :, None]
    far = np.concatenate([np.zeros((N, lo, L, STR), bool), far], axis=1)
    rec[:, g] = np.where(far, (xx + rng.integers(1, 4, far.shape)) & 3, xx).reshape(N, 16, W)
def two(a, g):
    rec, ver, edge, eff, x, v = a
    x[:, g] = 0; x[1::2, g, :LIM + 1] = 1; eff[:, g] = 0
def pack(a):
    rec, ver, edge, eff, x, v = [np.ascontiguousarray(z) for z in a]
    return {"rec0": rec.reshape(N, 128, W).astype(BF), "ver0": ver.reshape(N, 128, NB).astype(np.int32), "edge0": edge.reshape(N, 128, NB).astype(np.int32),
            "eff": eff.reshape(N, 128, E).astype(BF), "x0": x.reshape(N, 128, L).astype(BF), "v0": v.astype(np.int32)}
def setup_inputs(rng):
    return pack(parts(rng))
def skew(rng, hi, *s):
    e = rng.choice(np.array([1.0, 3.0, 8.0]), (N, 8) + (1,) * len(s))
    return np.minimum(((hi + 1) * rng.random((N, 8) + s) ** e).astype(np.int64), hi)
def setup_inputs_spread(rng):
    ex = rng.choice(np.array([0.5, 1.0, 2.0, 4.0]), (1, 8, 16, 1))
    val = np.minimum((4 * rng.random((N, 8, 16, W)) ** ex).astype(np.int64), 3)
    rec = np.where(rng.random((N, 8, 16, W)) < 0.75 * rng.random((N, 8, 1, W)), 9, val)
    x = np.minimum((4 * rng.random((N, 8, 16, L)) ** ex).astype(np.int64), 3)
    edge = np.where(rng.random((N, 8, 16, NB)) < rng.choice(np.array([0.1, 0.4, 0.7]), (N, 8, 1, 1)), skew(rng, W - 1, 16, NB), W + skew(rng, NB - 1, 16, NB))
    return pack((rec, skew(rng, W - 1, 16, NB), edge, skew(rng, 3, 16, E), x, skew(rng, W - 1, L)))
def end(rng, lo, hi, *s):
    return np.where(rng.random((N, 8) + s) < 0.5, lo, hi)
def setup_inputs_ends(rng):
    rec = end(rng, 0, 9, 16, W); ver = end(rng, 0, W - 1, 16, NB); edge = end(rng, 0, W + NB - 1, 16, NB); eff = end(rng, 0, 3, 16, E); x = end(rng, 0, 3, 16, L); v = end(rng, 0, W - 1, L)
    for g in (1, 3, 5):
        ver[:, g] = np.where(rng.random((N, 16, NB)) < 0.3, rng.integers(0, W, (N, 16, NB)), ver[:, g])
        edge[:, g] = np.where(rng.random((N, 16, NB)) < 0.3, rng.integers(0, W + NB, (N, 16, NB)), edge[:, g])
        v[:, g] = np.where(rng.random((N, L)) < 0.3, rng.integers(0, W, (N, L)), v[:, g])
    for g in (0, 7):
        rec[:, g, :, 0] = 0; rec[:, g, :, W - 1] = 0
        m = rng.random((N, 1, L)); x[:, g] = np.where(m < 0.25, 3, np.where(m < 0.5, 0, x[:, g]))
        x[:, g, :, L - 1] = 3; v[:, g, L - 1] = W - 1
    edge[:, 7, :, NB - 1] = W + NB - 1; edge[:, 7, :, 0] = 0
    x[N - 1, 7] = 0; x[N - 1, 7, :, L - 1] = 3
    return pack((rec, ver, edge, eff, x, v))
def setup_inputs_corners(rng):
    a = parts(rng); rec, ver, edge, eff, x, v = a
    ver[:, 0] = 0; ver[:, 1] = W - 1; rec[:, 1, :, W - 1] = rng.integers(0, 4, (N, 16))
    v[:, 2] = rng.integers(0, NB, (N, L)); edge[:, 2] = np.arange(NB); rec[:, 2, :, ::2] = 9
    edge[:, 3] = W + rng.integers(0, NB, (N, 16, NB)); ver[:, 3] = ver[:, 3] // STR * STR + rng.integers(0, T, (N, 16, NB)) * rng.integers(0, 2, (N, 16, NB))
    v[:, 3] = STR * np.argsort(rng.random((N, L)), axis=1) + rng.integers(0, 2, (N, L)) * rng.integers(0, T, (N, L))
    dd = np.repeat(rng.choice(np.array([0, 1, LIM, LIM + 1, LIM + 2, 16]), (N, L, 1)), STR, axis=2)
    dd[:, 3::4] = 16; dd[:, 3::4, STR - 1] = 15
    own(rng, a, 4, dd)
    i = np.arange(3, L, 4); kk = np.arange(16)[:, None]; p = np.where(rng.random((N, 1, len(i))) < 0.5, 15, rng.integers(0, 16, (N, 1, len(i))))
    ver[:, 4, :, 3:L:4] = np.where(kk == p, STR * i + STR - 1, STR * i + kk % (STR - 1))
    edge[:, 5] = W + rng.choice(np.array([0, NB - 1]), (N, 16, NB)); rec[:, 5, :, 0] = 9
    two(a, 6); own(rng, a, 6, rng.integers(0, LIM + 1, (N, L)), LIM + 1)
    fit = np.where((rng.random((N, 16, L + 1)) < 0.3) & (kk > LIM), 9, x[:, 6, :, :1])
    rec[:, 6, :, ::STR] = fit[:, :, :L]; rec[:, 6, :, W - 1] = fit[:, :, L]
    edge[:, 6] = np.where(rng.random((N, 16, NB)) < 0.5, rng.choice(np.array([0, W - 1]), (N, 16, NB)), STR * rng.integers(0, L, (N, 16, NB)))
    edge[1::2, 6, :, L - 1] = W + L - 1
    rec[:, 7] = rng.integers(0, 4, (N, 16, W))
    return pack(a)
def setup_inputs_crowd(rng):
    a = parts(rng); rec, ver, edge, eff, x, v = a; full = np.full((N, L), 16); less = full.copy(); less[:, L - 1] = 0
    soft = rng.integers(1, LIM + 1, (N, L)); soft[1::2, L - 1] = 0
    rec[:, 2:7] = np.where(rng.random((N, 5, 16, W)) < 0.5, 9, rng.integers(0, 4, (N, 5, 16, W)))
    two(a, 0); two(a, 1); two(a, 7)
    own(rng, a, 0, soft, LIM + 1); own(rng, a, 1, less); own(rng, a, 7, full)
    edge[:, 2:4] = W + rng.integers(0, NB, (N, 2, 16, NB))
    x[:, 2] = x[:, 2, :, :1].copy(); v[:, 2] = v[:, 2, :1].copy()
    x[:, 3, :, :L - 1] = x[:, 3, :, :1].copy(); v[:, 3, :L - 1] = v[:, 3, :1].copy()
    v[:, 4] = v[:, 4, :1].copy(); edge[:, 4] = W + rng.integers(0, NB, (N, 1, 1))
    edge[:, 5] = W + NB - 1; v[:, 5] = np.argsort(rng.random((N, W)), axis=1)[:, :L]
    v[:, 6] = np.arange(L); edge[:, 6, :, :L] = W + np.arange(L); ver[:, 6] = W - 1; ver[:, 6, :, L - 1] = 5
    return pack(a)
def check_inputs(d):
    bad = []
    for k, lo, hi in (("rec0", 0, 9), ("ver0", 0, W - 1), ("edge0", 0, W + NB - 1), ("eff", 0, 3), ("x0", 0, 3), ("v0", 0, W - 1)):
        a = np.asarray(d[k]).astype(np.float64)
        if not (np.min(a) >= lo and np.max(a) <= hi and np.all(a == np.floor(a))): bad.append("range of " + k)
    a = np.asarray(d["rec0"]).astype(np.float64)
    if np.any((a > 3) & (a < 9)): bad.append("rec0 holds a number between 3 and 9")
    return bad
def reference(rec0, ver0, edge0, eff, x0, v0):
    R = np.asarray(rec0).astype(np.int32).reshape(N, 8, 16, W); V = np.asarray(ver0).astype(np.int32).reshape(N, 8, 16, NB)
    S = np.tile(np.asarray(edge0).astype(np.int32).reshape(N, 8, 16, NB), (1, 1, 1, W // NB)); ef = np.asarray(eff).astype(np.int32).reshape(N, 8, 16, E)
    x = np.asarray(x0).astype(np.int32).reshape(N, 8, 16, L); v = np.asarray(v0).astype(np.int32); A = np.zeros((N, 8), np.int32)
    lane = np.arange(L); low = lane[None, :] < lane[:, None]; wt = (2 * np.arange(16) + 1)[:, None]
    for t in range(T):
        for q in range(N):
            r = (q - HOP * t) % N
            for g in range(8):
                Rg, Vg, Sg, xx, vv = R[q, g], V[q, g], S[q, g], x[r, g], v[r, g].copy()
                j = np.sum(wt * xx, axis=0) & 15; w = Sg[j, vv]; rw = Rg[:, w & (W - 1)]
                known = (w < W) & ~np.any((rw != xx) & (rw != 9), axis=0)
                b = w & (NB - 1); ver = Vg[:, b]; old = Rg[:, ver]
                mis = np.sum((old != xx[:, None, :]) & (old != 9), axis=0); k = np.argmin(mis, axis=0)
                d = mis[k, lane]; c = ver[k, lane]
                want = ~known & (d > 0)
                clash = low & want[None, :] & ((b[:, None] == b[None, :]) | (c[:, None] == c[None, :]))
                may = want & ~np.any(clash, axis=1)
                gen = may & (d <= LIM + (A[q, g] & 1)); cl = may & ~gen
                rc = Rg[:, c]; new = np.where(rc == xx, rc, 9); n = STR * lane + t
                eat = np.all((new[:, None, :] == 9) | (old == new[:, None, :]), axis=0)
                vn = np.where(known, w, np.where(cl, n, c)); sc = W + (Sg[:, c] & (NB - 1))
                Rg[:, c[gen]] = new[:, gen]; Rg[:, n[cl]] = xx[:, cl]
                Vg[:, b[gen]] = np.where(eat, c[None, :], ver)[:, gen]; Vg[(lane[cl] + t) & 15, b[cl]] = n[cl]
                Sg[:, n[cl]] = sc[:, cl]
                first = ~np.any(low & (vv[:, None] == vv[None, :]), axis=1)
                Sg[j[first], vv[first]] = vn[first]
                x[r, g] = (xx + ef[q, g][:, vn & (E - 1)]) & 3; v[r, g] = vn; A[q, g] = np.count_nonzero(cl)
    return {"yr": R.reshape(N, 128, W).astype(np.float32).astype(BF), "yl": V.reshape(N, 128, NB).astype(np.float32), "ys": np.sum(S, axis=2).astype(np.float32),
            "yx": x.reshape(N, 128, L).astype(np.float32).astype(BF), "yv": v.astype(np.float32)}

@@ -1,0 +1,715 @@
+import math
+from concourse.mybir import AluOpType as ALU, ActivationFunctionType as AF
+
+NT = 6
+HOP = 3
+SW = 608
+PARTS = ((288, 544), (0, 288), (576, 592))
+GV = 32
+GATHER, SCATTER, PE, WAKE, SLACK, HOPS = 1.5, 3.8, 0.5, 60.0, 70.0, (6000.0, 6000.0, 4600.0)
+KWV = True
+EQV = True
+AHEAD = 300
+ORDER = {}
+VOID = float(2 ** 30)
+LN3 = math.log(3.0)
+
+F, B, H, I, U = "float32", "bfloat16", "float16", "int32", "uint16"
+SCRATCH = {}
+for _d, _l in (
+    (B, "land:%d msg:%d " % (NT * SW, NT * SW) +
+        "R:2576 EF:2048 IP:800 G:4096 EQ:4096 Ea:4096 Eb:4096 sel:2048 selj:2048 sel0:2048 sel1:2048 selg:1024 rw:576 idb:128 "
+        "id2:128 id5:128 idp:128 bo:128 bo0:128 bo1:128 bofd:128 zer:512 c2k:256 kc:128 b8:32 xm:256 pw:8 tmpb:800 tmpc:1024 "
+        "tmpd:256 reci:2048 jm:256 kw:512 brep:256 x2:128 x2v:128 rc:256 eqc:256 t30:256 fd:256 ex:256 sg:256 sgb:256 "
+        "sb:256 sq:256 ay:8"),
+    (F, "SU:2560 VL:768 IOT:2048 idf:128 nidf:128 seg:128 tm:128 b8f:8 col:16 wex:16 tmpf:128 lane:16 cb:64 cd:64 key:64 dif:64 "
+        "td:64 cfd:8 j0:48 jd:48 jf:48 wW:16 verf:256 repf:256 ta:16 tb:16 tc:16 te:32 nk:16 thw:16 mn:256 want:16 far:16 wf:16 "
+        "base:16 dl:16 vn:16 suc:256 vnr:256 old:256 p2:256 sf:256 mm:256 pr:256 an:16 ac:8 tha:8 yso:256"),
+    (H, "prod:256 rep:256 repv:256 x1:256"), (B, "Ev:4096"), (F, "repg:256"),
+    (I, "coli:4 edi:512 vei:512 v0i:256 ei:16 bi:16 si:16 lm:32 di:512 dy:512"),
+    (U, "xl:16 jvL:48 bL:32 verL:256 cL:16 c2L:32 vnL:32 wrL:64"),
+):
+    for _w in _l.split():
+        SCRATCH[_w.split(":")[0]] = ("sbuf", [128, int(_w.split(":")[1])], _d)
+for _k in range(8):
+    SCRATCH["P%d" % _k] = ("psum", [128, 512], F)
+NDMA = 24
+SEMAPHORES = (["cv", "cs", "cp", "cg", "sent"] + ["arr%d_%d" % (t, k) for t in range(NT) for k in range(3)]
+              + ["dm%d" % k for k in range(NDMA)])
+
+
+def mask_of(engines):
+    return sum(1 << e for e in engines)
+
+
+def route(T, topo):
+    n = len(T.cores)
+    out = []
+    for r, c in enumerate(T.cores):
+        dsts = [T.cores[(r + HOP) % n]] * (NT - 1) + [T.cores[(r - HOP * (NT - 1)) % n]]
+        able = [h for h in topo.cores_of(c) if h not in T.cores and all(topo.may_write(h, d) for d in dsts)]
+        able.sort(key=lambda h: topo.die(h) != topo.die(c))
+        ea, eb = topo.engines(c, able[0]), topo.engines(c, able[1])
+        early, late = (able[0], ea[:len(ea) // 2]), (able[1], eb[len(eb) // 2:])
+        out.append((c, dsts, (early, early, late)))
+    return out
+
+
+def relay_program(g, core, T, topo, dsts, hops):
+    total = 0
+    for t in range(NT):
+        rid, pid = topo.addr(dsts[t], core)
+        for k, (h, eng) in enumerate(hops):
+            if h == core:
+                piece = T.land[:, t * SW + PARTS[k][0]:t * SW + PARTS[k][1]]
+                s = T.sem["arr%d_%d" % (t, k)]
+                g.wait_ge(s, len(eng))
+                g.remote_dma(piece, piece, s, T.sem.sent, pid, rid, topo.mask(core, dsts[t]))
+                total += len(topo.engines(core, dsts[t]))
+    g.wait_ge(T.sem.sent, total)
+
+
+def schedule(ops, full):
+    n = len(ops)
+    succ = [[] for _ in range(n)]
+    for i, d in enumerate(full):
+        for m in d:
+            succ[m].append(i)
+    eng = [o[0] for o in ops]
+    left = [len(d) for d in full]
+    ready = [0.0] * n
+    cand = {e: set() for e in set(eng)}
+    for i in range(n):
+        if not left[i]:
+            cand[eng[i]].add(i)
+    free = {e: 0.0 for e in cand}
+    order, done = [], [False] * n
+
+    def issue(i):
+        e = eng[i]
+        st = max(free[e], ready[i])
+        cand[e].discard(i)
+        done[i] = True
+        order.append(i)
+        free[e] = st + ops[i][5][0]
+        for s in succ[i]:
+            ready[s] = max(ready[s], free[e] + ops[i][5][1] + (0 if eng[s] == e == "p" else WAKE))
+            left[s] -= 1
+            if not left[s]:
+                cand[eng[s]].add(s)
+
+    def soonest(i, depth, memo):
+        if not left[i] or not depth:
+            return ready[i]
+        if i not in memo:
+            memo[i] = max([ready[i]] + [max(free[eng[m]], soonest(m, depth - 1, memo)) + ops[m][5][0] + ops[m][5][1]
+                                        + (0 if eng[m] == eng[i] == "p" else WAKE) for m in full[i] if not done[m]])
+        return memo[i]
+
+    rest = {e: [i for i in range(n) if eng[i] == e] for e in cand}
+    clock = dict(free)
+    while len(order) < n:
+        e = min((k for k in cand if cand[k]), key=lambda k: (max(clock[k], min(ready[i] for i in cand[k])), k))
+        now = max(clock[e], min(ready[i] for i in cand[e]))
+        while done[rest[e][0]]:
+            rest[e].pop(0)
+        memo, limit, pick = {}, 1e18, None
+        for i in rest[e][:AHEAD]:
+            if done[i]:
+                continue
+            if not left[i] and ready[i] <= now and now + ops[i][5][0] <= limit + SLACK:
+                pick = i
+                break
+            if not [m for m in full[i] if not done[m] and eng[m] == e]:
+                limit = min(limit, max(now, soonest(i, 12, memo)))
+        if pick is None:
+            later = [ready[i] for i in cand[e] if ready[i] > now] + [limit]
+            nxt = min(later)
+            if nxt > now:
+                clock[e] = nxt
+                continue
+            clock[e] = now + 20.0
+            continue
+        free[e] = max(free[e], now)
+        issue(pick)
+        clock[e] = free[e]
+    return order
+
+
+def emit(g, T, ops):
+    q = {"v": g.vector, "s": g.scalar, "p": g.tensor, "g": g, "y": g.sync}
+    sem = {"v": T.sem.cv, "s": T.sem.cs, "p": T.sem.cp, "g": T.sem.cg}
+    lastw, readers, bank, full, deps, need = {}, {}, {}, [], {}, set()
+    for n, (e, fn, rd, wr, kind, cost) in enumerate(ops):
+        d = set()
+        for r in rd + wr:
+            if r[0] == "@":
+                eng, now, before = bank.get(r, (e, [], []))
+                if eng != e:
+                    now, before = [], now
+                d.update(before)
+                if e == "p":
+                    d.update(now[-1:])
+                bank[r] = (e, now + [n], before)
+        for r in rd:
+            if r in lastw:
+                d.add(lastw[r])
+        for w in wr:
+            if w[0] != "@":
+                if w in lastw:
+                    d.add(lastw[w])
+                d.update(readers.get(w, []))
+        for r in rd:
+            if r[0] != "@":
+                readers.setdefault(r, []).append(n)
+        for w in wr:
+            if w[0] != "@":
+                lastw[w] = n
+                readers[w] = []
+        d.discard(n)
+        full.append(d)
+    if len(ops) not in ORDER:
+        ORDER[len(ops)] = schedule(ops, full)
+    order = ORDER[len(ops)]
+    pos = {n: k for k, n in enumerate(order)}
+    for n in order:
+        top = {}
+        for m in full[n]:
+            e2, k2 = ops[m][0], ops[m][4]
+            if k2 == "c":
+                if not (e2 == "p" and ops[n][0] == "p") and pos[m] > pos.get(top.get(e2), -1):
+                    top[e2] = m
+            elif k2 != "r":
+                top[("x", m)] = m
+        deps[n] = sorted(top.values())
+        need.update(top.values())
+    cnt = {k: 0 for k in sem}
+    tok, seen, ndma, ends = {}, {k: {} for k in q}, 0, []
+    for n in order:
+        e, fn, rd, wr, kind, cost = ops[n]
+        for m in deps[n]:
+            name, s, val = tok[m]
+            if seen[e].get(name, 0) < val:
+                q[e].wait_ge(s, val)
+                seen[e][name] = val
+        if kind == "c":
+            ins = fn()
+            if n in need:
+                cnt[e] += 1
+                ins.then_inc(sem[e], 1)
+                tok[n] = (e, sem[e], cnt[e])
+        elif kind == "d":
+            s = T.sem["dm%d" % ndma]
+            fn().then_inc(s, 16)
+            tok[n] = ("dm%d" % ndma, s, 16)
+            ends.append((e, tok[n]))
+            ndma += 1
+        elif kind == "r":
+            fn()
+        else:
+            tok[n] = kind
+    for e, (name, s, val) in ends:
+        if max(seen[k].get(name, 0) for k in q) < val:
+            q[e].wait_ge(s, val)
+
+
+def rank_program(g, core, T, topo):
+    rt = route(T, topo)
+    rank = T.rank_of(core)
+    if rank is None:
+        for c, dsts, hops in rt:
+            if core in [h for h, eng in hops]:
+                relay_program(g, core, T, topo, dsts, hops)
+        return
+    me, dsts, hops = rt[rank]
+    ops = []
+    V, S, P = g.vector, g.scalar, g.tensor
+
+    def op(e, fn, rd, wr, kind="c", cost=(64.0, 0.0)):
+        ops.append((e, fn, rd.split(), wr.split(), kind, cost))
+
+    def two(a):
+        return "16" in str(a.dtype)
+
+    def sides(out, a, per, rd=""):
+        names = rd.split()
+        if names[:1] == ["wrL"]:
+            return (50.0 + SCATTER * a.shape[1], 0.0)
+        if len(names) > 1 and [w for w in names if w[-1] == "L" and w != "VL" or w == "xl"]:
+            return (60.0 + GATHER * out.shape[1], 0.0)
+        if per == 0:
+            per = 0.5 if two(out) and two(a) else 1.0
+        return (max(64.0, per * a.shape[1]), 0.0)
+
+    def tt(out, a, b, o, rd, wr):
+        op("v", lambda: V.tensor_tensor(out, a, b, o), rd, wr, "c", sides(out, a, 1.0 if "@" in rd else 2.0, rd))
+
+    def ts(out, a, s1, o1, rd, wr, s2=None, o2=None):
+        c = sides(out, a, 0)
+        if o2 is None:
+            op("v", lambda: V.tensor_scalar(out, a, s1, None, o1), rd, wr, "c", c)
+        else:
+            op("v", lambda: V.tensor_scalar(out, a, s1, s2, o1, o2), rd, wr, "c", c)
+
+    def cp(out, a, rd, wr):
+        op("v", lambda: V.tensor_copy(out, a), rd, wr, "c", sides(out, a, 0, rd))
+
+    def ms(out, val, wr):
+        op("v", lambda: V.memset(out, val), "", wr, "c", sides(out, out, 0))
+
+    def scan(out, a, b, rd, wr):
+        op("v", lambda: V.tensor_tensor_scan(out, a, b, 0.0, ALU.add, ALU.min), rd, wr, "c", sides(out, a, 1.0))
+
+    def act(out, a, rd, wr, func=AF.Identity, bias=0.0, scale=1.0, acc=None):
+        c = sides(out, a, 1.0, rd)
+        op("s", lambda: S.activation(out, a, func, bias=bias, scale=scale, accum_out=acc), rd, wr, "c", c)
+
+    def mm(out, l, r, st, sp, rd, wr):
+        c = PE * max(min(64, l.shape[1]), r.shape[1]) * (1 if two(l) else 4)
+        op("p", lambda: P.matmul(out, l, r, st, sp), rd, wr, "c", (c, 0.0))
+
+    def mmf(bank, at, l, r, sp, rd, wr):
+        for k in range(4):
+            mm(bank[:, at + 64 * k:at + 64 * k + 64], l[:], r[:, 64 * k:64 * k + 64], False, sp and k == 3, rd, wr)
+
+    def iota(out, pat, base, cm, wr, small=True):
+        c = (130.0 + 2.0 * out.shape[1], 0.0)
+        if small:
+            op("g", lambda: g.iota(out, pat, base, cm, allow_small_or_imprecise_dtypes=True), "", wr, "c", c)
+        else:
+            op("g", lambda: g.iota(out, pat, base, cm), "", wr, "c", c)
+
+    def dma(e, out, a, rd, wr):
+        qq = g.sync if e == "y" else g.scalar
+        op(e, lambda: qq.dma_start(out, a), rd, wr, "d", (100.0, 2000.0 + a.shape[0] * a.shape[1] * (2 if two(a) else 4) / 200.0))
+
+    nsent = [0]
+
+    def send(t, k, rd):
+        h, eng = hops[k]
+        rid, pid = topo.addr(h, core)
+        a, b = t * SW + PARTS[k][0], t * SW + PARTS[k][1]
+        nsent[0] += len(eng)
+        op("g", lambda: g.remote_dma(T.land[:, a:b], T.msg[:, a:b], T.sem["arr%d_%d" % (t, k)], T.sem.sent, pid, rid, mask_of(eng)),
+           rd, "S%d_%d" % (t, k), "r", (500.0, 0.0))
+
+    def arrive(t, k):
+        h = [hp for c, ds, hp in rt if ds[t] == core][0][k][0]
+        nm = "arr%d_%d" % (t, k)
+        op("x", None, "S%d_%d" % (t, k), "L%d_%d" % (t, k), (nm, T.sem[nm], len(topo.engines(h, core))), (0.0, HOPS[k]))
+
+    def wrap(out, lhs, src_of, rd, wr):
+        for p in range(16):
+            mm(out, lhs[:, 128 * p:128 * p + 128], src_of(p), p == 0, p == 15, rd, wr)
+
+    def unlane(out, src_of, rd, wr):
+        for k in range(8):
+            mm(out, T.selg[:, 128 * k:128 * k + 128], src_of(k), k == 0, k == 7, rd + " selg", wr)
+
+    def dword(w, h, k):
+        sw = T.sel1 if w else T.sel0
+        mm(T.P6[:, 256 * w + 128 * h:256 * w + 128 * h + 128], sw[:, 128 * k:128 * k + 128],
+           T.EQ[:, 256 * k + 128 * h:256 * k + 128 * h + 128], False, False,
+           ("EQb%d EQc%d" % (k, k) if h else "EQa%d" % k) + " sel%d" % w, "@6 D")
+
+    def pairs(E, en, keyrep, key, gate, bank, bn, rd, last, extra=(), hooks={}):
+        extra = list(extra)
+        for c in range(16):
+            lo = 0 if c < 4 else 64 if c < 8 else 128
+            o = E[:, 256 * c + lo:256 * c + 256]
+            nm = "%s%d" % (en, c)
+            kcol = T.key[:, key + c:key + c + 1]
+            if gate is None:
+                ts(o, keyrep[:, lo:256], kcol, ALU.is_equal, rd, nm)
+            else:
+                ts(o, keyrep[:, lo:256], kcol, ALU.is_equal, rd, nm, gate[:, c:c + 1], ALU.mult)
+            w = T.rw[:, 64 * (c % 8):64 * (c % 8) + 64]
+            if c < 8:
+                mm(bank[lo:128, 0:64], E[:, 256 * c + lo:256 * c + 128], w, False, False, nm + " rw", bn)
+                w = T.rw[:, 512:576]
+            mm(bank[:, 64:128], E[:, 256 * c + 128:256 * c + 256], w, False, last and c == 15, nm + " rw", bn)
+            if extra:
+                dword(*extra.pop(0))
+            if c in hooks:
+                hooks[c]()
+
+    x = T.R[:, 2304:2560]
+    pm, pg = T.col[:, 1:2], T.col[:, 2:3]
+    dma("y", x, T.x0[:], "", "Rx")
+    dma("y", T.edi[:], T.edge0[:], "", "edi")
+    ms(T.v0i[:], 0, "v0i")
+    dma("s", T.v0i[0:128:16, :], T.v0[:], "v0i", "v0i")
+    dma("s", T.reci[:, 0:1024], T.rec0[:, 0:1024], "", "reci0")
+    dma("y", T.reci[:, 1024:2048], T.rec0[:, 1024:2048], "", "reci1")
+    dma("y", T.vei[:], T.ver0[:], "", "vei")
+    dma("y", T.EF[:, 0:128], T.eff[:], "", "EF")
+    iota(T.coli[:, 0:1], [[0, 1]], 0, 1, "coli0", False)
+    iota(T.xm[:], [[0, 32], [1, 8]], 0, 0, "xm")
+    iota(T.wex[:, 0:8], [[16, 8]], 0, 0, "wex")
+    iota(T.tmpb[:, 16:800], [[0, 49], [1, 16]], 0, 0, "tb16")
+    iota(T.tmpf[:], [[1, 128]], 0, -1, "tmpf")
+    iota(T.IOT[:], [[1, 2048]], -2048, 0, "IOT")
+    iota(T.zer[:], [[0, 512]], 0, 0, "zer")
+    iota(T.kc[:], [[0, 8], [2048, 16]], 0, 0, "kc")
+    iota(T.tmpc[:], [[-16, 8], [16, 8], [1, 16]], 0, 0, "tmpc")
+    iota(T.tm[:], [[0, 2], [1, 8], [0, 8]], 0, 0, "tm")
+    iota(T.tmpd[:, 0:128], [[1, 8], [0, 16]], 0, 0, "tmpd")
+    iota(T.lane[:], [[16, 16]], 0, 0, "lane")
+    iota(T.tc[:], [[1, 8], [16, 2]], 0, 0, "tc")
+    for buf, val, nm in ((T.seg[:], 0, "seg"), (T.seg[:, 0::16], 2 ** 22, "seg"), (T.R[:, 2048:2304], 0, "Rz"), (T.R[:, 2560:2576], 5, "R5"),
+                         (T.IP[:, 784:800], 0, "IPz"), (T.key[:, 32:48], 0, "key2"), (T.SU[:, 2048:2304], 0, "SUz"),
+                         (T.c2k[:], 2048, "c2k"), (T.jd[:, 32:48], PARTS[0][0], "jd2"), (T.VL[:, 512:768], 0, "VLz")):
+        iota(buf, [[0, buf.shape[1]]], val, 0, nm)
+    ms(T.sel[:], 0.0, "sel")
+    ts(T.coli[:, 1:2], T.coli[:, 0:1], 15, ALU.bitwise_and, "coli0", "coli1")
+    ts(T.coli[:, 2:3], T.coli[:, 0:1], 4, ALU.arith_shift_right, "coli0", "coli2")
+    ts(T.coli[:, 3:4], T.coli[:, 0:1], 7, ALU.bitwise_and, "coli0", "coli3")
+    cp(T.col[:, 0:4], T.coli[:, 0:4], "coli0 coli1 coli2 coli3", "col")
+    ts(T.xm[:], T.xm[:], pg, ALU.is_equal, "xm col", "xm")
+    ts(T.col[:, 4:5], pm, 2.0, ALU.mult, "col", "col4", 1.0, ALU.add)
+    b8 = T.xm[:, 0:8]
+    for p in range(16):
+        cp(T.sel[:, 129 * p:128 * p + 128:16], b8, "xm sel", "sel_%d" % p)
+    selall = " ".join("sel_%d" % p for p in range(16))
+    ts(T.col[:, 5:6], pm, -LN3, ALU.mult, "col", "col5", 56 * LN3, ALU.add)
+    ts(T.col[:, 6:7], T.col[:, 0:1], -LN3, ALU.mult, "col", "col6", 56 * LN3 + math.log(3.5), ALU.add)
+    act(T.pw[:, 0:1], T.col[:, 3:4], "col", "pw", AF.Exp, scale=math.log(4.0))
+    act(T.ex[:], x, "Rx col4", "ex", scale=T.col[:, 4:5])
+    cp(T.prod[:], T.v0i[:], "v0i", "prod")
+    act(T.wex[:, 8:16], T.wex[:, 0:8], "wex col5", "wex2", AF.Exp, bias=T.col[:, 5:6], scale=-LN3)
+    act(T.col[:, 7:8], T.col[:, 6:7], "col6", "col7", AF.Exp)
+    ts(T.SU[:, 0:512], T.edi[:], -2048.0, ALU.add, "edi", "SU")
+    ts(T.IP[:, 0:784], T.tmpb[:, 16:800], pm, ALU.is_equal, "tb16 col", "IP")
+    act(T.SU[:, 512:1024], T.SU[:, 0:512], "SU", "SUb")
+    ts(T.idb[:], T.tmpf[:], 0.0, ALU.is_equal, "tmpf", "idb")
+    for k in range(4):
+        n = 128 << k
+        dma("y", T.EF[:, n:2 * n], T.EF[:, 0:n], "EF", "EF")
+
+    def init_records():
+        ts(T.SU[:, 1024:1536], T.edi[:], -2048.0, ALU.add, "edi", "SUd")
+        act(T.SU[:, 1536:2048], T.SU[:, 0:512], "SU", "SUe")
+        ts(T.G[:, 0:1024], T.reci[:, 0:1024], 8.0, ALU.is_ge, "reci0", "G0", VOID, ALU.mult)
+
+    def init_records_2():
+        ts(T.G[:, 1024:2048], T.reci[:, 1024:2048], 8.0, ALU.is_ge, "reci1", "G1 Gv", VOID, ALU.mult)
+        for k in range(4):
+            bk = T["P%d" % (4 + k)]
+            mm(bk[:], T.idb[:], T.reci[:, 512 * k:512 * k + 512], True, False, "idb reci%d" % (k // 2), "@%d" % (4 + k))
+            mm(bk[:], T.idb[:], T.G[:, 512 * k:512 * k + 512], False, True, "idb G0" if k < 2 else "idb G1 Gv", "@%d ri%d" % (4 + k, k))
+        for k in range(4):
+            o, i = T.R[:, 512 * k:512 * k + 512], T["P%d" % (4 + k)][:]
+            (act if k < 3 else cp)(o, i, "@%d ri%d" % (4 + k, k), "R" if k == 3 else "Ri%d" % k)
+            if k == 2:
+                cp(T.VL[:, 0:512], T.vei[:], "vei", "VL")
+
+    def constants_1():
+        ts(T.idf[:], T.tmpf[:], 0.0, ALU.is_equal, "tmpf", "idf")
+        ts(T.b8[:, 8:16], b8, -32768.0, ALU.mult, "xm", "b8e")
+        ts(T.b8[:, 16:24], b8, -1.0 / 32768.0, ALU.mult, "xm", "b8v")
+        ts(T.rw[:, 512:576], T.xm[:, 0:64], float(2 ** 95), ALU.mult, "xm", "rwB")
+        for k in range(8):
+            ts(T.rw[:, 64 * k:64 * k + 64], T.xm[:, 0:64], T.wex[:, 8 + k:9 + k], ALU.mult, "xm wex2", "rw" if k == 7 else "rw_%d" % k)
+        ops[-1][2].extend(["rwB"] + ["rw_%d" % k for k in range(7)])
+
+    def constants_2():
+        ts(T.selg[:], T.tmpc[:], pm, ALU.is_equal, "tmpc col", "selg")
+        ts(T.tm[:], T.tm[:], pg, ALU.is_equal, "tm col col7", "tm", T.col[:, 7:8], ALU.mult)
+        ts(T.col[:, 8:9], pm, 8.0, ALU.is_ge, "col", "col8", 8.0, ALU.mult)
+        ts(T.lane[:], T.lane[:], pm, ALU.add, "lane col", "lane")
+        ts(T.xl[:], T.tc[:], T.col[:, 8:9], ALU.add, "tc col8", "xl")
+        ms(T.tha[:], -11.5, "tha")
+        ts(T.id2[:], T.idb[:], -2.0, ALU.mult, "idb", "id2")
+        ts(T.idp[:], T.idb[:], 2.0, ALU.mult, "idb", "idp")
+        ts(T.col[:, 9:10], pm, 8.0, ALU.is_lt, "col pw", "col9", T.pw[:, 0:1], ALU.mult)
+        ts(T.col[:, 10:11], T.col[:, 8:9], 0.25, ALU.mult, "col8 pw", "col10", T.pw[:, 0:1], ALU.mult)
+        ts(T.bo[:], T.tmpd[:, 0:128], pg, ALU.is_equal, "tmpd col", "bo")
+        ts(T.col[:, 11:13], T.col[:, 9:11], -1.0, ALU.mult, "col9 col10", "col11")
+        ts(T.cfd[:, 0:1], pm, -784.0, ALU.add, "col", "cfd", 1.0 / 4096.0, ALU.mult)
+        ts(T.cb[:, 32:48], T.lane[:], 8.0, ALU.mult, "lane", "cb2")
+        ts(T.id5[:], T.idb[:], -512.0, ALU.mult, "idb", "id5")
+
+    def constants_3():
+        for k, bi in ((0, 2048.0), (1, 512.0), (3, 2048.0)):
+            act(T.cb[:, 16 * k:16 * k + 16], T.lane[:], "lane", "cb%d" % k, bias=bi)
+        for k, (sc, bi) in enumerate(((1.0, 0.0), (1.0, 256.0), (7.0, -2304.0), (1.0, 0.0))):
+            act(T.cd[:, 16 * k:16 * k + 16], T.lane[:], "lane", "cd%d" % k, bias=bi, scale=sc)
+        act(T.j0[:, 32:48], T.lane[:], "lane", "j02")
+        act(T.nidf[:], T.idf[:], "idf", "nidf", scale=-1.0)
+        act(T.b8f[:], b8, "xm", "b8f")
+        act(T.bo0[:], T.bo[:], "bo col9", "bo0", scale=T.col[:, 9:10])
+        act(T.bo1[:], T.bo[:], "bo col10", "bo1", scale=T.col[:, 10:11])
+
+    def constants_4():
+        tt(T.bofd[:], T.bo[:], T.idb[:], ALU.subtract, "bo idb", "bofd")
+        ts(T.bofd[:], T.bofd[:], float(2 ** 20), ALU.mult, "bofd", "bofd")
+
+    Rall = "R Ri0 Ri1 Ri2"
+    jL, vL, xiL = T.jvL[:, 0:16], T.jvL[:, 16:32], T.jvL[:, 32:48]
+    bL, wL = T.bL[:, 0:16], T.bL[:, 16:32]
+
+    def early_in(s):
+        o = s * SW
+        arrive(s, 0)
+        arrive(s, 1)
+        la = "L%d_0 L%d_1" % (s, s)
+        wrap(T.P1[:, 384:418], T.selj, lambda p: T.land[:, o + p:o + 544:16], la + " selj", "@1 jw")
+        mm(T.P1[:, 418:434], T.idf[:], T.cb[:, 32:48], True, True, "idf cb2", "@1 jw")
+        mm(T.P1[:, 434:450], T.idb[:], T.land[:, o + 256:o + 272], True, False, la + " idb", "@1 jw")
+        mm(T.P1[:, 434:450], T.idb[:], T.land[:, o + 272:o + 288], False, True, la + " idb", "@1 jw")
+        act(T.j0[:, 0:16], T.P1[:, 384:400], "@1 jw", "j00")
+        act(T.j0[:, 16:32], T.P1[:, 434:450], "@1 jw", "j01")
+
+    def flags_in(s):
+        o = s * SW
+        tt(T.jd[:, 0:32], T.P1[:, 402:434], T.j0[:, 0:32], ALU.subtract, "@1 jw j00 j01", "jd0")
+        arrive(s, 2)
+        for k in range(3):
+            mm(T.P3[:, 16 * k:16 * k + 16], T.idb[:], T.land[:, o + 576:o + 592], True, True, "idb L%d_2" % s, "@3 c3")
+        tt(T.jf[:], T.P3[:, 0:48], T.jd[:], ALU.mult, "@3 c3 jd0 jd2", "jf")
+        tt(T.jf[:], T.jf[:], T.j0[:], ALU.add, "jf j00 j01 j02", "jf")
+        cp(T.jvL[:], T.jf[:], "jf", "jvL")
+
+    def take_x(s):
+        act(x, T.land[:, s * SW:s * SW + 544].indirect(xiL), "L%d_0 L%d_1 jvL" % (s, s), "Rx")
+
+    def equal_x(out, rec, rd, wr):
+        mm(T.P7[:, 0:256], T.id2[:], x, True, False, "id2 Rx", "@7 dx")
+        mm(T.P7[:, 0:256], T.idp[:], rec, False, True, "idp " + rd, "@7 dx")
+        act(T.sb[:], T.P7[:, 0:256], "@7 dx", "sb", AF.Abs)
+        act(out, T.sb[:], "sb", wr, AF.Relu, bias=1.0, scale=-1.0)
+
+    late = []
+    for t in range(NT):
+        o = t * SW
+        flg = T.msg[:, o + 544:o + 608]
+        gen, may, cl, first = [T.msg[:, o + 544 + 16 * k:o + 560 + 16 * k] for k in range(4)]
+        if t == 0:
+            wrap(T.P3[:, 16:32], T.sel, lambda p: T.prod[:, p::16], "prod " + selall, "@3 vw")
+            wrap(T.P3[:, 0:16], T.sel, lambda p: T.ex[:, p::16], "ex " + selall, "@3 jw0")
+            cp(T.jvL[:, 0:32], T.P3[:, 0:32], "@3 jw0 vw", "jvL")
+            cp(T.jf[:, 0:32], T.P3[:, 0:32], "@3 jw0 vw", "jf")
+        else:
+            flags_in(t - 1)
+        act(T.jm[:], T.IP[:, 0:784].indirect(jL), "IP jvL", "jm")
+        if t == 0:
+            init_records()
+        else:
+            take_x(t - 1)
+            late[0]()
+        tt(T.prod[:], T.SU[:, 0:2048].indirect(vL), T.jm[:], ALU.mult, "SU SUb SUd SUe jvL jm", "prod")
+        wrap(T.P3[:, 48:64], T.sel, lambda p: T.prod[:, p::16], "prod " + selall, "@3 ew")
+        mm(T.P0[:, 0:256], T.idb[:], x, True, True, "Rx idb", "@0 xP")
+        if t == 0:
+            init_records_2()
+        act(T.repg[:], T.IOT[:].indirect(vL), "IOT jvL", "repg")
+        act(T.key[:, 48:64], T.jf[:, 16:32], "jf", "key3", bias=-2048.0)
+        if t == 0:
+            constants_1()
+        else:
+            late[1]()
+        ew = T.P3[:, 48:64]
+        cp(T.ei[:], ew, "@3 ew", "ei")
+        ts(wL, ew, 2048.0, ALU.add, "@3 ew", "wL", 2047.0, ALU.min)
+        ts(T.bi[:], T.ei[:], 511, ALU.bitwise_and, "ei", "bi")
+        cp(bL, T.bi[:], "bi", "bL")
+        act(T.kw[:, 256:512], T.R[:, 0:2048].indirect(wL), Rall + " wL", "kw1")
+        act(T.wW[:], ew, "@3 ew", "wW", bias=2048.0)
+        act(T.tb[:], ew, "@3 ew", "tb", AF.Relu, bias=1.0)
+        ts(T.key[:, 16:32], T.bi[:], -256.0, ALU.add, "bi", "key1")
+        cp(T.verL[:], T.VL[:, 0:512].indirect(bL), "VL bL", "verL")
+        for nm, a, b in (("G0", 0, 64), ("G1", 64, 128 - GV), ("G2", 128, 192), ("G3", 192, 256)):
+            act(T.G[:, 16 * a:16 * b], T.R[:, 0:2048].indirect(T.verL[:, a:b]), Rall + " verL", nm)
+        if KWV:
+            tt(T.kw[:, 0:256], T.kw[:, 256:512], T.P0[:, 0:256], ALU.is_equal, "kw1 @0 xP", "kw0")
+        cp(T.verf[:], T.verL[:], "verL", "verf")
+        mm(T.P5[:, 0:128], T.idb[:], T.zer[:, 0:128], True, False, "idb zer", "@5 sv")
+        if KWV:
+            wrap(T.P3[:, 64:96], T.sel, lambda p: T.kw[:, p::16], "kw0 kw1 " + selall, "@3 kn")
+        for h in range(2):
+            bk = T["P%d" % (1 + h)]
+            mm(bk[:, 0:128], T.idb[:], T.kc[:], True, False, "idb kc", "@%d sc%d" % (1 + h, h))
+            mm(bk[:, 0:128], T.verf[:, 128 * h:128 * h + 128], T.idf[:], False, False, "verf idf", "@%d sc%d" % (1 + h, h))
+        if t == 0:
+            constants_2()
+        if GV:
+            cp(T.G[:, 16 * (128 - GV):2048], T.R[:, 0:2048].indirect(T.verL[:, 128 - GV:128]), Rall + " verL", "Gv")
+        b8e, b8v = T.b8[:, 8:16], T.b8[:, 16:24]
+        todo = [(w, h, k) for h in range(2) for w in range(2) for k in range(16)]
+        if t == 0:
+            todo.sort()
+        mm(T.P6[:], T.idb[:], T.zer[:], True, False, "idb zer", "@6 D")
+        for k in range(16):
+            mm(T.P1[:, k:128:16], T.G[:, k:2048:16], b8v, False, False, "G0 G1 Gv b8v", "@1 sc0")
+        for k in range(16):
+            tt(T.EQ[:, 256 * k:256 * k + 128], T.G[:, k:2048:16], T.P0[:, 0:128], ALU.is_equal, "G0 G1 Gv @0 xP", "EQa%d" % k)
+            mm(T.P1[:, k:128:16], T.EQ[:, 256 * k:256 * k + 128], b8e, False, k == 15, "EQa%d b8e" % k, "@1 sc0")
+        if not KWV:
+            equal_x(T.kw[:, 0:256], T.kw[:, 256:512], "kw1", "kw0")
+            wrap(T.P3[:, 64:96], T.sel, lambda p: T.kw[:, p::16], "kw0 kw1 " + selall, "@3 kn")
+        act(T.brep[:], T.IOT[:, 0:512].indirect(bL), "IOT bL", "brep", bias=1792.0)
+        act(T.ta[:], T.P3[:, 80:96], "@3 kn", "ta", bias=-15.5, scale=1.0 / VOID)
+        efn = T.EF[:, t:2048:8]
+        for bk, nm in ((T.P7[:, 256:512], "@7 sxb"), (T.P4[:, 128:384], "@4 xnb")):
+            mm(bk, T.idb[:], x, True, False, "idb Rx", nm)
+            mm(bk, T.idb[:], efn, False, nm[1] == "7", "idb EF", nm)
+        act(T.sgb[:], T.P7[:, 256:512], "@7 sxb", "sgb", AF.Sign, bias=-3.5)
+        if t == 0:
+            act(T.sel0[:], T.sel[:], selall + " col11", "sel0", scale=T.col[:, 11:12])
+        for k in range(16):
+            tt(T.EQ[:, 256 * k + 128:256 * k + 192], T.G[:, 2048 + k:3072:16], T.P0[:, 128:192], ALU.is_equal, "G2 @0 xP", "EQb%d" % k)
+        scan(T.mn[:, 0:128], T.seg[:], T.P1[:, 0:128], "seg @1 sc0", "mn0")
+        for k in range(16):
+            mm(T.P2[:, k:128:16], T.G[:, 2048 + k:4096:16], b8v, False, False, "G2 G3 b8v", "@2 sc1")
+        for k in range(16):
+            tt(T.EQ[:, 256 * k + 192:256 * k + 256], T.G[:, 3072 + k:4096:16], T.P0[:, 192:256], ALU.is_equal, "G3 @0 xP", "EQc%d" % k)
+            mm(T.P2[:, k:128:16], T.EQ[:, 256 * k + 128:256 * k + 256], b8e, False, k == 15, "EQb%d EQc%d b8e" % (k, k), "@2 sc1")
+        mm(T.P4[:, 128:384], T.id2[:], T.sgb[:], False, True, "id2 sgb", "@4 xnb")
+        act(T.msg[:, o + 288:o + 544], T.P4[:, 128:384], "@4 xnb", "mb", bias=-2.0)
+        send(t, 0, "mb")
+        tt(T.ta[:], T.ta[:], T.P3[:, 64:80], ALU.add, "ta @3 kn", "ta")
+        scan(T.mn[:, 128:256], T.seg[:], T.P2[:, 0:128], "seg @2 sc1", "mn1")
+        tt(T.nk[:], T.ta[:], T.tb[:], ALU.is_lt, "ta tb", "nk")
+        cp(T.si[:], T.mn[:, 15::16], "mn0 mn1", "si")
+        act(T.thw[:], T.nk[:], "nk", "thw", bias=84.5, scale=-100.0)
+        ts(T.lm[:, 0:16], T.si[:], 2047, ALU.bitwise_and, "si", "lm0")
+        ts(T.lm[:, 16:32], T.si[:], 15, ALU.arith_shift_right, "si", "lm1")
+        tt(T.x1[:], T.lm[:].indirect(T.xl[:]), T.xm[:], ALU.mult, "lm0 lm1 xl xm", "x1")
+        unlane(T.P3[:, 96:128], lambda k: T.x1[:, 32 * k:32 * k + 32], "x1", "@3 wc")
+        mm(T.P4[:, 0:128], T.idb[:], T.zer[:, 0:128], True, False, "idb zer", "@4 sb")
+        mm(T.P1[:, 128:384], T.idb[:], x, True, False, "idb Rx", "@1 sx")
+        mm(T.P2[:, 128:384], T.idb[:], x, True, False, "idb Rx", "@2 xn")
+        if t == 0:
+            constants_4()
+            constants_3()
+        cw, mw = T.P3[:, 96:112], T.P3[:, 112:128]
+        cp(T.cL[:], cw, "@3 wc", "cL")
+        tt(T.base[:], cw, T.wW[:], ALU.subtract, "@3 wc wW", "base")
+        tt(T.want[:], mw, T.thw[:], ALU.is_ge, "@3 wc thw", "want")
+        tt(T.base[:], T.base[:], T.nk[:], ALU.mult, "base nk", "base")
+        ts(T.far[:], mw, T.tha[:, 0:1], ALU.is_ge, "@3 wc tha", "far", 4096.0, ALU.mult)
+        tt(T.base[:], T.base[:], T.wW[:], ALU.add, "base wW", "base")
+        tt(T.te[:, 0:16], cw, T.far[:], ALU.max, "@3 wc far", "te0")
+        cp(T.vnL[:, 16:32], T.base[:], "base", "baseL")
+        act(T.repf[:], T.IOT[:].indirect(T.cL[:]), "IOT cL", "repf")
+        act(T.ex[:], T.EF[:].indirect(T.vnL[:, 16:32]), "EF baseL", "ex")
+        act(T.key[:, 0:16], cw, "@3 wc", "key0", bias=-2048.0)
+        act(T.te[:, 16:32], T.far[:], "far cfd", "te1", bias=784.0, scale=T.cfd[:, 0:1])
+        act(T.msg[:, o + 256:o + 272], T.base[:], "base", "mh")
+
+        def h6():
+            mm(T.P1[:, 128:384], T.idb[:], T.ex[:], False, True, "idb ex", "@1 sx")
+            mm(T.P2[:, 128:384], T.idb[:], T.ex[:], False, False, "idb ex", "@2 xn")
+            act(T.sg[:], T.P1[:, 128:384], "@1 sx", "sg", AF.Sign, bias=-3.5)
+            act(T.suc[:], T.SU[:, 0:2048].indirect(T.cL[:]), "SU cL", "suc")
+
+        def h10():
+            ts(T.c2L[:], T.te[:], 2560.0, ALU.min, "te0 te1", "c2L")
+            tt(T.msg[:, o + 272:o + 288], T.base[:], T.msg[:, o + 256:o + 272], ALU.subtract, "base mh", "ml")
+
+        def h13():
+            mm(T.P2[:, 128:384], T.id2[:], T.sg[:], False, True, "id2 sg", "@2 xn")
+            act(T.msg[:, o:o + 256], T.P2[:, 128:384], "@2 xn", "mx", bias=-2.0)
+            send(t, 1, "mh ml mx")
+
+        pairs(T.Ea, "Ea", T.brep, 16, T.want, T.P4, "@4 sb", "brep key1 want", False, (), {6: h6, 10: h10, 13: h13})
+        cp(T.rep[:], T.repf[:], "repf", "rep")
+        act(T.rc[:], T.R[:, 0:2576].indirect(T.c2L[:, 0:16]), Rall + " Rz Rx R5 c2L", "rc")
+        act(T.sq[:], T.suc[:], "suc", "sq", bias=139.501, scale=1.0 / 512.0)
+        act(T.fd[:], T.IP[:].indirect(T.c2L[:, 16:32]), "IP IPz c2L", "fd")
+        tt(T.wf[:], T.want[:], T.far[:], ALU.min, "want far", "wf")
+        if t == 0:
+            act(T.sel1[:], T.sel[:], selall + " col11", "sel1", scale=T.col[:, 12:13])
+
+        pairs(T.Eb, "Eb", T.rep, 0, T.want, T.P4, "@4 sb", "rep key0 want", True)
+        tt(T.x2[:], T.P4[:, 0:128], T.tm[:], ALU.is_lt, "@4 sb tm", "x2")
+        unlane(T.P3[:, 128:144], lambda k: T.x2[:, k::8], "x2", "@3 nc")
+        tt(T.dif[:], T.key[:], T.cd[:], ALU.subtract, "key0 key1 key2 key3 cd0 cd1 cd2 cd3", "dif")
+        tt(T.dl[:], T.cb[:, 32:48], T.base[:], ALU.subtract, "base cb2", "dl")
+        nc = T.P3[:, 128:144]
+        tt(cl, nc, T.wf[:], ALU.mult, "@3 nc wf", "cl")
+        send(t, 2, "cl")
+        if EQV:
+            tt(T.eqc[:], T.rc[:], T.P0[:, 0:256], ALU.is_equal, "rc @0 xP", "eqc")
+        else:
+            equal_x(T.eqc[:], T.rc[:], "rc", "eqc")
+        act(T.t30[:], T.eqc[:], "eqc", "t30", bias=VOID, scale=-VOID)
+        mm(T.P7[:, 256:512], T.id5[:], T.sq[:], True, False, "id5 sq", "@7 scp")
+        mmf(T.P7, 256, T.idf, T.suc, True, "idf suc", "@7 scp")
+        act(T.SU[:, 2304:2560], T.P7[:, 256:512], "@7 scp", "SUc", bias=512.0 * 140.0)
+        cp(T.repv[:], T.repg[:], "repg", "repv")
+        pairs(T.Ev, "Ev", T.repv, 48, None, T.P5, "@5 sv", "repv key3", True)
+        tt(T.x2v[:], T.P5[:, 0:128], T.tm[:], ALU.is_lt, "@5 sv tm", "x2v")
+        unlane(T.P5[:, 128:144], lambda k: T.x2v[:, k::8], "x2v", "@5 fw")
+        act(first, T.P5[:, 128:144], "@5 fw", "first")
+        tt(may, nc, T.want[:], ALU.mult, "@3 nc want", "may")
+        tt(T.ta[:], cl, T.dl[:], ALU.mult, "cl dl", "ta")
+        tt(gen, may, cl, ALU.subtract, "may cl", "gen")
+        tt(T.vn[:], T.ta[:], T.base[:], ALU.add, "ta base", "vn")
+        tt(T.td[:], flg, T.dif[:], ALU.mult, "gen may cl first dif", "td")
+        cp(T.vnL[:, 0:16], T.vn[:], "vn", "vnL")
+        tt(T.td[:], T.td[:], T.cb[:], ALU.add, "td cb0 cb1 cb2 cb3", "td")
+        act(T.vnr[:], T.IOT[:].indirect(T.vnL[:, 0:16]), "IOT vnL", "vnr")
+        cp(T.wrL[:], T.td[:], "td", "wrL")
+        act(T.sf[:], T.SU[:].indirect(T.wrL[:, 32:48]), "SU SUz SUc wrL", "sf")
+        act(T.SU[:, t:2048:8], T.sf[:], "sf", "SU")
+        act(T.old[:], T.SU[:, 0:2048].indirect(vL), "SU jvL", "old")
+        for a in todo:
+            dword(*a)
+        mm(T.P6[:, 0:256], T.bo0[:], T.eqc[:], False, False, "bo0 eqc", "@6 D")
+        mm(T.P6[:, 256:512], T.bo1[:], T.eqc[:], False, False, "bo1 eqc", "@6 D")
+        mm(T.P6[:, 0:256], T.bofd[:], T.fd[:], False, True, "bofd fd", "@6 D")
+        tt(T.R[:, 0:2304].indirect(T.wrL[:, 0:16]), T.t30[:], x, ALU.add, "wrL t30 Ri0 Ri1 Ri2 Rx", "R Rz")
+        ts(T.di[:, 0:256], T.P6[:, 0:256], float(0x5555), ALU.add, "@6 D", "di0")
+        ts(T.di[:, 256:512], T.P6[:, 256:512], float(0xAAAA), ALU.add, "@6 D", "di1")
+        ts(T.dy[:, 0:256], T.di[:, 0:256], 0xAAAA + 2 ** 20, ALU.bitwise_and, "di0", "dy0")
+        ts(T.dy[:, 256:512], T.di[:, 256:512], 2 * 0xAAAA, ALU.bitwise_and, "di1", "dy1")
+        mm(T.P4[:, 128:384], T.idb[:], T.zer[:, 0:256], True, False, "idb zer", "@4 d2")
+        mmf(T.P4, 128, T.idf, T.vnr, False, "idf vnr", "@4 d2")
+        mmf(T.P4, 128, T.nidf, T.old, True, "nidf old", "@4 d2")
+        act(T.sb[:], T.R[:, 0:2560].indirect(T.wrL[:, 32:48]), "R Rz Rx wrL", "sb")
+        act(T.R[:, t:2048:8], T.sb[:], "sb", "R")
+        if t == 0:
+            act(T.selj[:], T.sel[:], selall + " col4", "selj", scale=T.col[:, 4:5])
+        mm(T.P7[:, 0:256], T.idb[:], T.c2k[:], True, False, "idb c2k", "@7 df")
+        mmf(T.P7, 0, T.nidf, T.verf, False, "nidf verf", "@7 df")
+        mmf(T.P7, 0, T.idf, T.vnr, True, "idf vnr", "@7 df")
+        if t < NT - 1:
+            mm(T.P3[:, 144:160], T.bo[:], cl, True, True, "bo cl", "@3 aw")
+        if t < NT - 1:
+            tt(T.mm[:], T.dy[:, 0:256], T.dy[:, 256:512], ALU.is_equal, "dy0 dy1", "mm")
+        tt(T.p2[:], T.jm[:], T.P4[:, 128:384], ALU.mult, "jm @4 d2", "p2")
+        tt(T.SU[:, 0:2304].indirect(T.wrL[:, 48:64]), T.p2[:], T.old[:], ALU.add, "wrL p2 old", "SU SUz")
+        if t == NT - 1:
+            ts(T.reci[:], T.R[:, 0:2048], 9.0, ALU.min, "R", "reci0 reci1")
+            dma("y", T.yr[:], T.reci[:], "reci0", "")
+            tt(T.mm[:], T.dy[:, 0:256], T.dy[:, 256:512], ALU.is_equal, "dy0 dy1", "mm")
+        if t < NT - 1:
+            act(T.an[:], T.P3[:, 144:160], "@3 aw", "an ac", bias=244.5 / 16.0, acc=T.ac[:, 0:1])
+            act(T.ay[:, 0:1], T.ac[:, 0:1], "ac", "ay", bias=5.55, scale=0.5)
+            act(T.cd[:, 32:48], T.cd[:, 32:48], "cd2", "cd2", bias=1.0)
+            act(T.tha[:, 0:1], T.ay[:, 0:1], "ay ac", "tha", bias=T.ac[:, 0:1], scale=-2.0)
+            act(T.cfd[:, 0:1], T.cfd[:, 0:1], "cfd", "cfd", bias=1.0 / 4096.0)
+        early_in(t)
+        if t < NT - 1:
+            act(T.cb[:, 32:48], T.cb[:, 32:48], "cb2", "cb2", bias=1.0)
+        tt(T.pr[:], T.mm[:], T.P7[:, 0:256], ALU.mult, "mm @7 df", "pr")
+        late = [lambda: tt(T.VL[:].indirect(T.wrL[:, 16:24]), T.pr[:, 0:128], T.verf[:, 0:128], ALU.add, "wrL pr verf VLz", "VL"),
+                lambda: tt(T.VL[:].indirect(T.wrL[:, 24:32]), T.pr[:, 128:256], T.verf[:, 128:256], ALU.add, "wrL pr verf VLz", "VL")]
+
+    for k in range(16):
+        mm(T.P0[:, k:128:16], T.SU[:, 128 * k:128 * k + 128], T.b8f[:], True, True, "b8f SU", "@0 ys")
+    late[0]()
+    act(T.yso[:, 0:128], T.P0[:, 0:128], "@0 ys", "yso0", bias=32768.0)
+    flags_in(NT - 1)
+    mm(T.P2[:, 0:128], T.yso[:, 0:128], T.idf[:], True, True, "yso0 idf", "@2 yt")
+    late[1]()
+    dma("y", T.yl[:], T.VL[:, 0:512], "VL", "")
+    act(T.vnr[:], T.IOT[:].indirect(vL), "IOT jvL", "vnr", bias=2048.0)
+    dma("s", T.yv[:], T.vnr[0:128:16, :], "vnr", "")
+    take_x(NT - 1)
+    dma("s", T.yx[:], x, "Rx", "")
+    act(T.yso[:, 128:256], T.P2[:, 0:128], "@2 yt", "yso1")
+    dma("s", T.ys[:], T.yso[:, 128:256], "yso1", "")
+    emit(g, T, ops)
+    g.wait_ge(T.sem.sent, nsent[0])

@@ -1,41 +1,82 @@
 import math
+import numpy as np
 from concourse.mybir import AluOpType as ALU, ActivationFunctionType as AF
 
 NT = 6
 HOP = 3
-SW = 608
-PARTS = ((288, 544), (0, 288), (576, 592))
-GV = 32
-GATHER, SCATTER, PE, WAKE, SLACK, HOPS = 1.5, 3.8, 0.5, 60.0, 70.0, (6000.0, 6000.0, 4600.0)
-KWV = True
-EQV = True
-AHEAD = 300
+SW = 512
+LW = 48
+CYC, GATHER, SCATTER, PE, WAKE, HOPS = 1.04, 1.62, 3.95, 0.52, 150.0, (6000.0, 6000.0, 4700.0)
+OVER = ("over",)
+VERS, BREPS = False, False
+CHUNKS = (0, 64, 128, 192, 224, 256)
+FIRST, LATE, SPLIT, REPV, RG, XS = (0, 4, 16), False, (128, 96), (0, 1), 1, 1
+GV = -1
+SHAKE, SLACK = 150.0, 150.0
+PASSES = 1000
 ORDER = {}
-VOID = float(2 ** 30)
+VOID = float(2 ** 36)
+XO, VO = 32.0, 6144.0
+BIG = 8192.0
 LN3 = math.log(3.0)
+TAB = 256
+END = TAB + 2048 + 32
 
 F, B, H, I, U = "float32", "bfloat16", "float16", "int32", "uint16"
 SCRATCH = {}
 for _d, _l in (
     (B, "land:%d msg:%d " % (NT * SW, NT * SW) +
-        "R:2576 EF:2048 IP:800 G:4096 EQ:4096 Ea:4096 Eb:4096 sel:2048 selj:2048 sel0:2048 sel1:2048 selg:1024 rw:576 idb:128 "
-        "id2:128 id5:128 idp:128 bo:128 bo0:128 bo1:128 bofd:128 zer:512 c2k:256 kc:128 b8:32 xm:256 pw:8 tmpb:800 tmpc:1024 "
-        "tmpd:256 reci:2048 jm:256 kw:512 brep:256 x2:128 x2v:128 rc:256 eqc:256 t30:256 fd:256 ex:256 sg:256 sgb:256 "
-        "sb:256 sq:256 ay:8"),
-    (F, "SU:2560 VL:768 IOT:2048 idf:128 nidf:128 seg:128 tm:128 b8f:8 col:16 wex:16 tmpf:128 lane:16 cb:64 cd:64 key:64 dif:64 "
-        "td:64 cfd:8 j0:48 jd:48 jf:48 wW:16 verf:256 repf:256 ta:16 tb:16 tc:16 te:32 nk:16 thw:16 mn:256 want:16 far:16 wf:16 "
-        "base:16 dl:16 vn:16 suc:256 vnr:256 old:256 p2:256 sf:256 mm:256 pr:256 an:16 ac:8 tha:8 yso:256"),
-    (H, "prod:256 rep:256 repv:256 x1:256"), (B, "Ev:4096"), (F, "repg:256"),
-    (I, "coli:4 edi:512 vei:512 v0i:256 ei:16 bi:16 si:16 lm:32 di:512 dy:512"),
-    (U, "xl:16 jvL:48 bL:32 verL:256 cL:16 c2L:32 vnL:32 wrL:64"),
+        "EF:2048 IP:1568 G:4096 EQ:4096 Ea:4096 Eb:4096 sel:2048 selj:2048 selT:2048 selD:2048 selg:1024 rw:576 idb:128 "
+        "id2:128 id5:128 idV:128 idQ:128 idR:128 id32:128 id1:128 idM:128 idH:128 xw:256 IOB:512 idN:128 idP:128 one:128 bo:128 bo01:256 bo19:128 "
+        "kc:128 rE:24 b8:32 xm:64 "
+        "pw:8 cw:8 tmpb:784 tmpd:128 reci:2048 jm:256 kw:512 brep:256 x2:128 rc:256 nec:256 ex:256 sg:256 "
+        "sgb:256 sq:256 ay:8 tri:256 E1:384 sp:256 mm:256 keyb:16 gateb:16 rg:1536 farb:16 ncb:16 clb:16 xx:512"),
+    (F, "SS:%d RR:2576 IOT:2048 repf:256 gate:16 " % END +
+        "VL:768 idf:128 t30:256 sb:256 mk:256 ylo:512 seg:128 tm:128 col:32 wex:16 tmpf:128 lane:16 AC:96 BT:96 key:16 verf:256 mn:256 "
+        "suc:256 old:256 p2:256 sf:256 pr:256 an:16 ac:8 tha:8 yso:256"),
+    (H, "prod:256 urep:256 vf:16 vnh:16 um:512 jx:128 ux:128"),
+    (I, "coli:4 edi:512 vei:512 v0i:256 ei:16 bi:16 si:16 lm:32 li:96 di:512 dy:512"),
+    (U, "lland:%d lmsg:%d bL:32 verL:256 cL:16 wrL:48 ptL:16 xl:16" % (LW * (NT + 1), LW * NT)),
 ):
     for _w in _l.split():
         SCRATCH[_w.split(":")[0]] = ("sbuf", [128, int(_w.split(":")[1])], _d)
 for _k in range(8):
     SCRATCH["P%d" % _k] = ("psum", [128, 512], F)
-NDMA = 24
+NDMA = 30
 SEMAPHORES = (["cv", "cs", "cp", "cg", "sent"] + ["arr%d_%d" % (t, k) for t in range(NT) for k in range(3)]
               + ["dm%d" % k for k in range(NDMA)])
+
+
+def X(name, a=0, b=None, s=1, p=(0, 128)):
+    return (name, a, SCRATCH[name][1][1] if b is None else b, s, p, None)
+
+
+def by(win, off):
+    return win[:5] + (off,)
+
+
+def cols(v):
+    return 16 * cols(v[5]) if v[5] else len(range(v[1], v[2], v[3]))
+
+
+def bits(v):
+    if v[3] == 1:
+        return (1 << v[2]) - (1 << v[1])
+    return sum(1 << c for c in range(v[1], v[2], v[3]))
+
+
+def part(t, k):
+    if k == 2:
+        return X("lland", t * LW, t * LW + LW), X("lmsg", t * LW, t * LW + LW)
+    a = t * SW + 256 * k
+    return X("land", a, a + 256), X("msg", a, a + 256)
+
+
+def view(T, v):
+    if not isinstance(v, tuple):
+        return v
+    a = T[v[0]][v[4][0]:v[4][1], v[1]:v[2]:v[3]] if v[3] > 1 else T[v[0]][v[4][0]:v[4][1], v[1]:v[2]]
+    return a.indirect(view(T, v[5])) if v[5] else a
 
 
 def mask_of(engines):
@@ -61,7 +102,7 @@ def relay_program(g, core, T, topo, dsts, hops):
         rid, pid = topo.addr(dsts[t], core)
         for k, (h, eng) in enumerate(hops):
             if h == core:
-                piece = T.land[:, t * SW + PARTS[k][0]:t * SW + PARTS[k][1]]
+                piece = view(T, part(t, k)[0])
                 s = T.sem["arr%d_%d" % (t, k)]
                 g.wait_ge(s, len(eng))
                 g.remote_dma(piece, piece, s, T.sem.sent, pid, rid, topo.mask(core, dsts[t]))
@@ -69,115 +110,151 @@ def relay_program(g, core, T, topo, dsts, hops):
     g.wait_ge(T.sem.sent, total)
 
 
-def schedule(ops, full):
+def tag(o):
+    name, a, b, s = o[3][0][:4]
+    if name in ("G", "EQ"):
+        k = CHUNKS.index(a // 16 if name == "G" else a % 512 // 2)
+    elif name in ("Ea", "Eb", "rg"):
+        k = (a >= 2048, a % 256 >= 128, a >= 1024)[("Ea", "Eb", "rg").index(name)]
+    elif name in ("SS", "RR"):
+        k = a // 128 if a < TAB else "w" if s > 1 else "s"
+    elif name in ("msg", "sent"):
+        k = a % SW // 128 if name == "msg" else a % 3
+    elif name in ("xx", "lmsg", "ptL"):
+        k = ""
+    elif name in ("bL", "jm", "prod", "ei", "bi", "verL", "BT", "li", "kw"):
+        k = a if name != "li" else b
+    else:
+        k = 2 * a // SCRATCH[name][1][1]
+    return "%s%s" % (name, int(k) if k is True or k is False else k)
+
+
+def inline(ops, m, n):
+    return ops[m][0] == ops[n][0] and (ops[m][0] == "p" or ops[m][5][2:] == ops[n][5][2:] == ("over",))
+
+
+def schedule(ops, full, runs):
     n = len(ops)
-    succ = [[] for _ in range(n)]
-    for i, d in enumerate(full):
-        for m in d:
-            succ[m].append(i)
     eng = [o[0] for o in ops]
-    left = [len(d) for d in full]
-    ready = [0.0] * n
-    cand = {e: set() for e in set(eng)}
+    dur = [o[5][0] for o in ops]
+    banks = [sorted({v[0] for v in o[2] + o[3] if v[0][0] == "P"}) for o in ops]
+    pre = [[(m, ops[m][5][1] + (0 if inline(ops, m, i) else WAKE)) for m in sorted(d)] for i, d in enumerate(full)]
+    post = [[] for _ in range(n)]
     for i in range(n):
-        if not left[i]:
-            cand[eng[i]].add(i)
-    free = {e: 0.0 for e in cand}
-    order, done = [], [False] * n
+        for m, lat in pre[i]:
+            post[m].append((i, lat))
 
-    def issue(i):
-        e = eng[i]
-        st = max(free[e], ready[i])
-        cand[e].discard(i)
-        done[i] = True
-        order.append(i)
-        free[e] = st + ops[i][5][0]
-        for s in succ[i]:
-            ready[s] = max(ready[s], free[e] + ops[i][5][1] + (0 if eng[s] == e == "p" else WAKE))
-            left[s] -= 1
-            if not left[s]:
-                cand[eng[s]].add(s)
+    def lay(before, rank, first):
+        end = [0.0] * n
+        line = {k: ([], []) for k in names}
+        for i in rank:
+            t, d = first[i], dur[i]
+            for m, lat in before[i]:
+                if end[m] + lat > t:
+                    t = end[m] + lat
+            moved = d > 0
+            while moved:
+                moved = False
+                for name, pad in meets[i]:
+                    lo, hi = line[name]
+                    k = len(hi)
+                    while k and hi[k - 1] > t - pad + 1e-6:
+                        k -= 1
+                    while k < len(lo) and lo[k] - pad < t + d - 1e-6:
+                        t, k, moved = hi[k] + pad, k + 1, len(meets[i]) > 1
+            end[i] = t + d
+            for name in holds[i]:
+                lo, hi = line[name]
+                k = len(hi)
+                while k and hi[k - 1] > t + 1e-6:
+                    k -= 1
+                lo.insert(k, t)
+                hi.insert(k, t + d)
+        return end
 
-    def soonest(i, depth, memo):
-        if not left[i] or not depth:
-            return ready[i]
-        if i not in memo:
-            memo[i] = max([ready[i]] + [max(free[eng[m]], soonest(m, depth - 1, memo)) + ops[m][5][0] + ops[m][5][1]
-                                        + (0 if eng[m] == eng[i] == "p" else WAKE) for m in full[i] if not done[m]])
-        return memo[i]
+    def ranked(key, before, walk):
+        for i in walk:
+            for m, lat in before[i]:
+                if key[m] >= key[i]:
+                    key[i] = key[m] + 1e-3
+        return sorted(walk, key=lambda i: key[i])
 
-    rest = {e: [i for i in range(n) if eng[i] == e] for e in cand}
-    clock = dict(free)
-    while len(order) < n:
-        e = min((k for k in cand if cand[k]), key=lambda k: (max(clock[k], min(ready[i] for i in cand[k])), k))
-        now = max(clock[e], min(ready[i] for i in cand[e]))
-        while done[rest[e][0]]:
-            rest[e].pop(0)
-        memo, limit, pick = {}, 1e18, None
-        for i in rest[e][:AHEAD]:
-            if done[i]:
-                continue
-            if not left[i] and ready[i] <= now and now + ops[i][5][0] <= limit + SLACK:
-                pick = i
-                break
-            if not [m for m in full[i] if not done[m] and eng[m] == e]:
-                limit = min(limit, max(now, soonest(i, 12, memo)))
-        if pick is None:
-            later = [ready[i] for i in cand[e] if ready[i] > now] + [limit]
-            nxt = min(later)
-            if nxt > now:
-                clock[e] = nxt
-                continue
-            clock[e] = now + 20.0
-            continue
-        free[e] = max(free[e], now)
-        issue(pick)
-        clock[e] = free[e]
+    meets = [[(eng[i], 0.0)] + [(b + e, WAKE) for b in banks[i] for e in "vsp" if e != eng[i]] for i in range(n)]
+    holds = [[eng[i]] + [b + eng[i] for b in banks[i]] if dur[i] else [] for i in range(n)]
+    names = set(eng) | {"P%d%s" % (k, e) for k in range(8) for e in "vsp"}
+    group = [tag(o) if 1 <= o[6][0] <= NT and o[0] in "vsg" else o[0] + o[3][0][0] if o[3] else "out" for o in ops]
+    kinds = sorted(set(group))
+    after, up, down = [o[5][1] for o in ops], list(range(n)), list(range(n - 1, -1, -1))
+    seed, best, now = 1, None, None
+    key = [o[6][0] * 1e6 + o[6][1] * 1e5 + i for i, o in enumerate(ops)]
+    for k in range(PASSES):
+        end = lay(pre, ranked(key, pre, up), [0.0] * n)
+        total = max(end[i] + after[i] for i in up)
+        if now is None or total < now[0] + SLACK:
+            now = (total, end)
+        if best is None or total < best[0]:
+            best = (total, [end[i] - dur[i] for i in up])
+        shift = {}
+        for _ in range(3 if k > 3 else 0):
+            seed = (seed * 1103515245 + 12345) % 2 ** 31
+            shift[kinds[seed // 7 % len(kinds)]] = (seed // 1000 % 7 - 3) * SHAKE * (1 + seed // 77 % 3)
+        if k % 2:
+            key = [now[1][i] - dur[i] + shift.get(group[i], 0.0) for i in up]
+        else:
+            back = lay(post, ranked([-now[1][i] - shift.get(group[i], 0.0) for i in up], post, down), after)
+            key = [-back[i] for i in up]
+    order = sorted(range(n), key=lambda i: (best[1][i], i))
+    last = {}
+    for i in order:
+        for b in banks[i]:
+            if b in last and eng[last[b]] != eng[i]:
+                full[i].add(last[b])
+            last[b] = i
     return order
+
+
+def depend(ops):
+    live, bank, seen, full = {}, {}, {}, []
+    for n, (e, fn, rd, wr, kind, cost, key) in enumerate(ops):
+        d = set()
+        if e == "p":
+            if cost[2]:
+                d.update(sum(bank.setdefault(wr[0][0], [])[-1:], seen.pop(wr[0][0], [])))
+                bank[wr[0][0]].append([n])
+            else:
+                d.add(bank[wr[0][0]][-1][0])
+                bank[wr[0][0]][-1].append(n)
+        for v, m in [(v, bits(v)) for v in rd]:
+            d.update(r[1] for r in live.get(v[0], []) if r[2] and r[0] & m)
+            if v[0] in bank:
+                d.update(bank[v[0]][-1])
+                seen.setdefault(v[0], []).append(n)
+        for v, m in [(v, bits(v)) for v in wr]:
+            d.update(r[1] for r in live.get(v[0], []) if r[0] & m)
+            live[v[0]] = [(r[0] & ~m, r[1], r[2]) for r in live.get(v[0], []) if r[0] & ~m] + [(m, n, True)]
+        for v in rd:
+            live.setdefault(v[0], []).append((bits(v), n, False))
+        d.discard(n)
+        full.append(d)
+    return full, bank
 
 
 def emit(g, T, ops):
     q = {"v": g.vector, "s": g.scalar, "p": g.tensor, "g": g, "y": g.sync}
     sem = {"v": T.sem.cv, "s": T.sem.cs, "p": T.sem.cp, "g": T.sem.cg}
-    lastw, readers, bank, full, deps, need = {}, {}, {}, [], {}, set()
-    for n, (e, fn, rd, wr, kind, cost) in enumerate(ops):
-        d = set()
-        for r in rd + wr:
-            if r[0] == "@":
-                eng, now, before = bank.get(r, (e, [], []))
-                if eng != e:
-                    now, before = [], now
-                d.update(before)
-                if e == "p":
-                    d.update(now[-1:])
-                bank[r] = (e, now + [n], before)
-        for r in rd:
-            if r in lastw:
-                d.add(lastw[r])
-        for w in wr:
-            if w[0] != "@":
-                if w in lastw:
-                    d.add(lastw[w])
-                d.update(readers.get(w, []))
-        for r in rd:
-            if r[0] != "@":
-                readers.setdefault(r, []).append(n)
-        for w in wr:
-            if w[0] != "@":
-                lastw[w] = n
-                readers[w] = []
-        d.discard(n)
-        full.append(d)
     if len(ops) not in ORDER:
-        ORDER[len(ops)] = schedule(ops, full)
-    order = ORDER[len(ops)]
+        full, runs = depend(ops)
+        ORDER[len(ops)] = (full, runs, schedule(ops, full, runs))
+    full, runs, order = ORDER[len(ops)]
     pos = {n: k for k, n in enumerate(order)}
+    stops = {max(r, key=pos.get) for b in runs for r in runs[b]}
+    deps, need = {}, set()
     for n in order:
         top = {}
         for m in full[n]:
             e2, k2 = ops[m][0], ops[m][4]
             if k2 == "c":
-                if not (e2 == "p" and ops[n][0] == "p") and pos[m] > pos.get(top.get(e2), -1):
+                if not inline(ops, m, n) and pos[m] > pos.get(top.get(e2), -1):
                     top[e2] = m
             elif k2 != "r":
                 top[("x", m)] = m
@@ -186,14 +263,14 @@ def emit(g, T, ops):
     cnt = {k: 0 for k in sem}
     tok, seen, ndma, ends = {}, {k: {} for k in q}, 0, []
     for n in order:
-        e, fn, rd, wr, kind, cost = ops[n]
+        e, fn, rd, wr, kind, cost, key = ops[n]
         for m in deps[n]:
             name, s, val = tok[m]
             if seen[e].get(name, 0) < val:
                 q[e].wait_ge(s, val)
                 seen[e][name] = val
         if kind == "c":
-            ins = fn()
+            ins = fn(n in stops) if e == "p" else fn()
             if n in need:
                 cnt[e] += 1
                 ins.then_inc(sem[e], 1)
@@ -223,493 +300,518 @@ def rank_program(g, core, T, topo):
         return
     me, dsts, hops = rt[rank]
     ops = []
+    urge = [0, 0]
+
+    def level(k):
+        urge[1] = k
+
     V, S, P = g.vector, g.scalar, g.tensor
 
-    def op(e, fn, rd, wr, kind="c", cost=(64.0, 0.0)):
-        ops.append((e, fn, rd.split(), wr.split(), kind, cost))
+    def op(e, fn, rd, wr, cost, kind="c"):
+        rd = [v for v in rd if isinstance(v, tuple)]
+        rd += [v[5] for v in rd + wr if v[5]]
+        ops.append((e, fn, rd, list(wr), kind, cost, tuple(urge)))
 
-    def two(a):
-        return "16" in str(a.dtype)
+    def w(v):
+        return view(T, v)
 
-    def sides(out, a, per, rd=""):
-        names = rd.split()
-        if names[:1] == ["wrL"]:
-            return (50.0 + SCATTER * a.shape[1], 0.0)
-        if len(names) > 1 and [w for w in names if w[-1] == "L" and w != "VL" or w == "xl"]:
-            return (60.0 + GATHER * out.shape[1], 0.0)
-        if per == 0:
-            per = 0.5 if two(out) and two(a) else 1.0
-        return (max(64.0, per * a.shape[1]), 0.0)
+    def two(*a):
+        return all("16" in SCRATCH[v[0]][2] for v in a)
 
-    def tt(out, a, b, o, rd, wr):
-        op("v", lambda: V.tensor_tensor(out, a, b, o), rd, wr, "c", sides(out, a, 1.0 if "@" in rd else 2.0, rd))
+    def took(out, a, per):
+        if out[5]:
+            return (50.0 + SCATTER * cols(out), 0.0)
+        if a[5]:
+            return (60.0 + GATHER * cols(out), 0.0)
+        return (CYC * max(64.0, (per or (0.5 if two(out, a) else 1.0)) * cols(a)), 0.0)
 
-    def ts(out, a, s1, o1, rd, wr, s2=None, o2=None):
-        c = sides(out, a, 0)
+    def tt(out, a, b, o, over=()):
+        op("v", lambda: V.tensor_tensor(w(out), w(a), w(b), o), [a, b], [out],
+           took(out, a, 1.0 if "P" in a[0][0] + b[0][0] else 2.0) + over)
+
+    def ts(out, a, s1, o1, s2=None, o2=None):
         if o2 is None:
-            op("v", lambda: V.tensor_scalar(out, a, s1, None, o1), rd, wr, "c", c)
+            op("v", lambda: V.tensor_scalar(w(out), w(a), w(s1), None, o1), [a, s1], [out], took(out, a, 0))
         else:
-            op("v", lambda: V.tensor_scalar(out, a, s1, s2, o1, o2), rd, wr, "c", c)
+            op("v", lambda: V.tensor_scalar(w(out), w(a), w(s1), w(s2), o1, o2), [a, s1, s2], [out], took(out, a, 0))
 
-    def cp(out, a, rd, wr):
-        op("v", lambda: V.tensor_copy(out, a), rd, wr, "c", sides(out, a, 0, rd))
+    def cp(out, a):
+        op("v", lambda: V.tensor_copy(w(out), w(a)), [a], [out], took(out, a, 0))
 
-    def ms(out, val, wr):
-        op("v", lambda: V.memset(out, val), "", wr, "c", sides(out, out, 0))
+    def ms(out, val):
+        op("v", lambda: V.memset(w(out), val), [], [out], took(out, out, 0))
 
-    def scan(out, a, b, rd, wr):
-        op("v", lambda: V.tensor_tensor_scan(out, a, b, 0.0, ALU.add, ALU.min), rd, wr, "c", sides(out, a, 1.0))
+    def scan(out, a, b):
+        op("v", lambda: V.tensor_tensor_scan(w(out), w(a), w(b), 0.0, ALU.add, ALU.min), [a, b], [out], took(out, a, 1.0))
 
-    def act(out, a, rd, wr, func=AF.Identity, bias=0.0, scale=1.0, acc=None):
-        c = sides(out, a, 1.0, rd)
-        op("s", lambda: S.activation(out, a, func, bias=bias, scale=scale, accum_out=acc), rd, wr, "c", c)
-
-    def mm(out, l, r, st, sp, rd, wr):
-        c = PE * max(min(64, l.shape[1]), r.shape[1]) * (1 if two(l) else 4)
-        op("p", lambda: P.matmul(out, l, r, st, sp), rd, wr, "c", (c, 0.0))
-
-    def mmf(bank, at, l, r, sp, rd, wr):
-        for k in range(4):
-            mm(bank[:, at + 64 * k:at + 64 * k + 64], l[:], r[:, 64 * k:64 * k + 64], False, sp and k == 3, rd, wr)
-
-    def iota(out, pat, base, cm, wr, small=True):
-        c = (130.0 + 2.0 * out.shape[1], 0.0)
-        if small:
-            op("g", lambda: g.iota(out, pat, base, cm, allow_small_or_imprecise_dtypes=True), "", wr, "c", c)
+    def act(out, a, func=AF.Identity, bias=0.0, scale=1.0, acc=None):
+        if out[5]:
+            op("s", lambda: S.activation(w(out), w(a), func), [a], [out], took(out, a, 1.0))
         else:
-            op("g", lambda: g.iota(out, pat, base, cm), "", wr, "c", c)
+            op("s", lambda: S.activation(w(out), w(a), func, bias=w(bias), scale=w(scale), accum_out=w(acc)), [a, bias, scale],
+               [out] + ([acc] if acc else []), took(out, a, 1.0))
 
-    def dma(e, out, a, rd, wr):
+    def mm(out, l, r, st=False, sp=False):
+        c = PE * max(min(64, cols(l)), cols(r)) * (1 if two(l) else 4)
+        op("p", lambda last: P.matmul(w(out), w(l), w(r), st, last), [l, r], [out], (c, 0.0, st))
+
+    def sub(v, a, b, s=1):
+        return (v[0], v[1] + a * v[3], min(v[2], v[1] + b * v[3]), v[3] * s) + v[4:]
+
+    def mmf(out, l, r, st=False, sp=False):
+        n = cols(r) // 64
+        for k in range(n):
+            mm(sub(out, 64 * k, 64 * k + 64), l, sub(r, 64 * k, 64 * k + 64), st and k == 0, sp and k == n - 1)
+
+    def iota(out, pat, base, cm=0):
+        c = (130.0 + 2.0 * CYC * cols(out), 0.0)
+        if SCRATCH[out[0]][2] == I:
+            op("g", lambda: g.iota(w(out), pat, base, cm), [], [out], c)
+        else:
+            op("g", lambda: g.iota(w(out), pat, base, cm, allow_small_or_imprecise_dtypes=True), [], [out], c)
+
+    def fill(out, val):
+        iota(out, [[0, cols(out)]], val)
+
+    def select(out, a, pat, o, val, base, cm):
+        op("g", lambda: g.affine_select(w(out), w(a), pat, o, val, base, cm), [a], [out], (170.0 + 2.0 * CYC * cols(out), 0.0))
+
+    def dma(e, out, a, nbytes):
         qq = g.sync if e == "y" else g.scalar
-        op(e, lambda: qq.dma_start(out, a), rd, wr, "d", (100.0, 2000.0 + a.shape[0] * a.shape[1] * (2 if two(a) else 4) / 200.0))
+        op(e, lambda: qq.dma_start(w(out), w(a)), [a], [out] if isinstance(out, tuple) else [], (100.0, 2000.0 + nbytes / 200.0), "d")
 
     nsent = [0]
 
-    def send(t, k, rd):
+    def send(t, k):
         h, eng = hops[k]
         rid, pid = topo.addr(h, core)
-        a, b = t * SW + PARTS[k][0], t * SW + PARTS[k][1]
+        far, near = part(t, k)
         nsent[0] += len(eng)
-        op("g", lambda: g.remote_dma(T.land[:, a:b], T.msg[:, a:b], T.sem["arr%d_%d" % (t, k)], T.sem.sent, pid, rid, mask_of(eng)),
-           rd, "S%d_%d" % (t, k), "r", (500.0, 0.0))
-
-    def arrive(t, k):
+        op("g", lambda: g.remote_dma(w(far), w(near), T.sem["arr%d_%d" % (t, k)], T.sem.sent, pid, rid, mask_of(eng)),
+           [near], [("sent", 3 * t + k, 3 * t + k + 1, 1, None, None)], (500.0, 0.0), "r")
         h = [hp for c, ds, hp in rt if ds[t] == core][0][k][0]
         nm = "arr%d_%d" % (t, k)
-        op("x", None, "S%d_%d" % (t, k), "L%d_%d" % (t, k), (nm, T.sem[nm], len(topo.engines(h, core))), (0.0, HOPS[k]))
+        op("x", None, [("sent", 3 * t + k, 3 * t + k + 1, 1, None, None)], [far], (0.0, HOPS[k]),
+           (nm, T.sem[nm], len(topo.engines(h, core))))
 
-    def wrap(out, lhs, src_of, rd, wr):
+    def wrap(out, lhs, src, st=True):
         for p in range(16):
-            mm(out, lhs[:, 128 * p:128 * p + 128], src_of(p), p == 0, p == 15, rd, wr)
+            mm(out, X(lhs, 128 * p, 128 * p + 128), sub(src, p, cols(src), 16), st and p == 0, p == 15)
 
-    def unlane(out, src_of, rd, wr):
-        for k in range(8):
-            mm(out, T.selg[:, 128 * k:128 * k + 128], src_of(k), k == 0, k == 7, rd + " selg", wr)
+    def unwrap(out, lhs, src, st=True):
+        for p in range(16):
+            mm(sub(out, p, cols(out), 16), X(lhs, 128 * p, 128 * p + 128), src, st and p == 0, p == 15)
 
-    def dword(w, h, k):
-        sw = T.sel1 if w else T.sel0
-        mm(T.P6[:, 256 * w + 128 * h:256 * w + 128 * h + 128], sw[:, 128 * k:128 * k + 128],
-           T.EQ[:, 256 * k + 128 * h:256 * k + 128 * h + 128], False, False,
-           ("EQb%d EQc%d" % (k, k) if h else "EQa%d" % k) + " sel%d" % w, "@6 D")
+    def pairs(E, rep, key, gate, c, lo, hi, st=False, sp=False):
+        o = X(E, 256 * c + lo, 256 * c + hi)
+        if gate:
+            ts(o, X(rep, lo, hi), X(key, c, c + 1), ALU.is_equal, X(gate, c, c + 1), ALU.mult)
+        else:
+            ts(o, X(rep, lo, hi), X(key, c, c + 1), ALU.is_equal)
+        if key == "key":
+            count(E, "rw", c, lo, hi, st)
 
-    def pairs(E, en, keyrep, key, gate, bank, bn, rd, last, extra=(), hooks={}):
-        extra = list(extra)
-        for c in range(16):
-            lo = 0 if c < 4 else 64 if c < 8 else 128
-            o = E[:, 256 * c + lo:256 * c + 256]
-            nm = "%s%d" % (en, c)
-            kcol = T.key[:, key + c:key + c + 1]
-            if gate is None:
-                ts(o, keyrep[:, lo:256], kcol, ALU.is_equal, rd, nm)
-            else:
-                ts(o, keyrep[:, lo:256], kcol, ALU.is_equal, rd, nm, gate[:, c:c + 1], ALU.mult)
-            w = T.rw[:, 64 * (c % 8):64 * (c % 8) + 64]
-            if c < 8:
-                mm(bank[lo:128, 0:64], E[:, 256 * c + lo:256 * c + 128], w, False, False, nm + " rw", bn)
-                w = T.rw[:, 512:576]
-            mm(bank[:, 64:128], E[:, 256 * c + 128:256 * c + 256], w, False, last and c == 15, nm + " rw", bn)
-            if extra:
-                dword(*extra.pop(0))
-            if c in hooks:
-                hooks[c]()
+    def count(E, rw, c, lo, hi, st=False):
+        if lo < 128:
+            lo = lo // 64 * 64
+            mm(X("P4", 0, 64, 1, (lo, 128)), X(E, 256 * c + lo, 256 * c + 128), X(rw, 64 * c, 64 * c + 64), st)
+        if hi > 128:
+            k = (c - 8 if c >= 8 else 8) if rw == "rw" else c + 8
+            mm(X("P4", 64, 128), X(E, 256 * c + 128, 256 * c + 256), X(rw, 64 * k, 64 * k + 64))
 
-    x = T.R[:, 2304:2560]
-    pm, pg = T.col[:, 1:2], T.col[:, 2:3]
-    dma("y", x, T.x0[:], "", "Rx")
-    dma("y", T.edi[:], T.edge0[:], "", "edi")
-    ms(T.v0i[:], 0, "v0i")
-    dma("s", T.v0i[0:128:16, :], T.v0[:], "v0i", "v0i")
-    dma("s", T.reci[:, 0:1024], T.rec0[:, 0:1024], "", "reci0")
-    dma("y", T.reci[:, 1024:2048], T.rec0[:, 1024:2048], "", "reci1")
-    dma("y", T.vei[:], T.ver0[:], "", "vei")
-    dma("y", T.EF[:, 0:128], T.eff[:], "", "EF")
-    iota(T.coli[:, 0:1], [[0, 1]], 0, 1, "coli0", False)
-    iota(T.xm[:], [[0, 32], [1, 8]], 0, 0, "xm")
-    iota(T.wex[:, 0:8], [[16, 8]], 0, 0, "wex")
-    iota(T.tmpb[:, 16:800], [[0, 49], [1, 16]], 0, 0, "tb16")
-    iota(T.tmpf[:], [[1, 128]], 0, -1, "tmpf")
-    iota(T.IOT[:], [[1, 2048]], -2048, 0, "IOT")
-    iota(T.zer[:], [[0, 512]], 0, 0, "zer")
-    iota(T.kc[:], [[0, 8], [2048, 16]], 0, 0, "kc")
-    iota(T.tmpc[:], [[-16, 8], [16, 8], [1, 16]], 0, 0, "tmpc")
-    iota(T.tm[:], [[0, 2], [1, 8], [0, 8]], 0, 0, "tm")
-    iota(T.tmpd[:, 0:128], [[1, 8], [0, 16]], 0, 0, "tmpd")
-    iota(T.lane[:], [[16, 16]], 0, 0, "lane")
-    iota(T.tc[:], [[1, 8], [16, 2]], 0, 0, "tc")
-    for buf, val, nm in ((T.seg[:], 0, "seg"), (T.seg[:, 0::16], 2 ** 22, "seg"), (T.R[:, 2048:2304], 0, "Rz"), (T.R[:, 2560:2576], 5, "R5"),
-                         (T.IP[:, 784:800], 0, "IPz"), (T.key[:, 32:48], 0, "key2"), (T.SU[:, 2048:2304], 0, "SUz"),
-                         (T.c2k[:], 2048, "c2k"), (T.jd[:, 32:48], PARTS[0][0], "jd2"), (T.VL[:, 512:768], 0, "VLz")):
-        iota(buf, [[0, buf.shape[1]]], val, 0, nm)
-    ms(T.sel[:], 0.0, "sel")
-    ts(T.coli[:, 1:2], T.coli[:, 0:1], 15, ALU.bitwise_and, "coli0", "coli1")
-    ts(T.coli[:, 2:3], T.coli[:, 0:1], 4, ALU.arith_shift_right, "coli0", "coli2")
-    ts(T.coli[:, 3:4], T.coli[:, 0:1], 7, ALU.bitwise_and, "coli0", "coli3")
-    cp(T.col[:, 0:4], T.coli[:, 0:4], "coli0 coli1 coli2 coli3", "col")
-    ts(T.xm[:], T.xm[:], pg, ALU.is_equal, "xm col", "xm")
-    ts(T.col[:, 4:5], pm, 2.0, ALU.mult, "col", "col4", 1.0, ALU.add)
-    b8 = T.xm[:, 0:8]
-    for p in range(16):
-        cp(T.sel[:, 129 * p:128 * p + 128:16], b8, "xm sel", "sel_%d" % p)
-    selall = " ".join("sel_%d" % p for p in range(16))
-    ts(T.col[:, 5:6], pm, -LN3, ALU.mult, "col", "col5", 56 * LN3, ALU.add)
-    ts(T.col[:, 6:7], T.col[:, 0:1], -LN3, ALU.mult, "col", "col6", 56 * LN3 + math.log(3.5), ALU.add)
-    act(T.pw[:, 0:1], T.col[:, 3:4], "col", "pw", AF.Exp, scale=math.log(4.0))
-    act(T.ex[:], x, "Rx col4", "ex", scale=T.col[:, 4:5])
-    cp(T.prod[:], T.v0i[:], "v0i", "prod")
-    act(T.wex[:, 8:16], T.wex[:, 0:8], "wex col5", "wex2", AF.Exp, bias=T.col[:, 5:6], scale=-LN3)
-    act(T.col[:, 7:8], T.col[:, 6:7], "col6", "col7", AF.Exp)
-    ts(T.SU[:, 0:512], T.edi[:], -2048.0, ALU.add, "edi", "SU")
-    ts(T.IP[:, 0:784], T.tmpb[:, 16:800], pm, ALU.is_equal, "tb16 col", "IP")
-    act(T.SU[:, 512:1024], T.SU[:, 0:512], "SU", "SUb")
-    ts(T.idb[:], T.tmpf[:], 0.0, ALU.is_equal, "tmpf", "idb")
+    def col(k):
+        return X("col", k, k + 1)
+
+    x, xP = X("xx", 0, 256), X("P0", 0, 512, 2)
+    R, SU = X("RR", TAB, TAB + 2048), X("SS", TAB, TAB + 2048)
+    pm, pg, b8 = col(1), col(2), X("xm", 0, 8)
+    idb, idf = X("idb"), X("idf")
+    dma("y", X("xx", 256, 512), T.x0[:], 65536)
+    dma("y", X("edi"), T.edge0[:], 262144)
+    ms(X("v0i"), 0)
+    op("s", lambda: S.dma_start(T.v0i[0:128:16, :], T.v0[:]), [], [X("v0i")], (100.0, 2000.0), "d")
+    dma("s", X("reci", 0, 1024), T.rec0[:, 0:1024], 262144)
+    dma("y", X("reci", 1024, 2048), T.rec0[:, 1024:2048], 262144)
+    dma("y", X("vei"), T.ver0[:], 262144)
     for k in range(4):
-        n = 128 << k
-        dma("y", T.EF[:, n:2 * n], T.EF[:, 0:n], "EF", "EF")
+        dma("y", X("EF", 128 * k, 128 * k + 128), T.eff[:], 32768)
+    for n in (512, 1024):
+        dma("y", X("EF", n, 2 * n), X("EF", 0, n), 256 * n)
+    iota(X("coli", 0, 1), [[0, 1]], 0, 1)
+    iota(X("xm"), [[0, 8], [1, 8]], 0)
+    iota(X("tmpb", 0, 784), [[0, 49], [1, 16]], 0)
+    iota(X("tmpf"), [[1, 128]], 0, -1)
+    fill(X("one", 0, 128), 1)
+    iota(X("wex", 0, 8), [[16, 8]], 0)
+    iota(X("tmpd"), [[1, 8], [0, 16]], 0)
+    iota(X("kc", 0, 128), [[0, 8], [2048, 16]], 0)
+    iota(X("lane"), [[16, 16]], 0)
+    fill(X("RR", 2304, 2320), 5)
+    fill(X("RR", 2320, 2576), 0)
+    fill(X("seg"), 0)
+    fill(X("seg", 0, 128, 16), 2 ** 22)
+    iota(X("tm"), [[0, 2], [1, 8], [0, 8]], 0)
+    fill(X("SS", 2304, END), 0)
+    fill(X("VL", 512, 768), 0)
+    fill(X("selg"), 0)
+    ms(X("sel"), 0.0)
+    ts(X("coli", 1, 2), X("coli", 0, 1), 15, ALU.bitwise_and)
+    ts(X("coli", 2, 3), X("coli", 0, 1), 4, ALU.arith_shift_right)
+    ts(X("coli", 3, 4), X("coli", 0, 1), 7, ALU.bitwise_and)
+    cp(X("col", 0, 4), X("coli"))
+    ts(X("xm"), X("xm"), pg, ALU.is_equal)
+    ts(col(4), pm, 2.0, ALU.mult, 1.0, ALU.add)
+    for p in range(16):
+        cp(X("sel", 129 * p, 128 * p + 128, 16), b8)
+    ts(col(5), pm, -LN3, ALU.mult, 56 * LN3, ALU.add)
+    ts(col(6), col(0), -LN3, ALU.mult, 56 * LN3 + math.log(3.5), ALU.add)
+    act(X("pw", 0, 1), col(3), AF.Exp, scale=math.log(4.0))
+    ops[-1] = ops[-1][:5] + ((1400.0, 0.0), (0, 0))
+    act(X("ex"), X("xx", 256, 512), scale=col(4))
+    cp(X("prod"), X("v0i"))
+    act(X("wex", 8, 16), X("wex", 0, 8), AF.Exp, bias=col(5), scale=-LN3)
+    act(col(7), col(6), AF.Exp)
+    act(x, X("xx", 256, 512), AF.Silu, bias=XO)
+    ops[-1] = ops[-1][:2] + (ops[-1][2] + [X("pw", 0, 1), X("wex", 8, 16), col(7)],) + ops[-1][3:5] + ((1800.0, 0.0), (0, 0))
+    ts(sub(SU, 0, 512), X("edi"), -2048.0, ALU.add)
+    ts(X("IP", 0, 784), X("tmpb", 0, 784), pm, ALU.is_equal)
+    act(sub(SU, 512, 1024), sub(SU, 0, 512))
+    ts(idb, X("tmpf"), 0.0, ALU.is_equal)
+    ts(sub(SU, 1024, 1536), X("edi"), -2048.0, ALU.add)
+    act(sub(SU, 1536, 2048), sub(SU, 0, 512))
+    for k in range(2):
+        ts(X("G", 1024 * k, 1024 * k + 1024), X("reci", 1024 * k, 1024 * k + 1024), 8.0, ALU.is_ge, VOID, ALU.mult)
+    for k in range(4):
+        bk = X("P%d" % (4 + k))
+        mm(bk, idb, X("reci", 512 * k, 512 * k + 512), True)
+        mm(bk, idb, X("G", 512 * k, 512 * k + 512), False, True)
+        if k < 3:
+            act(sub(R, 512 * k, 512 * k + 512), bk, bias=XO)
+        else:
+            ts(sub(R, 512 * k, 512 * k + 512), bk, XO, ALU.add)
+    ts(X("VL", 0, 512), X("vei"), VO, ALU.add)
+    ts(idf, X("tmpf"), 0.0, ALU.is_equal)
+    for k, val in enumerate((-2.0 ** 15 / VOID, -2.0 ** 20, -2.0 ** 20 / VOID)):
+        ts(X("b8", 8 * k, 8 * k + 8), b8, val, ALU.mult)
+    b8v, b8x, b8xv = X("b8", 0, 8), X("b8", 8, 16), X("b8", 16, 24)
+    ts(col(8), pm, 8.0, ALU.is_ge, 2.0, ALU.mult)
+    ts(col(9), pm, 8.0, ALU.is_lt, X("pw", 0, 1), ALU.mult)
+    ts(col(10), col(8), X("pw", 0, 1), ALU.mult)
+    ts(X("rE", 0, 8), b8, -32768.0, ALU.mult)
+    ts(X("rE", 8, 16), b8, col(9), ALU.mult, -1.0, ALU.mult)
+    ts(X("rE", 16, 24), b8, col(10), ALU.mult, -1.0, ALU.mult)
+    act(col(12), X("idf", 0, 1), scale=2.0 ** 24)
+    act(col(13), X("idf", 1, 2), bias=col(12), scale=-17 * 2.0 ** 15)
+    act(col(14), X("idf", 2, 3), bias=col(13), scale=2.0 ** 11)
+    act(col(15), X("idf", 3, 4), bias=col(14), scale=-15 * BIG)
+    act(X("cw"), X("one", 0, 8), scale=col(15))
+    ts(X("rw", 512, 576), X("xm"), float(2 ** 95), ALU.mult)
+    for k in range(8):
+        act(X("rw", 64 * k, 64 * k + 64), X("xm"), scale=X("wex", 8 + k, 9 + k))
+    for k in range(8):
+        act(X("selg", 144 * k, 144 * k + 16), X("IP", 0, 16))
+    ts(X("xw", 192, 256), X("tm", 0, 64), pg, ALU.is_equal)
+    ts(X("tm"), X("tm"), pg, ALU.is_equal, col(7), ALU.mult)
+    ts(X("lane"), X("lane"), pm, ALU.add)
+    ms(X("tha"), 11.5)
+    ts(X("bo"), X("tmpd"), pg, ALU.is_equal)
+    ts(X("tri"), X("tmpb", 0, 256), pm, ALU.is_le, 4096.0, ALU.mult)
+    ts(col(11), pm, 2048.0, ALU.add)
+    ts(col(16), pm, 2064.0, ALU.add)
+    for k in range(4):
+        act(X("selj", 512 * k, 512 * k + 512), X("sel", 512 * k, 512 * k + 512), scale=col(4))
+    dma("y", X("IP", 784, 1568), X("IP", 0, 784), 200000)
+    iota(X("IOB"), [[1, 512]], -256)
+    for p in range(16):
+        ts(X("selT", 128 * p, 128 * p + 128), X("bo"), X("IP", p, p + 1), ALU.mult)
+    select(X("selD"), X("selT"), [[0, 16], [-1, 128]], ALU.not_equal, -1.0, 0, 1)
+    act(X("xw", 0, 64), X("xm"), scale=col(4))
+    act(X("xw", 64, 128), X("xw", 0, 64), scale=-2.0)
+    fill(X("xw", 128, 192), -(256 * int(XO) + 512) // 128)
+    iota(X("IOT"), [[1, 2048]], 0)
+    iota(X("an"), [[1, 16]], 0)
+    cp(X("xl"), X("an"))
+    for nm, val in (("idM", -BIG / 2), ("idH", BIG / 2), ("id1", -1.0), ("id2", -2.0), ("id5", -512.0), ("idV", VOID), ("idQ", 2 * BIG), ("idR", -2 * BIG), ("id32", 32.0), ("idN", -BIG), ("idP", BIG)):
+        act(X(nm), idb, scale=val)
+    act(X("col", 24, 32), b8)
+    ts(X("bo01", 0, 128), X("bo"), col(9), ALU.mult, -1.0, ALU.mult)
+    ts(X("bo01", 128, 256), X("bo"), col(10), ALU.mult, -1.0, ALU.mult)
+    act(X("bo19"), X("bo"), scale=2.0 ** 19)
+    for k, (sc, bi) in enumerate(((0, 1.5 * BIG - 256 * XO), (1, 1.5 * BIG), (0, 1.5 * BIG - TAB), (1, 1.5 * BIG),
+                                  (0, 2.5 * BIG), (0, 2 * BIG + 256))):
+        act(X("AC", 16 * k, 16 * k + 16), X("lane"), bias=float(bi), scale=float(sc))
+    for k, sc, bi in ((1, 1, 256), (3, 8, TAB), (4, 1, 2064), (5, 1, 512)):
+        act(X("BT", 16 * k, 16 * k + 16), X("lane"), bias=float(bi), scale=float(sc))
 
-    def init_records():
-        ts(T.SU[:, 1024:1536], T.edi[:], -2048.0, ALU.add, "edi", "SUd")
-        act(T.SU[:, 1536:2048], T.SU[:, 0:512], "SU", "SUe")
-        ts(T.G[:, 0:1024], T.reci[:, 0:1024], 8.0, ALU.is_ge, "reci0", "G0", VOID, ALU.mult)
-
-    def init_records_2():
-        ts(T.G[:, 1024:2048], T.reci[:, 1024:2048], 8.0, ALU.is_ge, "reci1", "G1 Gv", VOID, ALU.mult)
-        for k in range(4):
-            bk = T["P%d" % (4 + k)]
-            mm(bk[:], T.idb[:], T.reci[:, 512 * k:512 * k + 512], True, False, "idb reci%d" % (k // 2), "@%d" % (4 + k))
-            mm(bk[:], T.idb[:], T.G[:, 512 * k:512 * k + 512], False, True, "idb G0" if k < 2 else "idb G1 Gv", "@%d ri%d" % (4 + k, k))
-        for k in range(4):
-            o, i = T.R[:, 512 * k:512 * k + 512], T["P%d" % (4 + k)][:]
-            (act if k < 3 else cp)(o, i, "@%d ri%d" % (4 + k, k), "R" if k == 3 else "Ri%d" % k)
-            if k == 2:
-                cp(T.VL[:, 0:512], T.vei[:], "vei", "VL")
-
-    def constants_1():
-        ts(T.idf[:], T.tmpf[:], 0.0, ALU.is_equal, "tmpf", "idf")
-        ts(T.b8[:, 8:16], b8, -32768.0, ALU.mult, "xm", "b8e")
-        ts(T.b8[:, 16:24], b8, -1.0 / 32768.0, ALU.mult, "xm", "b8v")
-        ts(T.rw[:, 512:576], T.xm[:, 0:64], float(2 ** 95), ALU.mult, "xm", "rwB")
-        for k in range(8):
-            ts(T.rw[:, 64 * k:64 * k + 64], T.xm[:, 0:64], T.wex[:, 8 + k:9 + k], ALU.mult, "xm wex2", "rw" if k == 7 else "rw_%d" % k)
-        ops[-1][2].extend(["rwB"] + ["rw_%d" % k for k in range(7)])
-
-    def constants_2():
-        ts(T.selg[:], T.tmpc[:], pm, ALU.is_equal, "tmpc col", "selg")
-        ts(T.tm[:], T.tm[:], pg, ALU.is_equal, "tm col col7", "tm", T.col[:, 7:8], ALU.mult)
-        ts(T.col[:, 8:9], pm, 8.0, ALU.is_ge, "col", "col8", 8.0, ALU.mult)
-        ts(T.lane[:], T.lane[:], pm, ALU.add, "lane col", "lane")
-        ts(T.xl[:], T.tc[:], T.col[:, 8:9], ALU.add, "tc col8", "xl")
-        ms(T.tha[:], -11.5, "tha")
-        ts(T.id2[:], T.idb[:], -2.0, ALU.mult, "idb", "id2")
-        ts(T.idp[:], T.idb[:], 2.0, ALU.mult, "idb", "idp")
-        ts(T.col[:, 9:10], pm, 8.0, ALU.is_lt, "col pw", "col9", T.pw[:, 0:1], ALU.mult)
-        ts(T.col[:, 10:11], T.col[:, 8:9], 0.25, ALU.mult, "col8 pw", "col10", T.pw[:, 0:1], ALU.mult)
-        ts(T.bo[:], T.tmpd[:, 0:128], pg, ALU.is_equal, "tmpd col", "bo")
-        ts(T.col[:, 11:13], T.col[:, 9:11], -1.0, ALU.mult, "col9 col10", "col11")
-        ts(T.cfd[:, 0:1], pm, -784.0, ALU.add, "col", "cfd", 1.0 / 4096.0, ALU.mult)
-        ts(T.cb[:, 32:48], T.lane[:], 8.0, ALU.mult, "lane", "cb2")
-        ts(T.id5[:], T.idb[:], -512.0, ALU.mult, "idb", "id5")
-
-    def constants_3():
-        for k, bi in ((0, 2048.0), (1, 512.0), (3, 2048.0)):
-            act(T.cb[:, 16 * k:16 * k + 16], T.lane[:], "lane", "cb%d" % k, bias=bi)
-        for k, (sc, bi) in enumerate(((1.0, 0.0), (1.0, 256.0), (7.0, -2304.0), (1.0, 0.0))):
-            act(T.cd[:, 16 * k:16 * k + 16], T.lane[:], "lane", "cd%d" % k, bias=bi, scale=sc)
-        act(T.j0[:, 32:48], T.lane[:], "lane", "j02")
-        act(T.nidf[:], T.idf[:], "idf", "nidf", scale=-1.0)
-        act(T.b8f[:], b8, "xm", "b8f")
-        act(T.bo0[:], T.bo[:], "bo col9", "bo0", scale=T.col[:, 9:10])
-        act(T.bo1[:], T.bo[:], "bo col10", "bo1", scale=T.col[:, 10:11])
-
-    def constants_4():
-        tt(T.bofd[:], T.bo[:], T.idb[:], ALU.subtract, "bo idb", "bofd")
-        ts(T.bofd[:], T.bofd[:], float(2 ** 20), ALU.mult, "bofd", "bofd")
-
-    Rall = "R Ri0 Ri1 Ri2"
-    jL, vL, xiL = T.jvL[:, 0:16], T.jvL[:, 16:32], T.jvL[:, 32:48]
-    bL, wL = T.bL[:, 0:16], T.bL[:, 16:32]
-
-    def early_in(s):
-        o = s * SW
-        arrive(s, 0)
-        arrive(s, 1)
-        la = "L%d_0 L%d_1" % (s, s)
-        wrap(T.P1[:, 384:418], T.selj, lambda p: T.land[:, o + p:o + 544:16], la + " selj", "@1 jw")
-        mm(T.P1[:, 418:434], T.idf[:], T.cb[:, 32:48], True, True, "idf cb2", "@1 jw")
-        mm(T.P1[:, 434:450], T.idb[:], T.land[:, o + 256:o + 272], True, False, la + " idb", "@1 jw")
-        mm(T.P1[:, 434:450], T.idb[:], T.land[:, o + 272:o + 288], False, True, la + " idb", "@1 jw")
-        act(T.j0[:, 0:16], T.P1[:, 384:400], "@1 jw", "j00")
-        act(T.j0[:, 16:32], T.P1[:, 434:450], "@1 jw", "j01")
-
-    def flags_in(s):
-        o = s * SW
-        tt(T.jd[:, 0:32], T.P1[:, 402:434], T.j0[:, 0:32], ALU.subtract, "@1 jw j00 j01", "jd0")
-        arrive(s, 2)
-        for k in range(3):
-            mm(T.P3[:, 16 * k:16 * k + 16], T.idb[:], T.land[:, o + 576:o + 592], True, True, "idb L%d_2" % s, "@3 c3")
-        tt(T.jf[:], T.P3[:, 0:48], T.jd[:], ALU.mult, "@3 c3 jd0 jd2", "jf")
-        tt(T.jf[:], T.jf[:], T.j0[:], ALU.add, "jf j00 j01 j02", "jf")
-        cp(T.jvL[:], T.jf[:], "jf", "jvL")
-
-    def take_x(s):
-        act(x, T.land[:, s * SW:s * SW + 544].indirect(xiL), "L%d_0 L%d_1 jvL" % (s, s), "Rx")
-
-    def equal_x(out, rec, rd, wr):
-        mm(T.P7[:, 0:256], T.id2[:], x, True, False, "id2 Rx", "@7 dx")
-        mm(T.P7[:, 0:256], T.idp[:], rec, False, True, "idp " + rd, "@7 dx")
-        act(T.sb[:], T.P7[:, 0:256], "@7 dx", "sb", AF.Abs)
-        act(out, T.sb[:], "sb", wr, AF.Relu, bias=1.0, scale=-1.0)
-
-    late = []
+    bL, wL = X("bL", 0, 16), X("bL", 16, 32)
     for t in range(NT):
         o = t * SW
-        flg = T.msg[:, o + 544:o + 608]
-        gen, may, cl, first = [T.msg[:, o + 544 + 16 * k:o + 560 + 16 * k] for k in range(4)]
+        lst = part(t - 1, 2)[0] if t else X("lland", NT * LW, NT * LW + LW)
+        jL, xiL, vL = sub(lst, 0, 16), sub(lst, 16, 32), sub(lst, 32, 48)
         if t == 0:
-            wrap(T.P3[:, 16:32], T.sel, lambda p: T.prod[:, p::16], "prod " + selall, "@3 vw")
-            wrap(T.P3[:, 0:16], T.sel, lambda p: T.ex[:, p::16], "ex " + selall, "@3 jw0")
-            cp(T.jvL[:, 0:32], T.P3[:, 0:32], "@3 jw0 vw", "jvL")
-            cp(T.jf[:, 0:32], T.P3[:, 0:32], "@3 jw0 vw", "jf")
-        else:
-            flags_in(t - 1)
-        act(T.jm[:], T.IP[:, 0:784].indirect(jL), "IP jvL", "jm")
-        if t == 0:
-            init_records()
-        else:
-            take_x(t - 1)
-            late[0]()
-        tt(T.prod[:], T.SU[:, 0:2048].indirect(vL), T.jm[:], ALU.mult, "SU SUb SUd SUe jvL jm", "prod")
-        wrap(T.P3[:, 48:64], T.sel, lambda p: T.prod[:, p::16], "prod " + selall, "@3 ew")
-        mm(T.P0[:, 0:256], T.idb[:], x, True, True, "Rx idb", "@0 xP")
-        if t == 0:
-            init_records_2()
-        act(T.repg[:], T.IOT[:].indirect(vL), "IOT jvL", "repg")
-        act(T.key[:, 48:64], T.jf[:, 16:32], "jf", "key3", bias=-2048.0)
-        if t == 0:
-            constants_1()
-        else:
-            late[1]()
-        ew = T.P3[:, 48:64]
-        cp(T.ei[:], ew, "@3 ew", "ei")
-        ts(wL, ew, 2048.0, ALU.add, "@3 ew", "wL", 2047.0, ALU.min)
-        ts(T.bi[:], T.ei[:], 511, ALU.bitwise_and, "ei", "bi")
-        cp(bL, T.bi[:], "bi", "bL")
-        act(T.kw[:, 256:512], T.R[:, 0:2048].indirect(wL), Rall + " wL", "kw1")
-        act(T.wW[:], ew, "@3 ew", "wW", bias=2048.0)
-        act(T.tb[:], ew, "@3 ew", "tb", AF.Relu, bias=1.0)
-        ts(T.key[:, 16:32], T.bi[:], -256.0, ALU.add, "bi", "key1")
-        cp(T.verL[:], T.VL[:, 0:512].indirect(bL), "VL bL", "verL")
-        for nm, a, b in (("G0", 0, 64), ("G1", 64, 128 - GV), ("G2", 128, 192), ("G3", 192, 256)):
-            act(T.G[:, 16 * a:16 * b], T.R[:, 0:2048].indirect(T.verL[:, a:b]), Rall + " verL", nm)
-        if KWV:
-            tt(T.kw[:, 0:256], T.kw[:, 256:512], T.P0[:, 0:256], ALU.is_equal, "kw1 @0 xP", "kw0")
-        cp(T.verf[:], T.verL[:], "verL", "verf")
-        mm(T.P5[:, 0:128], T.idb[:], T.zer[:, 0:128], True, False, "idb zer", "@5 sv")
-        if KWV:
-            wrap(T.P3[:, 64:96], T.sel, lambda p: T.kw[:, p::16], "kw0 kw1 " + selall, "@3 kn")
+            wrap(X("P3", 16, 32), "sel", X("prod"))
+            wrap(X("P3", 0, 16), "sel", X("ex"))
+            cp(jL, X("P3", 0, 16))
+            cp(vL, X("P3", 16, 32))
+            cp(X("ei"), X("P3", 16, 32))
+            ts(X("bi"), X("ei"), 511, ALU.bitwise_and)
+            cp(X("cL"), X("bi"))
+        urge[0] = t + 1
+        level(0)
+        x = X("xx", 256 * (t % 2), 256 * (t % 2) + 256)
+        for c0, c1 in zip(FIRST, FIRST[1:]):
+            u, v = 16 * c0, 16 * c1
+            act(X("jm", u, v), by(X("IP", 0, 1568 if t else 784), sub(jL, c0, c1)), bias=BIG, scale=-2 * BIG)
+            tt(X("prod", u, v), by(SU, sub(vL, c0, c1)) if t else by(sub(SU, 0, 512), X("cL", c0, c1)), X("jm", u, v), ALU.max)
+            if t and c1 == 16:
+                (act if XS else cp)(x, by(X("land", o - SW, o), xiL))
+            ew = X("P3" if c0 == 0 else "P5", c0, c1)
+            wrap(ew, "sel", X("prod", u, v))
+            cp(X("ei", c0, c1), ew)
+            ts(X("bi", c0, c1), X("ei", c0, c1), 511, ALU.bitwise_and)
+            cp(sub(bL, c0, c1), X("bi", c0, c1))
+            ts(X("verL", u, v), by(X("VL", 0, 512), sub(bL, c0, c1)), -VO, ALU.add)
+            ts(sub(wL, c0, c1), ew, 2048.0 - 15 * BIG, ALU.add, 2048.0, ALU.min)
+        select(X("RR", 0, TAB), x, [[0, 256]], ALU.is_ge, 0.0, 0, 0)
+        mm(xP, idb, x, True)
+        mm(X("P0", 1, 512, 2), idb, x)
+        for u, v in zip(CHUNKS, CHUNKS[1:]):
+            (cp if u == GV else act)(X("G", 16 * u, 16 * v), by(R, X("verL", u, v)))
+            if u == 0:
+                act(X("kw", 256, 512), by(X("RR", TAB, 2320), wL))
+        cp(X("verf"), X("verL"))
+        ts(X("keyb"), X("bi"), -256.0, ALU.add)
+        tt(X("kw", 0, 256), X("kw", 256, 512), xP, ALU.is_equal)
+        level(1)
+        cp(X("brep"), by(X("IOB"), bL))
+        for c in range(16 * RG):
+            pairs("Ea", "brep", "keyb", None, c, 128 if c >= 8 else 16 * c if t else c // 4 * 64, 256)
+
+        def patchers():
+            cp(X("vf"), vL)
+            mm(X("P4", 128, 384), idb, X("tri"), True)
+            unwrap(X("P4", 128, 384), "selD", X("vf"), False)
+            unwrap(X("P4", 384, 512), "selT", X("vf", 1, 16, 2), False)
+            for p in range(16):
+                mm(X("P4", 384 + p, 512, 16), X("id1"), X("vf", 0, 16, 2))
+            ts(X("E1"), X("P4", 128, 512), 0.0, ALU.is_equal, 4096.0, ALU.mult)
+            mm(X("P4", 0, 16), idb, X("vf"), True)
+            wrap(X("P4", 0, 16), "sel", X("E1", 0, 256), False)
+            wrap(X("P4", 1, 16, 2), "sel", X("E1", 256, 384), False)
+            for k in range(2):
+                ts(X("ptL", k, 16, 2), X("P4", k, 16, 2), col(11 + 5 * k), ALU.min)
+
+        if t:
+            patchers()
+        mmf(X("P6", 0, 64), idf, X("AC", 0, 64), True)
+        mm(X("P6", 64, 96), idf, X("AC", 64, 96))
+        mm(X("P6", 32, 48), idf, X("BT", 48, 64))
+        mm(X("P6", 80, 96), idb, X("keyb"))
+        efn, px = X("EF", t, 2048, 8), X("P7", 256, 512)
+        mm(px, idb, x, True)
+        mm(px, idb, efn, False, True)
+        act(X("sgb"), px, AF.Sign, bias=-3.5 - XO)
+        mm(px, idb, x, True)
+        mm(px, idb, efn)
+        mm(px, X("id2"), X("sgb"), False, True)
+        act(X("msg", o, o + 256), px, bias=-2.0)
+        send(t, 0)
+        wrap(X("P6", 0, 16), "selj", X("msg", o, o + 256), False)
         for h in range(2):
-            bk = T["P%d" % (1 + h)]
-            mm(bk[:, 0:128], T.idb[:], T.kc[:], True, False, "idb kc", "@%d sc%d" % (1 + h, h))
-            mm(bk[:, 0:128], T.verf[:, 128 * h:128 * h + 128], T.idf[:], False, False, "verf idf", "@%d sc%d" % (1 + h, h))
-        if t == 0:
-            constants_2()
-        if GV:
-            cp(T.G[:, 16 * (128 - GV):2048], T.R[:, 0:2048].indirect(T.verL[:, 128 - GV:128]), Rall + " verL", "Gv")
-        b8e, b8v = T.b8[:, 8:16], T.b8[:, 16:24]
-        todo = [(w, h, k) for h in range(2) for w in range(2) for k in range(16)]
-        if t == 0:
-            todo.sort()
-        mm(T.P6[:], T.idb[:], T.zer[:], True, False, "idb zer", "@6 D")
-        for k in range(16):
-            mm(T.P1[:, k:128:16], T.G[:, k:2048:16], b8v, False, False, "G0 G1 Gv b8v", "@1 sc0")
-        for k in range(16):
-            tt(T.EQ[:, 256 * k:256 * k + 128], T.G[:, k:2048:16], T.P0[:, 0:128], ALU.is_equal, "G0 G1 Gv @0 xP", "EQa%d" % k)
-            mm(T.P1[:, k:128:16], T.EQ[:, 256 * k:256 * k + 128], b8e, False, k == 15, "EQa%d b8e" % k, "@1 sc0")
-        if not KWV:
-            equal_x(T.kw[:, 0:256], T.kw[:, 256:512], "kw1", "kw0")
-            wrap(T.P3[:, 64:96], T.sel, lambda p: T.kw[:, p::16], "kw0 kw1 " + selall, "@3 kn")
-        act(T.brep[:], T.IOT[:, 0:512].indirect(bL), "IOT bL", "brep", bias=1792.0)
-        act(T.ta[:], T.P3[:, 80:96], "@3 kn", "ta", bias=-15.5, scale=1.0 / VOID)
-        efn = T.EF[:, t:2048:8]
-        for bk, nm in ((T.P7[:, 256:512], "@7 sxb"), (T.P4[:, 128:384], "@4 xnb")):
-            mm(bk, T.idb[:], x, True, False, "idb Rx", nm)
-            mm(bk, T.idb[:], efn, False, nm[1] == "7", "idb EF", nm)
-        act(T.sgb[:], T.P7[:, 256:512], "@7 sxb", "sgb", AF.Sign, bias=-3.5)
-        if t == 0:
-            act(T.sel0[:], T.sel[:], selall + " col11", "sel0", scale=T.col[:, 11:12])
-        for k in range(16):
-            tt(T.EQ[:, 256 * k + 128:256 * k + 192], T.G[:, 2048 + k:3072:16], T.P0[:, 128:192], ALU.is_equal, "G2 @0 xP", "EQb%d" % k)
-        scan(T.mn[:, 0:128], T.seg[:], T.P1[:, 0:128], "seg @1 sc0", "mn0")
-        for k in range(16):
-            mm(T.P2[:, k:128:16], T.G[:, 2048 + k:4096:16], b8v, False, False, "G2 G3 b8v", "@2 sc1")
-        for k in range(16):
-            tt(T.EQ[:, 256 * k + 192:256 * k + 256], T.G[:, 3072 + k:4096:16], T.P0[:, 192:256], ALU.is_equal, "G3 @0 xP", "EQc%d" % k)
-            mm(T.P2[:, k:128:16], T.EQ[:, 256 * k + 128:256 * k + 256], b8e, False, k == 15, "EQb%d EQc%d b8e" % (k, k), "@2 sc1")
-        mm(T.P4[:, 128:384], T.id2[:], T.sgb[:], False, True, "id2 sgb", "@4 xnb")
-        act(T.msg[:, o + 288:o + 544], T.P4[:, 128:384], "@4 xnb", "mb", bias=-2.0)
-        send(t, 0, "mb")
-        tt(T.ta[:], T.ta[:], T.P3[:, 64:80], ALU.add, "ta @3 kn", "ta")
-        scan(T.mn[:, 128:256], T.seg[:], T.P2[:, 0:128], "seg @2 sc1", "mn1")
-        tt(T.nk[:], T.ta[:], T.tb[:], ALU.is_lt, "ta tb", "nk")
-        cp(T.si[:], T.mn[:, 15::16], "mn0 mn1", "si")
-        act(T.thw[:], T.nk[:], "nk", "thw", bias=84.5, scale=-100.0)
-        ts(T.lm[:, 0:16], T.si[:], 2047, ALU.bitwise_and, "si", "lm0")
-        ts(T.lm[:, 16:32], T.si[:], 15, ALU.arith_shift_right, "si", "lm1")
-        tt(T.x1[:], T.lm[:].indirect(T.xl[:]), T.xm[:], ALU.mult, "lm0 lm1 xl xm", "x1")
-        unlane(T.P3[:, 96:128], lambda k: T.x1[:, 32 * k:32 * k + 32], "x1", "@3 wc")
-        mm(T.P4[:, 0:128], T.idb[:], T.zer[:, 0:128], True, False, "idb zer", "@4 sb")
-        mm(T.P1[:, 128:384], T.idb[:], x, True, False, "idb Rx", "@1 sx")
-        mm(T.P2[:, 128:384], T.idb[:], x, True, False, "idb Rx", "@2 xn")
-        if t == 0:
-            constants_4()
-            constants_3()
-        cw, mw = T.P3[:, 96:112], T.P3[:, 112:128]
-        cp(T.cL[:], cw, "@3 wc", "cL")
-        tt(T.base[:], cw, T.wW[:], ALU.subtract, "@3 wc wW", "base")
-        tt(T.want[:], mw, T.thw[:], ALU.is_ge, "@3 wc thw", "want")
-        tt(T.base[:], T.base[:], T.nk[:], ALU.mult, "base nk", "base")
-        ts(T.far[:], mw, T.tha[:, 0:1], ALU.is_ge, "@3 wc tha", "far", 4096.0, ALU.mult)
-        tt(T.base[:], T.base[:], T.wW[:], ALU.add, "base wW", "base")
-        tt(T.te[:, 0:16], cw, T.far[:], ALU.max, "@3 wc far", "te0")
-        cp(T.vnL[:, 16:32], T.base[:], "base", "baseL")
-        act(T.repf[:], T.IOT[:].indirect(T.cL[:]), "IOT cL", "repf")
-        act(T.ex[:], T.EF[:].indirect(T.vnL[:, 16:32]), "EF baseL", "ex")
-        act(T.key[:, 0:16], cw, "@3 wc", "key0", bias=-2048.0)
-        act(T.te[:, 16:32], T.far[:], "far cfd", "te1", bias=784.0, scale=T.cfd[:, 0:1])
-        act(T.msg[:, o + 256:o + 272], T.base[:], "base", "mh")
-
-        def h6():
-            mm(T.P1[:, 128:384], T.idb[:], T.ex[:], False, True, "idb ex", "@1 sx")
-            mm(T.P2[:, 128:384], T.idb[:], T.ex[:], False, False, "idb ex", "@2 xn")
-            act(T.sg[:], T.P1[:, 128:384], "@1 sx", "sg", AF.Sign, bias=-3.5)
-            act(T.suc[:], T.SU[:, 0:2048].indirect(T.cL[:]), "SU cL", "suc")
-
-        def h10():
-            ts(T.c2L[:], T.te[:], 2560.0, ALU.min, "te0 te1", "c2L")
-            tt(T.msg[:, o + 272:o + 288], T.base[:], T.msg[:, o + 256:o + 272], ALU.subtract, "base mh", "ml")
-
-        def h13():
-            mm(T.P2[:, 128:384], T.id2[:], T.sg[:], False, True, "id2 sg", "@2 xn")
-            act(T.msg[:, o:o + 256], T.P2[:, 128:384], "@2 xn", "mx", bias=-2.0)
-            send(t, 1, "mh ml mx")
-
-        pairs(T.Ea, "Ea", T.brep, 16, T.want, T.P4, "@4 sb", "brep key1 want", False, (), {6: h6, 10: h10, 13: h13})
-        cp(T.rep[:], T.repf[:], "repf", "rep")
-        act(T.rc[:], T.R[:, 0:2576].indirect(T.c2L[:, 0:16]), Rall + " Rz Rx R5 c2L", "rc")
-        act(T.sq[:], T.suc[:], "suc", "sq", bias=139.501, scale=1.0 / 512.0)
-        act(T.fd[:], T.IP[:].indirect(T.c2L[:, 16:32]), "IP IPz c2L", "fd")
-        tt(T.wf[:], T.want[:], T.far[:], ALU.min, "want far", "wf")
-        if t == 0:
-            act(T.sel1[:], T.sel[:], selall + " col11", "sel1", scale=T.col[:, 12:13])
-
-        pairs(T.Eb, "Eb", T.rep, 0, T.want, T.P4, "@4 sb", "rep key0 want", True)
-        tt(T.x2[:], T.P4[:, 0:128], T.tm[:], ALU.is_lt, "@4 sb tm", "x2")
-        unlane(T.P3[:, 128:144], lambda k: T.x2[:, k::8], "x2", "@3 nc")
-        tt(T.dif[:], T.key[:], T.cd[:], ALU.subtract, "key0 key1 key2 key3 cd0 cd1 cd2 cd3", "dif")
-        tt(T.dl[:], T.cb[:, 32:48], T.base[:], ALU.subtract, "base cb2", "dl")
-        nc = T.P3[:, 128:144]
-        tt(cl, nc, T.wf[:], ALU.mult, "@3 nc wf", "cl")
-        send(t, 2, "cl")
-        if EQV:
-            tt(T.eqc[:], T.rc[:], T.P0[:, 0:256], ALU.is_equal, "rc @0 xP", "eqc")
+            a = 128 * h
+            bk = "P%d" % (1 + h)
+            level(0)
+            mm(X(bk, 0, 128), X("verf", a, a + 128), idf, True)
+            pw = X(bk, 128, 136)
+            mm(pw, X("one", 0, 128), X("cw"))
+            mm(pw, X("prod", a, a + 128), b8)
+            mm(pw, X("kw", a, a + 128), b8x)
+            mm(pw, X("kw", 256 + a, 384 + a), b8xv)
+            if SPLIT[h] == 128:
+                mm(X(bk, 0, 128), idb, X("kc", 0, 128))
+            for u, v in [z for z in zip(CHUNKS, CHUNKS[1:]) if a <= z[0] < a + 128]:
+                for k in range(8):
+                    tt(X("EQ", 512 * k + 2 * u, 512 * k + 2 * v), X("G", 16 * u + k, 16 * v, 8), X("P0", 2 * u, 2 * v), ALU.is_equal)
+            for u, v in ((0, SPLIT[h]), (SPLIT[h], 128))[:1 + (SPLIT[h] < 128)]:
+                for k in range(16):
+                    mm(X(bk, k, 128, 16, (u, v)), X("G", 16 * (a + u) + k, 16 * (a + v), 16), b8v)
+                for k in range(16):
+                    at = 512 * (k // 2) + 2 * a + k % 2
+                    mm(X(bk, k // 2 + 8 * (k % 2), 128, 16, (u, v)), X("EQ", at + 2 * u, at + 2 * v - k % 2, 2), X("rE", 0, 8))
+            if SPLIT[h] < 128:
+                mm(X(bk, 0, 128), idb, X("kc", 0, 128))
+            e = 8 * h
+            scan(X("mn", a, a + 128), X("seg"), X(bk, 0, 128))
+            si = X("si", e, e + 8)
+            tt(si, X("mn", a + 15, a + 128, 16), pw, ALU.min)
+            ts(X("lm", 2 * e, 2 * e + 8), si, 2047, ALU.bitwise_and)
+            ts(X("lm", 2 * e + 8, 2 * e + 16), si, 15, ALU.arith_shift_right)
+            tt(X("um", 2 * a, 2 * a + 256), by(X("lm", 2 * e, 2 * e + 16), X("xl")), X("IP", 0, 256), ALU.mult)
+            cw, mw = X("P3", 16 + 2 * e, 24 + 2 * e), X("P3", 24 + 2 * e, 32 + 2 * e)
+            mm(cw, X("um", 2 * a, 2 * a + 128), b8, True)
+            mm(mw, X("um", 2 * a + 128, 2 * a + 256), b8)
+            cL = X("cL", e, e + 8)
+            cp(cL, cw)
+            ts(X("gate", e, e + 8), mw, -15.0, ALU.is_ge)
+            cp(X("key", e, e + 8), cw)
+            act(X("farb", e, e + 8), mw, AF.Sign, bias=X("tha", 0, 1))
+            if REPV[h]:
+                cp(X("ux"), by(X("lm", 2 * e, 2 * e + 16), X("xl", 0, 8)))
+                mm(X("P5", 256, 384), X("ux"), idb, True)
+                cp(X("urep", a, a + 128), X("P5", 256, 384))
+            else:
+                act(X("repf", a, a + 128), by(X("IOT"), cL))
+                cp(X("urep", a, a + 128), X("repf", a, a + 128))
+            level(1)
+            if not RG:
+                for c in range(8 * h, 8 * h + 8):
+                    lo = 128 if h else 16 * c if t else c // 4 * 64
+                    pairs("Ea", "brep", "keyb", "gate", c, lo, 256)
+                    count("Ea", "rw", c, lo, 256, c == 0)
+                for c in range(8 + 8 * h):
+                    pairs("Eb", "urep", "key", "gate", c, 128 if h else c // 4 * 64, 128 + 128 * h)
+            elif h == 0:
+                for c in range(8):
+                    pairs("Eb", "urep", "key", "gate", c, c // 4 * 64, 128, c == 0)
+                for c in range(8):
+                    act(X("rg", 64 * c, 64 * c + 64), X("rw", 64 * c, 64 * c + 64), scale=X("gate", c, c + 1))
+                    act(X("rg", 512 + 64 * c, 576 + 64 * c), X("rw", 512, 576), scale=X("gate", c, c + 1))
+                    count("Ea", "rg", c, 16 * c, 256)
+            else:
+                for c in range(8, 16):
+                    act(X("rg", 512 + 64 * c, 576 + 64 * c), X("rw", 64 * c - 512, 64 * c - 448), scale=X("gate", c, c + 1))
+                    count("Ea", "rg", c, 128, 256)
+                for c in range(16):
+                    pairs("Eb", "urep", "key", "gate", c, 128, 256)
+            xh, exh, px = sub(x, a, a + 128), X("ex", a, a + 128), X("P7", 256 + a, 384 + a)
+            act(exh, by(X("EF"), cL))
+            mm(px, idb, xh, True)
+            mm(px, idb, exh, False, True)
+            act(X("sg", a, a + 128), px, AF.Sign, bias=-3.5 - XO)
+            for k, z in enumerate((xh, X("one"), exh, X("sg", a, a + 128))):
+                mm(X("P7", 0, 64), z, X("xw", 64 * (0, 2, 0, 1)[k], 64 * (1, 3, 1, 2)[k]), k == 0)
+            tt(X("jx", 64 * h, 64 * h + 64), X("P7", 0, 64), X("xw", 192, 256), ALU.mult)
+            if h:
+                for k in range(8):
+                    mm(X("P7", 64, 80), X("selg", 128 * k, 128 * k + 128), X("jx", k, 128, 8), k == 0)
+                act(X("BT", 0, 16), X("P7", 64, 80), bias=784.0)
+            mm(px, idb, xh, True)
+            mm(px, idb, exh)
+            mm(px, X("id2"), X("sg", a, a + 128), False, True)
+            act(X("msg", o + 256 + a, o + 384 + a), px, bias=-2.0)
+            level(2)
+            act(X("rc", a, a + 128), by(R, cL))
+            tt(X("nec", a, a + 128), X("rc", a, a + 128), sub(xP, a, a + 128), ALU.not_equal)
+            act(X("suc", a, a + 128), by(SU, cL))
+            act(X("sq", a, a + 128), X("suc", a, a + 128), bias=139.501, scale=1.0 / 512.0)
+            px = X("P5", a, a + 128)
+            mm(px, X("id5"), X("sq", a, a + 128), True)
+            mmf(px, idf, X("suc", a, a + 128), False, True)
+            act(X("SS", a, a + 128), px, bias=512.0 * 140.0)
+        level(3)
+        mm(X("P0", 0, 256), X("id32"), X("IP", t, t + 256), True)
+        unwrap(X("P0", 0, 256), "selT", X("farb"), False)
+        act(X("sp"), X("P0", 0, 256), AF.Sign, bias=-32.0)
+        for h in range(2):
+            a, bk = 128 * h, "P%d" % (1 + h)
+            for k in range(16):
+                at = 512 * (k // 2) + 2 * a + k % 2
+                mm(X(bk, 128 + k // 2 + 8 * (k % 2), 384, 16), X("EQ", at, at + 256 - k % 2, 2), X("rE", 8, 24), k == 0)
+            mm(X(bk, 128, 384), X("nec", a, a + 128), X("bo01"))
+            mm(X(bk, 128, 256), X("sp", a, a + 128), X("bo19"), False, True)
+            d0, d1 = 256 * h, 256 * h + 128
+            ts(X("di", d0, d1), X(bk, 128, 256), float(0xAAAA + 2 ** 23), ALU.add)
+            ts(X("di", d1, d1 + 128), X(bk, 256, 384), float(2 * 0xAAAA), ALU.add)
+            ts(X("dy", d0, d1), X("di", d0, d1), 0xAAAA + 2 ** 20, ALU.bitwise_and)
+            ts(X("dy", d1, d1 + 128), X("di", d1, d1 + 128), 2 * 0xAAAA, ALU.bitwise_and)
+            tt(X("mm", a, a + 128), X("dy", d0, d1), X("dy", d1, d1 + 128), ALU.is_equal)
+        level(1)
+        send(t, 1)
+        act(X("BT", 32, 48), X("key"), bias=2048.0)
+        mm(X("P6", 64, 80), idf, X("key"))
+        for k in range(5):
+            mm(X("P6", 16 * k, 16 + 16 * k), X("idM" if k < 4 else "idH"), X("farb"))
+        act(X("gateb"), X("gate"))
+        for k in (4, 5):
+            mm(X("P6", 16 * k, 16 + 16 * k), X("idN"), X("gateb"))
+        tt(X("x2"), X("P4", 0, 128), X("tm"), ALU.is_lt)
+        for k in range(8):
+            mm(X("P3", 288, 304), X("selg", 128 * k, 128 * k + 128), X("x2", k, 128, 8), k == 0, k == 7)
+        act(X("ncb"), X("P3", 288, 304))
+        for k in range(6):
+            mm(X("P6", 16 * k, 16 + 16 * k), X("idN"), X("ncb"))
+        tt(X("li"), X("P6", 0, 96), X("BT"), ALU.min)
+        if t < NT - 1:
+            act(X("clb"), X("P6", 16, 32), AF.Sign, bias=-300.0)
+        ts(X("li", 32, 48), X("li", 32, 48), 2047, ALU.bitwise_and)
+        cp(part(t, 2)[1], X("li", 0, 48))
+        send(t, 2)
+        cp(X("wrL"), X("li", 48, 96))
+        selL, genL, blkL = X("wrL", 0, 16), X("wrL", 16, 32), X("wrL", 32, 48)
+        ts(X("vnh"), X("li", 32, 48), -2048.0, ALU.add)
+        level(4)
+        act(X("sf"), by(X("SS", 0, 2304), selL))
+        act(X("SS", TAB + t, 2304, 8), X("sf"))
+        tt(X("old"), by(SU, vL), X("jm"), ALU.min)
+        mm(X("P3", 128, 384), X("id1"), X("jm"), True)
+        unwrap(X("P3", 128, 384), "selT", X("vnh"), False)
+        act(X("p2"), X("P3", 128, 384), bias=-BIG)
+        if not t:
+            patchers()
+        mm(X("P7", 256, 512), X("idV"), X("nec"), True)
+        mm(X("P7", 256, 512), idb, x)
+        act(X("t30"), X("P7", 256, 512))
+        for bank, up, down in (("P5", "idR", "idN"), ("P6", "idQ", "idP")):
+            mm(X(bank, 256, 512), X(down), X("sp"), True)
+            if bank == "P5":
+                mmf(X(bank, 256, 512), idf, X("verf"))
+            else:
+                unwrap(X(bank, 256, 512), "selT", X("vnh"), False)
+            for h in range(2):
+                mm(X(bank, 256 + 128 * h, 384 + 128 * h), X("mm", 128 * h, 128 * h + 128), X(up))
+        act(X("mk"), X("P5", 256, 512), bias=-2048.0)
+        tt(X("pr"), X("P6", 256, 512), X("mk"), ALU.max)
+        for c in range(7, -1, -1):
+            tt(by(X("SS", TAB, END), X("ptL", 2 * c, 2 * c + 2)), X("p2", 32 * c, 32 * c + 32), X("old", 32 * c, 32 * c + 32), ALU.max)
+        act(by(X("RR", TAB, 2576), genL), X("t30"), AF.Silu)
+        act(X("sb"), by(X("RR", 0, 2304), selL))
+        if t < NT - 1:
+            select(X("RR", TAB + t, 2304, 8), X("sb"), [[0, 256]], ALU.is_ge, 0.0, 0, 0)
         else:
-            equal_x(T.eqc[:], T.rc[:], "rc", "eqc")
-        act(T.t30[:], T.eqc[:], "eqc", "t30", bias=VOID, scale=-VOID)
-        mm(T.P7[:, 256:512], T.id5[:], T.sq[:], True, False, "id5 sq", "@7 scp")
-        mmf(T.P7, 256, T.idf, T.suc, True, "idf suc", "@7 scp")
-        act(T.SU[:, 2304:2560], T.P7[:, 256:512], "@7 scp", "SUc", bias=512.0 * 140.0)
-        cp(T.repv[:], T.repg[:], "repg", "repv")
-        pairs(T.Ev, "Ev", T.repv, 48, None, T.P5, "@5 sv", "repv key3", True)
-        tt(T.x2v[:], T.P5[:, 0:128], T.tm[:], ALU.is_lt, "@5 sv tm", "x2v")
-        unlane(T.P5[:, 128:144], lambda k: T.x2v[:, k::8], "x2v", "@5 fw")
-        act(first, T.P5[:, 128:144], "@5 fw", "first")
-        tt(may, nc, T.want[:], ALU.mult, "@3 nc want", "may")
-        tt(T.ta[:], cl, T.dl[:], ALU.mult, "cl dl", "ta")
-        tt(gen, may, cl, ALU.subtract, "may cl", "gen")
-        tt(T.vn[:], T.ta[:], T.base[:], ALU.add, "ta base", "vn")
-        tt(T.td[:], flg, T.dif[:], ALU.mult, "gen may cl first dif", "td")
-        cp(T.vnL[:, 0:16], T.vn[:], "vn", "vnL")
-        tt(T.td[:], T.td[:], T.cb[:], ALU.add, "td cb0 cb1 cb2 cb3", "td")
-        act(T.vnr[:], T.IOT[:].indirect(T.vnL[:, 0:16]), "IOT vnL", "vnr")
-        cp(T.wrL[:], T.td[:], "td", "wrL")
-        act(T.sf[:], T.SU[:].indirect(T.wrL[:, 32:48]), "SU SUz SUc wrL", "sf")
-        act(T.SU[:, t:2048:8], T.sf[:], "sf", "SU")
-        act(T.old[:], T.SU[:, 0:2048].indirect(vL), "SU jvL", "old")
-        for a in todo:
-            dword(*a)
-        mm(T.P6[:, 0:256], T.bo0[:], T.eqc[:], False, False, "bo0 eqc", "@6 D")
-        mm(T.P6[:, 256:512], T.bo1[:], T.eqc[:], False, False, "bo1 eqc", "@6 D")
-        mm(T.P6[:, 0:256], T.bofd[:], T.fd[:], False, True, "bofd fd", "@6 D")
-        tt(T.R[:, 0:2304].indirect(T.wrL[:, 0:16]), T.t30[:], x, ALU.add, "wrL t30 Ri0 Ri1 Ri2 Rx", "R Rz")
-        ts(T.di[:, 0:256], T.P6[:, 0:256], float(0x5555), ALU.add, "@6 D", "di0")
-        ts(T.di[:, 256:512], T.P6[:, 256:512], float(0xAAAA), ALU.add, "@6 D", "di1")
-        ts(T.dy[:, 0:256], T.di[:, 0:256], 0xAAAA + 2 ** 20, ALU.bitwise_and, "di0", "dy0")
-        ts(T.dy[:, 256:512], T.di[:, 256:512], 2 * 0xAAAA, ALU.bitwise_and, "di1", "dy1")
-        mm(T.P4[:, 128:384], T.idb[:], T.zer[:, 0:256], True, False, "idb zer", "@4 d2")
-        mmf(T.P4, 128, T.idf, T.vnr, False, "idf vnr", "@4 d2")
-        mmf(T.P4, 128, T.nidf, T.old, True, "nidf old", "@4 d2")
-        act(T.sb[:], T.R[:, 0:2560].indirect(T.wrL[:, 32:48]), "R Rz Rx wrL", "sb")
-        act(T.R[:, t:2048:8], T.sb[:], "sb", "R")
-        if t == 0:
-            act(T.selj[:], T.sel[:], selall + " col4", "selj", scale=T.col[:, 4:5])
-        mm(T.P7[:, 0:256], T.idb[:], T.c2k[:], True, False, "idb c2k", "@7 df")
-        mmf(T.P7, 0, T.nidf, T.verf, False, "nidf verf", "@7 df")
-        mmf(T.P7, 0, T.idf, T.vnr, True, "idf vnr", "@7 df")
+            act(X("RR", TAB + t, 2304, 8), X("sb"))
+        act(by(X("VL"), blkL), X("pr"), AF.Silu)
         if t < NT - 1:
-            mm(T.P3[:, 144:160], T.bo[:], cl, True, True, "bo cl", "@3 aw")
-        if t < NT - 1:
-            tt(T.mm[:], T.dy[:, 0:256], T.dy[:, 256:512], ALU.is_equal, "dy0 dy1", "mm")
-        tt(T.p2[:], T.jm[:], T.P4[:, 128:384], ALU.mult, "jm @4 d2", "p2")
-        tt(T.SU[:, 0:2304].indirect(T.wrL[:, 48:64]), T.p2[:], T.old[:], ALU.add, "wrL p2 old", "SU SUz")
-        if t == NT - 1:
-            ts(T.reci[:], T.R[:, 0:2048], 9.0, ALU.min, "R", "reci0 reci1")
-            dma("y", T.yr[:], T.reci[:], "reci0", "")
-            tt(T.mm[:], T.dy[:, 0:256], T.dy[:, 256:512], ALU.is_equal, "dy0 dy1", "mm")
-        if t < NT - 1:
-            act(T.an[:], T.P3[:, 144:160], "@3 aw", "an ac", bias=244.5 / 16.0, acc=T.ac[:, 0:1])
-            act(T.ay[:, 0:1], T.ac[:, 0:1], "ac", "ay", bias=5.55, scale=0.5)
-            act(T.cd[:, 32:48], T.cd[:, 32:48], "cd2", "cd2", bias=1.0)
-            act(T.tha[:, 0:1], T.ay[:, 0:1], "ay ac", "tha", bias=T.ac[:, 0:1], scale=-2.0)
-            act(T.cfd[:, 0:1], T.cfd[:, 0:1], "cfd", "cfd", bias=1.0 / 4096.0)
-        early_in(t)
-        if t < NT - 1:
-            act(T.cb[:, 32:48], T.cb[:, 32:48], "cb2", "cb2", bias=1.0)
-        tt(T.pr[:], T.mm[:], T.P7[:, 0:256], ALU.mult, "mm @7 df", "pr")
-        late = [lambda: tt(T.VL[:].indirect(T.wrL[:, 16:24]), T.pr[:, 0:128], T.verf[:, 0:128], ALU.add, "wrL pr verf VLz", "VL"),
-                lambda: tt(T.VL[:].indirect(T.wrL[:, 24:32]), T.pr[:, 128:256], T.verf[:, 128:256], ALU.add, "wrL pr verf VLz", "VL")]
+            mm(X("P3", 352, 368), X("bo"), X("clb"), True, True)
+            act(X("an"), X("P3", 352, 368), bias=395.5 / 16, scale=-0.5, acc=X("ac", 0, 1))
+            act(X("ay", 0, 1), X("ac", 0, 1), bias=-5.5, scale=0.5)
+            act(X("tha", 0, 1), X("ay", 0, 1), bias=X("ac", 0, 1), scale=-2.0)
+            act(X("BT", 48, 64), X("BT", 48, 64), bias=1.0)
 
+    urge[:] = [NT + 1, 0.5]
+    for k in range(4):
+        lo, hi = 512 * k, 512 * k + 512
+        if k % 2:
+            ts(X("G", lo, hi), sub(R, lo, hi), XO + 9, ALU.min)
+            ts(X("reci", lo, hi), X("G", lo, hi), -XO, ALU.add)
+        else:
+            act(X("G", lo, hi), sub(R, lo, hi), bias=-1.5 * XO)
+            ts(X("reci", lo, hi), X("G", lo, hi), 0.5 * XO, ALU.add, 9.0, ALU.min)
+        dma("y", T.yr[:, lo:hi], X("reci", lo, hi), 131072)
+    ts(X("ylo"), X("VL", 0, 512), 1.5 * 2 ** 23 - VO, ALU.add, -1.5 * 2 ** 23, ALU.add)
+    dma("y", T.yl[:], X("ylo"), 262144)
     for k in range(16):
-        mm(T.P0[:, k:128:16], T.SU[:, 128 * k:128 * k + 128], T.b8f[:], True, True, "b8f SU", "@0 ys")
-    late[0]()
-    act(T.yso[:, 0:128], T.P0[:, 0:128], "@0 ys", "yso0", bias=32768.0)
-    flags_in(NT - 1)
-    mm(T.P2[:, 0:128], T.yso[:, 0:128], T.idf[:], True, True, "yso0 idf", "@2 yt")
-    late[1]()
-    dma("y", T.yl[:], T.VL[:, 0:512], "VL", "")
-    act(T.vnr[:], T.IOT[:].indirect(vL), "IOT jvL", "vnr", bias=2048.0)
-    dma("s", T.yv[:], T.vnr[0:128:16, :], "vnr", "")
-    take_x(NT - 1)
-    dma("s", T.yx[:], x, "Rx", "")
-    act(T.yso[:, 128:256], T.P2[:, 0:128], "@2 yt", "yso1")
-    dma("s", T.ys[:], T.yso[:, 128:256], "yso1", "")
+        mm(X("P0", k, 128, 16), sub(SU, 128 * k, 128 * k + 128), X("col", 24, 32), True, True)
+    act(X("yso", 0, 128), X("P0", 0, 128), bias=32768.0)
+    mm(X("P2", 0, 128), X("yso", 0, 128), idf, True, True)
+    act(X("yso", 128, 256), X("P2", 0, 128))
+    dma("s", T.ys[:], X("yso", 128, 256), 65536)
+    lst = part(NT - 1, 2)[0]
+    cp(X("vf"), sub(lst, 32, 48))
+    x = X("xx", 256 * (NT % 2), 256 * (NT % 2) + 256)
+    act(x, by(X("land", (NT - 1) * SW, NT * SW), sub(lst, 16, 32)), bias=-XO)
+    dma("s", T.yx[:], x, 65536)
+    unwrap(X("P1", 0, 256), "selT", X("vf"))
+    cp(X("suc"), X("P1", 0, 256))
+    op("y", lambda: g.sync.dma_start(T.yv[:], T.suc[0:128:16, :]), [X("suc")], [], (100.0, 2000.0), "d")
     emit(g, T, ops)
     g.wait_ge(T.sem.sent, nsent[0])

import math
import numpy as np
from concourse.mybir import AluOpType as ALU, ActivationFunctionType as AF

NT = 6
HOP = 3
SW = 512
LW = 48
CYC, GATHER, SCATTER, PE, WAKE, HOPS = 1.04, 1.62, 3.95, 0.52, 150.0, (6000.0, 6000.0, 4700.0)
OVER = ("over",)
VERS, BREPS = False, False
CHUNKS = (0, 64, 128, 192, 224, 256)
FIRST, LATE, SPLIT, REPV, RG, XS = (0, 4, 16), False, (128, 96), (0, 1), 1, 1
GV = -1
SHAKE, SLACK = 150.0, 150.0
PASSES = 1000
ORDER = {}
VOID = float(2 ** 36)
XO, VO = 32.0, 6144.0
BIG = 8192.0
LN3 = math.log(3.0)
TAB = 256
END = TAB + 2048 + 32

F, B, H, I, U = "float32", "bfloat16", "float16", "int32", "uint16"
SCRATCH = {}
for _d, _l in (
    (B, "land:%d msg:%d " % (NT * SW, NT * SW) +
        "EF:2048 IP:1568 G:4096 EQ:4096 Ea:4096 Eb:4096 sel:2048 selj:2048 selT:2048 selD:2048 selg:1024 rw:576 idb:128 "
        "id2:128 id5:128 idV:128 idQ:128 idR:128 id32:128 id1:128 idM:128 idH:128 xw:256 IOB:512 idN:128 idP:128 one:128 bo:128 bo01:256 bo19:128 "
        "kc:128 rE:24 b8:32 xm:64 "
        "pw:8 cw:8 tmpb:784 tmpd:128 reci:2048 jm:256 kw:512 brep:256 x2:128 rc:256 nec:256 ex:256 sg:256 "
        "sgb:256 sq:256 ay:8 tri:256 E1:384 sp:256 mm:256 keyb:16 gateb:16 rg:1536 farb:16 ncb:16 clb:16 xx:512"),
    (F, "SS:%d RR:2576 IOT:2048 repf:256 gate:16 " % END +
        "VL:768 idf:128 t30:256 sb:256 mk:256 ylo:512 seg:128 tm:128 col:32 wex:16 tmpf:128 lane:16 AC:96 BT:96 key:16 verf:256 mn:256 "
        "suc:256 old:256 p2:256 sf:256 pr:256 an:16 ac:8 tha:8 yso:256"),
    (H, "prod:256 urep:256 vf:16 vnh:16 um:512 jx:128 ux:128"),
    (I, "coli:4 edi:512 vei:512 v0i:256 ei:16 bi:16 si:16 lm:32 li:96 di:512 dy:512"),
    (U, "lland:%d lmsg:%d bL:32 verL:256 cL:16 wrL:48 ptL:16 xl:16" % (LW * (NT + 1), LW * NT)),
):
    for _w in _l.split():
        SCRATCH[_w.split(":")[0]] = ("sbuf", [128, int(_w.split(":")[1])], _d)
for _k in range(8):
    SCRATCH["P%d" % _k] = ("psum", [128, 512], F)
NDMA = 30
SEMAPHORES = (["cv", "cs", "cp", "cg", "sent"] + ["arr%d_%d" % (t, k) for t in range(NT) for k in range(3)]
              + ["dm%d" % k for k in range(NDMA)])


def X(name, a=0, b=None, s=1, p=(0, 128)):
    return (name, a, SCRATCH[name][1][1] if b is None else b, s, p, None)


def by(win, off):
    return win[:5] + (off,)


def cols(v):
    return 16 * cols(v[5]) if v[5] else len(range(v[1], v[2], v[3]))


def bits(v):
    if v[3] == 1:
        return (1 << v[2]) - (1 << v[1])
    return sum(1 << c for c in range(v[1], v[2], v[3]))


def part(t, k):
    if k == 2:
        return X("lland", t * LW, t * LW + LW), X("lmsg", t * LW, t * LW + LW)
    a = t * SW + 256 * k
    return X("land", a, a + 256), X("msg", a, a + 256)


def view(T, v):
    if not isinstance(v, tuple):
        return v
    a = T[v[0]][v[4][0]:v[4][1], v[1]:v[2]:v[3]] if v[3] > 1 else T[v[0]][v[4][0]:v[4][1], v[1]:v[2]]
    return a.indirect(view(T, v[5])) if v[5] else a


def mask_of(engines):
    return sum(1 << e for e in engines)


def route(T, topo):
    n = len(T.cores)
    out = []
    for r, c in enumerate(T.cores):
        dsts = [T.cores[(r + HOP) % n]] * (NT - 1) + [T.cores[(r - HOP * (NT - 1)) % n]]
        able = [h for h in topo.cores_of(c) if h not in T.cores and all(topo.may_write(h, d) for d in dsts)]
        able.sort(key=lambda h: topo.die(h) != topo.die(c))
        ea, eb = topo.engines(c, able[0]), topo.engines(c, able[1])
        early, late = (able[0], ea[:len(ea) // 2]), (able[1], eb[len(eb) // 2:])
        out.append((c, dsts, (early, early, late)))
    return out


def relay_program(g, core, T, topo, dsts, hops):
    total = 0
    for t in range(NT):
        rid, pid = topo.addr(dsts[t], core)
        for k, (h, eng) in enumerate(hops):
            if h == core:
                piece = view(T, part(t, k)[0])
                s = T.sem["arr%d_%d" % (t, k)]
                g.wait_ge(s, len(eng))
                g.remote_dma(piece, piece, s, T.sem.sent, pid, rid, topo.mask(core, dsts[t]))
                total += len(topo.engines(core, dsts[t]))
    g.wait_ge(T.sem.sent, total)


def tag(o):
    name, a, b, s = o[3][0][:4]
    if name in ("G", "EQ"):
        k = CHUNKS.index(a // 16 if name == "G" else a % 512 // 2)
    elif name in ("Ea", "Eb", "rg"):
        k = (a >= 2048, a % 256 >= 128, a >= 1024)[("Ea", "Eb", "rg").index(name)]
    elif name in ("SS", "RR"):
        k = a // 128 if a < TAB else "w" if s > 1 else "s"
    elif name in ("msg", "sent"):
        k = a % SW // 128 if name == "msg" else a % 3
    elif name in ("xx", "lmsg", "ptL"):
        k = ""
    elif name in ("bL", "jm", "prod", "ei", "bi", "verL", "BT", "li", "kw"):
        k = a if name != "li" else b
    else:
        k = 2 * a // SCRATCH[name][1][1]
    return "%s%s" % (name, int(k) if k is True or k is False else k)


def inline(ops, m, n):
    return ops[m][0] == ops[n][0] and (ops[m][0] == "p" or ops[m][5][2:] == ops[n][5][2:] == ("over",))


def schedule(ops, full, runs):
    n = len(ops)
    eng = [o[0] for o in ops]
    dur = [o[5][0] for o in ops]
    banks = [sorted({v[0] for v in o[2] + o[3] if v[0][0] == "P"}) for o in ops]
    pre = [[(m, ops[m][5][1] + (0 if inline(ops, m, i) else WAKE)) for m in sorted(d)] for i, d in enumerate(full)]
    post = [[] for _ in range(n)]
    for i in range(n):
        for m, lat in pre[i]:
            post[m].append((i, lat))

    def lay(before, rank, first):
        end = [0.0] * n
        line = {k: ([], []) for k in names}
        for i in rank:
            t, d = first[i], dur[i]
            for m, lat in before[i]:
                if end[m] + lat > t:
                    t = end[m] + lat
            moved = d > 0
            while moved:
                moved = False
                for name, pad in meets[i]:
                    lo, hi = line[name]
                    k = len(hi)
                    while k and hi[k - 1] > t - pad + 1e-6:
                        k -= 1
                    while k < len(lo) and lo[k] - pad < t + d - 1e-6:
                        t, k, moved = hi[k] + pad, k + 1, len(meets[i]) > 1
            end[i] = t + d
            for name in holds[i]:
                lo, hi = line[name]
                k = len(hi)
                while k and hi[k - 1] > t + 1e-6:
                    k -= 1
                lo.insert(k, t)
                hi.insert(k, t + d)
        return end

    def ranked(key, before, walk):
        for i in walk:
            for m, lat in before[i]:
                if key[m] >= key[i]:
                    key[i] = key[m] + 1e-3
        return sorted(walk, key=lambda i: key[i])

    meets = [[(eng[i], 0.0)] + [(b + e, WAKE) for b in banks[i] for e in "vsp" if e != eng[i]] for i in range(n)]
    holds = [[eng[i]] + [b + eng[i] for b in banks[i]] if dur[i] else [] for i in range(n)]
    names = set(eng) | {"P%d%s" % (k, e) for k in range(8) for e in "vsp"}
    group = [tag(o) if 1 <= o[6][0] <= NT and o[0] in "vsg" else o[0] + o[3][0][0] if o[3] else "out" for o in ops]
    kinds = sorted(set(group))
    after, up, down = [o[5][1] for o in ops], list(range(n)), list(range(n - 1, -1, -1))
    seed, best, now = 1, None, None
    key = [o[6][0] * 1e6 + o[6][1] * 1e5 + i for i, o in enumerate(ops)]
    for k in range(PASSES):
        end = lay(pre, ranked(key, pre, up), [0.0] * n)
        total = max(end[i] + after[i] for i in up)
        if now is None or total < now[0] + SLACK:
            now = (total, end)
        if best is None or total < best[0]:
            best = (total, [end[i] - dur[i] for i in up])
        shift = {}
        for _ in range(3 if k > 3 else 0):
            seed = (seed * 1103515245 + 12345) % 2 ** 31
            shift[kinds[seed // 7 % len(kinds)]] = (seed // 1000 % 7 - 3) * SHAKE * (1 + seed // 77 % 3)
        if k % 2:
            key = [now[1][i] - dur[i] + shift.get(group[i], 0.0) for i in up]
        else:
            back = lay(post, ranked([-now[1][i] - shift.get(group[i], 0.0) for i in up], post, down), after)
            key = [-back[i] for i in up]
    order = sorted(range(n), key=lambda i: (best[1][i], i))
    last = {}
    for i in order:
        for b in banks[i]:
            if b in last and eng[last[b]] != eng[i]:
                full[i].add(last[b])
            last[b] = i
    return order


def depend(ops):
    live, bank, seen, full = {}, {}, {}, []
    for n, (e, fn, rd, wr, kind, cost, key) in enumerate(ops):
        d = set()
        if e == "p":
            if cost[2]:
                d.update(sum(bank.setdefault(wr[0][0], [])[-1:], seen.pop(wr[0][0], [])))
                bank[wr[0][0]].append([n])
            else:
                d.add(bank[wr[0][0]][-1][0])
                bank[wr[0][0]][-1].append(n)
        for v, m in [(v, bits(v)) for v in rd]:
            d.update(r[1] for r in live.get(v[0], []) if r[2] and r[0] & m)
            if v[0] in bank:
                d.update(bank[v[0]][-1])
                seen.setdefault(v[0], []).append(n)
        for v, m in [(v, bits(v)) for v in wr]:
            d.update(r[1] for r in live.get(v[0], []) if r[0] & m)
            live[v[0]] = [(r[0] & ~m, r[1], r[2]) for r in live.get(v[0], []) if r[0] & ~m] + [(m, n, True)]
        for v in rd:
            live.setdefault(v[0], []).append((bits(v), n, False))
        d.discard(n)
        full.append(d)
    return full, bank


def emit(g, T, ops):
    q = {"v": g.vector, "s": g.scalar, "p": g.tensor, "g": g, "y": g.sync}
    sem = {"v": T.sem.cv, "s": T.sem.cs, "p": T.sem.cp, "g": T.sem.cg}
    if len(ops) not in ORDER:
        full, runs = depend(ops)
        ORDER[len(ops)] = (full, runs, schedule(ops, full, runs))
    full, runs, order = ORDER[len(ops)]
    pos = {n: k for k, n in enumerate(order)}
    stops = {max(r, key=pos.get) for b in runs for r in runs[b]}
    deps, need = {}, set()
    for n in order:
        top = {}
        for m in full[n]:
            e2, k2 = ops[m][0], ops[m][4]
            if k2 == "c":
                if not inline(ops, m, n) and pos[m] > pos.get(top.get(e2), -1):
                    top[e2] = m
            elif k2 != "r":
                top[("x", m)] = m
        deps[n] = sorted(top.values())
        need.update(top.values())
    cnt = {k: 0 for k in sem}
    tok, seen, ndma, ends = {}, {k: {} for k in q}, 0, []
    for n in order:
        e, fn, rd, wr, kind, cost, key = ops[n]
        for m in deps[n]:
            name, s, val = tok[m]
            if seen[e].get(name, 0) < val:
                q[e].wait_ge(s, val)
                seen[e][name] = val
        if kind == "c":
            ins = fn(n in stops) if e == "p" else fn()
            if n in need:
                cnt[e] += 1
                ins.then_inc(sem[e], 1)
                tok[n] = (e, sem[e], cnt[e])
        elif kind == "d":
            s = T.sem["dm%d" % ndma]
            fn().then_inc(s, 16)
            tok[n] = ("dm%d" % ndma, s, 16)
            ends.append((e, tok[n]))
            ndma += 1
        elif kind == "r":
            fn()
        else:
            tok[n] = kind
    for e, (name, s, val) in ends:
        if max(seen[k].get(name, 0) for k in q) < val:
            q[e].wait_ge(s, val)


def rank_program(g, core, T, topo):
    rt = route(T, topo)
    rank = T.rank_of(core)
    if rank is None:
        for c, dsts, hops in rt:
            if core in [h for h, eng in hops]:
                relay_program(g, core, T, topo, dsts, hops)
        return
    me, dsts, hops = rt[rank]
    ops = []
    urge = [0, 0]

    def level(k):
        urge[1] = k

    V, S, P = g.vector, g.scalar, g.tensor

    def op(e, fn, rd, wr, cost, kind="c"):
        rd = [v for v in rd if isinstance(v, tuple)]
        rd += [v[5] for v in rd + wr if v[5]]
        ops.append((e, fn, rd, list(wr), kind, cost, tuple(urge)))

    def w(v):
        return view(T, v)

    def two(*a):
        return all("16" in SCRATCH[v[0]][2] for v in a)

    def took(out, a, per):
        if out[5]:
            return (50.0 + SCATTER * cols(out), 0.0)
        if a[5]:
            return (60.0 + GATHER * cols(out), 0.0)
        return (CYC * max(64.0, (per or (0.5 if two(out, a) else 1.0)) * cols(a)), 0.0)

    def tt(out, a, b, o, over=()):
        op("v", lambda: V.tensor_tensor(w(out), w(a), w(b), o), [a, b], [out],
           took(out, a, 1.0 if "P" in a[0][0] + b[0][0] else 2.0) + over)

    def ts(out, a, s1, o1, s2=None, o2=None):
        if o2 is None:
            op("v", lambda: V.tensor_scalar(w(out), w(a), w(s1), None, o1), [a, s1], [out], took(out, a, 0))
        else:
            op("v", lambda: V.tensor_scalar(w(out), w(a), w(s1), w(s2), o1, o2), [a, s1, s2], [out], took(out, a, 0))

    def cp(out, a):
        op("v", lambda: V.tensor_copy(w(out), w(a)), [a], [out], took(out, a, 0))

    def ms(out, val):
        op("v", lambda: V.memset(w(out), val), [], [out], took(out, out, 0))

    def scan(out, a, b):
        op("v", lambda: V.tensor_tensor_scan(w(out), w(a), w(b), 0.0, ALU.add, ALU.min), [a, b], [out], took(out, a, 1.0))

    def act(out, a, func=AF.Identity, bias=0.0, scale=1.0, acc=None):
        if out[5]:
            op("s", lambda: S.activation(w(out), w(a), func), [a], [out], took(out, a, 1.0))
        else:
            op("s", lambda: S.activation(w(out), w(a), func, bias=w(bias), scale=w(scale), accum_out=w(acc)), [a, bias, scale],
               [out] + ([acc] if acc else []), took(out, a, 1.0))

    def mm(out, l, r, st=False, sp=False):
        c = PE * max(min(64, cols(l)), cols(r)) * (1 if two(l) else 4)
        op("p", lambda last: P.matmul(w(out), w(l), w(r), st, last), [l, r], [out], (c, 0.0, st))

    def sub(v, a, b, s=1):
        return (v[0], v[1] + a * v[3], min(v[2], v[1] + b * v[3]), v[3] * s) + v[4:]

    def mmf(out, l, r, st=False, sp=False):
        n = cols(r) // 64
        for k in range(n):
            mm(sub(out, 64 * k, 64 * k + 64), l, sub(r, 64 * k, 64 * k + 64), st and k == 0, sp and k == n - 1)

    def iota(out, pat, base, cm=0):
        c = (130.0 + 2.0 * CYC * cols(out), 0.0)
        if SCRATCH[out[0]][2] == I:
            op("g", lambda: g.iota(w(out), pat, base, cm), [], [out], c)
        else:
            op("g", lambda: g.iota(w(out), pat, base, cm, allow_small_or_imprecise_dtypes=True), [], [out], c)

    def fill(out, val):
        iota(out, [[0, cols(out)]], val)

    def select(out, a, pat, o, val, base, cm):
        op("g", lambda: g.affine_select(w(out), w(a), pat, o, val, base, cm), [a], [out], (170.0 + 2.0 * CYC * cols(out), 0.0))

    def dma(e, out, a, nbytes):
        qq = g.sync if e == "y" else g.scalar
        op(e, lambda: qq.dma_start(w(out), w(a)), [a], [out] if isinstance(out, tuple) else [], (100.0, 2000.0 + nbytes / 200.0), "d")

    nsent = [0]

    def send(t, k):
        h, eng = hops[k]
        rid, pid = topo.addr(h, core)
        far, near = part(t, k)
        nsent[0] += len(eng)
        op("g", lambda: g.remote_dma(w(far), w(near), T.sem["arr%d_%d" % (t, k)], T.sem.sent, pid, rid, mask_of(eng)),
           [near], [("sent", 3 * t + k, 3 * t + k + 1, 1, None, None)], (500.0, 0.0), "r")
        h = [hp for c, ds, hp in rt if ds[t] == core][0][k][0]
        nm = "arr%d_%d" % (t, k)
        op("x", None, [("sent", 3 * t + k, 3 * t + k + 1, 1, None, None)], [far], (0.0, HOPS[k]),
           (nm, T.sem[nm], len(topo.engines(h, core))))

    def wrap(out, lhs, src, st=True):
        for p in range(16):
            mm(out, X(lhs, 128 * p, 128 * p + 128), sub(src, p, cols(src), 16), st and p == 0, p == 15)

    def unwrap(out, lhs, src, st=True):
        for p in range(16):
            mm(sub(out, p, cols(out), 16), X(lhs, 128 * p, 128 * p + 128), src, st and p == 0, p == 15)

    def pairs(E, rep, key, gate, c, lo, hi, st=False, sp=False):
        o = X(E, 256 * c + lo, 256 * c + hi)
        if gate:
            ts(o, X(rep, lo, hi), X(key, c, c + 1), ALU.is_equal, X(gate, c, c + 1), ALU.mult)
        else:
            ts(o, X(rep, lo, hi), X(key, c, c + 1), ALU.is_equal)
        if key == "key":
            count(E, "rw", c, lo, hi, st)

    def count(E, rw, c, lo, hi, st=False):
        if lo < 128:
            lo = lo // 64 * 64
            mm(X("P4", 0, 64, 1, (lo, 128)), X(E, 256 * c + lo, 256 * c + 128), X(rw, 64 * c, 64 * c + 64), st)
        if hi > 128:
            k = (c - 8 if c >= 8 else 8) if rw == "rw" else c + 8
            mm(X("P4", 64, 128), X(E, 256 * c + 128, 256 * c + 256), X(rw, 64 * k, 64 * k + 64))

    def col(k):
        return X("col", k, k + 1)

    x, xP = X("xx", 0, 256), X("P0", 0, 512, 2)
    R, SU = X("RR", TAB, TAB + 2048), X("SS", TAB, TAB + 2048)
    pm, pg, b8 = col(1), col(2), X("xm", 0, 8)
    idb, idf = X("idb"), X("idf")
    dma("y", X("xx", 256, 512), T.x0[:], 65536)
    dma("y", X("edi"), T.edge0[:], 262144)
    ms(X("v0i"), 0)
    op("s", lambda: S.dma_start(T.v0i[0:128:16, :], T.v0[:]), [], [X("v0i")], (100.0, 2000.0), "d")
    dma("s", X("reci", 0, 1024), T.rec0[:, 0:1024], 262144)
    dma("y", X("reci", 1024, 2048), T.rec0[:, 1024:2048], 262144)
    dma("y", X("vei"), T.ver0[:], 262144)
    for k in range(4):
        dma("y", X("EF", 128 * k, 128 * k + 128), T.eff[:], 32768)
    for n in (512, 1024):
        dma("y", X("EF", n, 2 * n), X("EF", 0, n), 256 * n)
    iota(X("coli", 0, 1), [[0, 1]], 0, 1)
    iota(X("xm"), [[0, 8], [1, 8]], 0)
    iota(X("tmpb", 0, 784), [[0, 49], [1, 16]], 0)
    iota(X("tmpf"), [[1, 128]], 0, -1)
    fill(X("one", 0, 128), 1)
    iota(X("wex", 0, 8), [[16, 8]], 0)
    iota(X("tmpd"), [[1, 8], [0, 16]], 0)
    iota(X("kc", 0, 128), [[0, 8], [2048, 16]], 0)
    iota(X("lane"), [[16, 16]], 0)
    fill(X("RR", 2304, 2320), 5)
    fill(X("RR", 2320, 2576), 0)
    fill(X("seg"), 0)
    fill(X("seg", 0, 128, 16), 2 ** 22)
    iota(X("tm"), [[0, 2], [1, 8], [0, 8]], 0)
    fill(X("SS", 2304, END), 0)
    fill(X("VL", 512, 768), 0)
    fill(X("selg"), 0)
    ms(X("sel"), 0.0)
    ts(X("coli", 1, 2), X("coli", 0, 1), 15, ALU.bitwise_and)
    ts(X("coli", 2, 3), X("coli", 0, 1), 4, ALU.arith_shift_right)
    ts(X("coli", 3, 4), X("coli", 0, 1), 7, ALU.bitwise_and)
    cp(X("col", 0, 4), X("coli"))
    ts(X("xm"), X("xm"), pg, ALU.is_equal)
    ts(col(4), pm, 2.0, ALU.mult, 1.0, ALU.add)
    for p in range(16):
        cp(X("sel", 129 * p, 128 * p + 128, 16), b8)
    ts(col(5), pm, -LN3, ALU.mult, 56 * LN3, ALU.add)
    ts(col(6), col(0), -LN3, ALU.mult, 56 * LN3 + math.log(3.5), ALU.add)
    act(X("pw", 0, 1), col(3), AF.Exp, scale=math.log(4.0))
    ops[-1] = ops[-1][:5] + ((1400.0, 0.0), (0, 0))
    act(X("ex"), X("xx", 256, 512), scale=col(4))
    cp(X("prod"), X("v0i"))
    act(X("wex", 8, 16), X("wex", 0, 8), AF.Exp, bias=col(5), scale=-LN3)
    act(col(7), col(6), AF.Exp)
    act(x, X("xx", 256, 512), AF.Silu, bias=XO)
    ops[-1] = ops[-1][:2] + (ops[-1][2] + [X("pw", 0, 1), X("wex", 8, 16), col(7)],) + ops[-1][3:5] + ((1800.0, 0.0), (0, 0))
    ts(sub(SU, 0, 512), X("edi"), -2048.0, ALU.add)
    ts(X("IP", 0, 784), X("tmpb", 0, 784), pm, ALU.is_equal)
    act(sub(SU, 512, 1024), sub(SU, 0, 512))
    ts(idb, X("tmpf"), 0.0, ALU.is_equal)
    ts(sub(SU, 1024, 1536), X("edi"), -2048.0, ALU.add)
    act(sub(SU, 1536, 2048), sub(SU, 0, 512))
    for k in range(2):
        ts(X("G", 1024 * k, 1024 * k + 1024), X("reci", 1024 * k, 1024 * k + 1024), 8.0, ALU.is_ge, VOID, ALU.mult)
    for k in range(4):
        bk = X("P%d" % (4 + k))
        mm(bk, idb, X("reci", 512 * k, 512 * k + 512), True)
        mm(bk, idb, X("G", 512 * k, 512 * k + 512), False, True)
        if k < 3:
            act(sub(R, 512 * k, 512 * k + 512), bk, bias=XO)
        else:
            ts(sub(R, 512 * k, 512 * k + 512), bk, XO, ALU.add)
    ts(X("VL", 0, 512), X("vei"), VO, ALU.add)
    ts(idf, X("tmpf"), 0.0, ALU.is_equal)
    for k, val in enumerate((-2.0 ** 15 / VOID, -2.0 ** 20, -2.0 ** 20 / VOID)):
        ts(X("b8", 8 * k, 8 * k + 8), b8, val, ALU.mult)
    b8v, b8x, b8xv = X("b8", 0, 8), X("b8", 8, 16), X("b8", 16, 24)
    ts(col(8), pm, 8.0, ALU.is_ge, 2.0, ALU.mult)
    ts(col(9), pm, 8.0, ALU.is_lt, X("pw", 0, 1), ALU.mult)
    ts(col(10), col(8), X("pw", 0, 1), ALU.mult)
    ts(X("rE", 0, 8), b8, -32768.0, ALU.mult)
    ts(X("rE", 8, 16), b8, col(9), ALU.mult, -1.0, ALU.mult)
    ts(X("rE", 16, 24), b8, col(10), ALU.mult, -1.0, ALU.mult)
    act(col(12), X("idf", 0, 1), scale=2.0 ** 24)
    act(col(13), X("idf", 1, 2), bias=col(12), scale=-17 * 2.0 ** 15)
    act(col(14), X("idf", 2, 3), bias=col(13), scale=2.0 ** 11)
    act(col(15), X("idf", 3, 4), bias=col(14), scale=-15 * BIG)
    act(X("cw"), X("one", 0, 8), scale=col(15))
    ts(X("rw", 512, 576), X("xm"), float(2 ** 95), ALU.mult)
    for k in range(8):
        act(X("rw", 64 * k, 64 * k + 64), X("xm"), scale=X("wex", 8 + k, 9 + k))
    for k in range(8):
        act(X("selg", 144 * k, 144 * k + 16), X("IP", 0, 16))
    ts(X("xw", 192, 256), X("tm", 0, 64), pg, ALU.is_equal)
    ts(X("tm"), X("tm"), pg, ALU.is_equal, col(7), ALU.mult)
    ts(X("lane"), X("lane"), pm, ALU.add)
    ms(X("tha"), 11.5)
    ts(X("bo"), X("tmpd"), pg, ALU.is_equal)
    ts(X("tri"), X("tmpb", 0, 256), pm, ALU.is_le, 4096.0, ALU.mult)
    ts(col(11), pm, 2048.0, ALU.add)
    ts(col(16), pm, 2064.0, ALU.add)
    for k in range(4):
        act(X("selj", 512 * k, 512 * k + 512), X("sel", 512 * k, 512 * k + 512), scale=col(4))
    dma("y", X("IP", 784, 1568), X("IP", 0, 784), 200000)
    iota(X("IOB"), [[1, 512]], -256)
    for p in range(16):
        ts(X("selT", 128 * p, 128 * p + 128), X("bo"), X("IP", p, p + 1), ALU.mult)
    select(X("selD"), X("selT"), [[0, 16], [-1, 128]], ALU.not_equal, -1.0, 0, 1)
    act(X("xw", 0, 64), X("xm"), scale=col(4))
    act(X("xw", 64, 128), X("xw", 0, 64), scale=-2.0)
    fill(X("xw", 128, 192), -(256 * int(XO) + 512) // 128)
    iota(X("IOT"), [[1, 2048]], 0)
    iota(X("an"), [[1, 16]], 0)
    cp(X("xl"), X("an"))
    for nm, val in (("idM", -BIG / 2), ("idH", BIG / 2), ("id1", -1.0), ("id2", -2.0), ("id5", -512.0), ("idV", VOID), ("idQ", 2 * BIG), ("idR", -2 * BIG), ("id32", 32.0), ("idN", -BIG), ("idP", BIG)):
        act(X(nm), idb, scale=val)
    act(X("col", 24, 32), b8)
    ts(X("bo01", 0, 128), X("bo"), col(9), ALU.mult, -1.0, ALU.mult)
    ts(X("bo01", 128, 256), X("bo"), col(10), ALU.mult, -1.0, ALU.mult)
    act(X("bo19"), X("bo"), scale=2.0 ** 19)
    for k, (sc, bi) in enumerate(((0, 1.5 * BIG - 256 * XO), (1, 1.5 * BIG), (0, 1.5 * BIG - TAB), (1, 1.5 * BIG),
                                  (0, 2.5 * BIG), (0, 2 * BIG + 256))):
        act(X("AC", 16 * k, 16 * k + 16), X("lane"), bias=float(bi), scale=float(sc))
    for k, sc, bi in ((1, 1, 256), (3, 8, TAB), (4, 1, 2064), (5, 1, 512)):
        act(X("BT", 16 * k, 16 * k + 16), X("lane"), bias=float(bi), scale=float(sc))

    bL, wL = X("bL", 0, 16), X("bL", 16, 32)
    for t in range(NT):
        o = t * SW
        lst = part(t - 1, 2)[0] if t else X("lland", NT * LW, NT * LW + LW)
        jL, xiL, vL = sub(lst, 0, 16), sub(lst, 16, 32), sub(lst, 32, 48)
        if t == 0:
            wrap(X("P3", 16, 32), "sel", X("prod"))
            wrap(X("P3", 0, 16), "sel", X("ex"))
            cp(jL, X("P3", 0, 16))
            cp(vL, X("P3", 16, 32))
            cp(X("ei"), X("P3", 16, 32))
            ts(X("bi"), X("ei"), 511, ALU.bitwise_and)
            cp(X("cL"), X("bi"))
        urge[0] = t + 1
        level(0)
        x = X("xx", 256 * (t % 2), 256 * (t % 2) + 256)
        for c0, c1 in zip(FIRST, FIRST[1:]):
            u, v = 16 * c0, 16 * c1
            act(X("jm", u, v), by(X("IP", 0, 1568 if t else 784), sub(jL, c0, c1)), bias=BIG, scale=-2 * BIG)
            tt(X("prod", u, v), by(SU, sub(vL, c0, c1)) if t else by(sub(SU, 0, 512), X("cL", c0, c1)), X("jm", u, v), ALU.max)
            if t and c1 == 16:
                (act if XS else cp)(x, by(X("land", o - SW, o), xiL))
            ew = X("P3" if c0 == 0 else "P5", c0, c1)
            wrap(ew, "sel", X("prod", u, v))
            cp(X("ei", c0, c1), ew)
            ts(X("bi", c0, c1), X("ei", c0, c1), 511, ALU.bitwise_and)
            cp(sub(bL, c0, c1), X("bi", c0, c1))
            ts(X("verL", u, v), by(X("VL", 0, 512), sub(bL, c0, c1)), -VO, ALU.add)
            ts(sub(wL, c0, c1), ew, 2048.0 - 15 * BIG, ALU.add, 2048.0, ALU.min)
        select(X("RR", 0, TAB), x, [[0, 256]], ALU.is_ge, 0.0, 0, 0)
        mm(xP, idb, x, True)
        mm(X("P0", 1, 512, 2), idb, x)
        for u, v in zip(CHUNKS, CHUNKS[1:]):
            (cp if u == GV else act)(X("G", 16 * u, 16 * v), by(R, X("verL", u, v)))
            if u == 0:
                act(X("kw", 256, 512), by(X("RR", TAB, 2320), wL))
        cp(X("verf"), X("verL"))
        ts(X("keyb"), X("bi"), -256.0, ALU.add)
        tt(X("kw", 0, 256), X("kw", 256, 512), xP, ALU.is_equal)
        level(1)
        cp(X("brep"), by(X("IOB"), bL))
        for c in range(16 * RG):
            pairs("Ea", "brep", "keyb", None, c, 128 if c >= 8 else 16 * c if t else c // 4 * 64, 256)

        def patchers():
            cp(X("vf"), vL)
            mm(X("P4", 128, 384), idb, X("tri"), True)
            unwrap(X("P4", 128, 384), "selD", X("vf"), False)
            unwrap(X("P4", 384, 512), "selT", X("vf", 1, 16, 2), False)
            for p in range(16):
                mm(X("P4", 384 + p, 512, 16), X("id1"), X("vf", 0, 16, 2))
            ts(X("E1"), X("P4", 128, 512), 0.0, ALU.is_equal, 4096.0, ALU.mult)
            mm(X("P4", 0, 16), idb, X("vf"), True)
            wrap(X("P4", 0, 16), "sel", X("E1", 0, 256), False)
            wrap(X("P4", 1, 16, 2), "sel", X("E1", 256, 384), False)
            for k in range(2):
                ts(X("ptL", k, 16, 2), X("P4", k, 16, 2), col(11 + 5 * k), ALU.min)

        if t:
            patchers()
        mmf(X("P6", 0, 64), idf, X("AC", 0, 64), True)
        mm(X("P6", 64, 96), idf, X("AC", 64, 96))
        mm(X("P6", 32, 48), idf, X("BT", 48, 64))
        mm(X("P6", 80, 96), idb, X("keyb"))
        efn, px = X("EF", t, 2048, 8), X("P7", 256, 512)
        mm(px, idb, x, True)
        mm(px, idb, efn, False, True)
        act(X("sgb"), px, AF.Sign, bias=-3.5 - XO)
        mm(px, idb, x, True)
        mm(px, idb, efn)
        mm(px, X("id2"), X("sgb"), False, True)
        act(X("msg", o, o + 256), px, bias=-2.0)
        send(t, 0)
        wrap(X("P6", 0, 16), "selj", X("msg", o, o + 256), False)
        for h in range(2):
            a = 128 * h
            bk = "P%d" % (1 + h)
            level(0)
            mm(X(bk, 0, 128), X("verf", a, a + 128), idf, True)
            pw = X(bk, 128, 136)
            mm(pw, X("one", 0, 128), X("cw"))
            mm(pw, X("prod", a, a + 128), b8)
            mm(pw, X("kw", a, a + 128), b8x)
            mm(pw, X("kw", 256 + a, 384 + a), b8xv)
            if SPLIT[h] == 128:
                mm(X(bk, 0, 128), idb, X("kc", 0, 128))
            for u, v in [z for z in zip(CHUNKS, CHUNKS[1:]) if a <= z[0] < a + 128]:
                for k in range(8):
                    tt(X("EQ", 512 * k + 2 * u, 512 * k + 2 * v), X("G", 16 * u + k, 16 * v, 8), X("P0", 2 * u, 2 * v), ALU.is_equal)
            for u, v in ((0, SPLIT[h]), (SPLIT[h], 128))[:1 + (SPLIT[h] < 128)]:
                for k in range(16):
                    mm(X(bk, k, 128, 16, (u, v)), X("G", 16 * (a + u) + k, 16 * (a + v), 16), b8v)
                for k in range(16):
                    at = 512 * (k // 2) + 2 * a + k % 2
                    mm(X(bk, k // 2 + 8 * (k % 2), 128, 16, (u, v)), X("EQ", at + 2 * u, at + 2 * v - k % 2, 2), X("rE", 0, 8))
            if SPLIT[h] < 128:
                mm(X(bk, 0, 128), idb, X("kc", 0, 128))
            e = 8 * h
            scan(X("mn", a, a + 128), X("seg"), X(bk, 0, 128))
            si = X("si", e, e + 8)
            tt(si, X("mn", a + 15, a + 128, 16), pw, ALU.min)
            ts(X("lm", 2 * e, 2 * e + 8), si, 2047, ALU.bitwise_and)
            ts(X("lm", 2 * e + 8, 2 * e + 16), si, 15, ALU.arith_shift_right)
            tt(X("um", 2 * a, 2 * a + 256), by(X("lm", 2 * e, 2 * e + 16), X("xl")), X("IP", 0, 256), ALU.mult)
            cw, mw = X("P3", 16 + 2 * e, 24 + 2 * e), X("P3", 24 + 2 * e, 32 + 2 * e)
            mm(cw, X("um", 2 * a, 2 * a + 128), b8, True)
            mm(mw, X("um", 2 * a + 128, 2 * a + 256), b8)
            cL = X("cL", e, e + 8)
            cp(cL, cw)
            ts(X("gate", e, e + 8), mw, -15.0, ALU.is_ge)
            cp(X("key", e, e + 8), cw)
            act(X("farb", e, e + 8), mw, AF.Sign, bias=X("tha", 0, 1))
            if REPV[h]:
                cp(X("ux"), by(X("lm", 2 * e, 2 * e + 16), X("xl", 0, 8)))
                mm(X("P5", 256, 384), X("ux"), idb, True)
                cp(X("urep", a, a + 128), X("P5", 256, 384))
            else:
                act(X("repf", a, a + 128), by(X("IOT"), cL))
                cp(X("urep", a, a + 128), X("repf", a, a + 128))
            level(1)
            if not RG:
                for c in range(8 * h, 8 * h + 8):
                    lo = 128 if h else 16 * c if t else c // 4 * 64
                    pairs("Ea", "brep", "keyb", "gate", c, lo, 256)
                    count("Ea", "rw", c, lo, 256, c == 0)
                for c in range(8 + 8 * h):
                    pairs("Eb", "urep", "key", "gate", c, 128 if h else c // 4 * 64, 128 + 128 * h)
            elif h == 0:
                for c in range(8):
                    pairs("Eb", "urep", "key", "gate", c, c // 4 * 64, 128, c == 0)
                for c in range(8):
                    act(X("rg", 64 * c, 64 * c + 64), X("rw", 64 * c, 64 * c + 64), scale=X("gate", c, c + 1))
                    act(X("rg", 512 + 64 * c, 576 + 64 * c), X("rw", 512, 576), scale=X("gate", c, c + 1))
                    count("Ea", "rg", c, 16 * c, 256)
            else:
                for c in range(8, 16):
                    act(X("rg", 512 + 64 * c, 576 + 64 * c), X("rw", 64 * c - 512, 64 * c - 448), scale=X("gate", c, c + 1))
                    count("Ea", "rg", c, 128, 256)
                for c in range(16):
                    pairs("Eb", "urep", "key", "gate", c, 128, 256)
            xh, exh, px = sub(x, a, a + 128), X("ex", a, a + 128), X("P7", 256 + a, 384 + a)
            act(exh, by(X("EF"), cL))
            mm(px, idb, xh, True)
            mm(px, idb, exh, False, True)
            act(X("sg", a, a + 128), px, AF.Sign, bias=-3.5 - XO)
            for k, z in enumerate((xh, X("one"), exh, X("sg", a, a + 128))):
                mm(X("P7", 0, 64), z, X("xw", 64 * (0, 2, 0, 1)[k], 64 * (1, 3, 1, 2)[k]), k == 0)
            tt(X("jx", 64 * h, 64 * h + 64), X("P7", 0, 64), X("xw", 192, 256), ALU.mult)
            if h:
                for k in range(8):
                    mm(X("P7", 64, 80), X("selg", 128 * k, 128 * k + 128), X("jx", k, 128, 8), k == 0)
                act(X("BT", 0, 16), X("P7", 64, 80), bias=784.0)
            mm(px, idb, xh, True)
            mm(px, idb, exh)
            mm(px, X("id2"), X("sg", a, a + 128), False, True)
            act(X("msg", o + 256 + a, o + 384 + a), px, bias=-2.0)
            level(2)
            act(X("rc", a, a + 128), by(R, cL))
            tt(X("nec", a, a + 128), X("rc", a, a + 128), sub(xP, a, a + 128), ALU.not_equal)
            act(X("suc", a, a + 128), by(SU, cL))
            act(X("sq", a, a + 128), X("suc", a, a + 128), bias=139.501, scale=1.0 / 512.0)
            px = X("P5", a, a + 128)
            mm(px, X("id5"), X("sq", a, a + 128), True)
            mmf(px, idf, X("suc", a, a + 128), False, True)
            act(X("SS", a, a + 128), px, bias=512.0 * 140.0)
        level(3)
        mm(X("P0", 0, 256), X("id32"), X("IP", t, t + 256), True)
        unwrap(X("P0", 0, 256), "selT", X("farb"), False)
        act(X("sp"), X("P0", 0, 256), AF.Sign, bias=-32.0)
        for h in range(2):
            a, bk = 128 * h, "P%d" % (1 + h)
            for k in range(16):
                at = 512 * (k // 2) + 2 * a + k % 2
                mm(X(bk, 128 + k // 2 + 8 * (k % 2), 384, 16), X("EQ", at, at + 256 - k % 2, 2), X("rE", 8, 24), k == 0)
            mm(X(bk, 128, 384), X("nec", a, a + 128), X("bo01"))
            mm(X(bk, 128, 256), X("sp", a, a + 128), X("bo19"), False, True)
            d0, d1 = 256 * h, 256 * h + 128
            ts(X("di", d0, d1), X(bk, 128, 256), float(0xAAAA + 2 ** 23), ALU.add)
            ts(X("di", d1, d1 + 128), X(bk, 256, 384), float(2 * 0xAAAA), ALU.add)
            ts(X("dy", d0, d1), X("di", d0, d1), 0xAAAA + 2 ** 20, ALU.bitwise_and)
            ts(X("dy", d1, d1 + 128), X("di", d1, d1 + 128), 2 * 0xAAAA, ALU.bitwise_and)
            tt(X("mm", a, a + 128), X("dy", d0, d1), X("dy", d1, d1 + 128), ALU.is_equal)
        level(1)
        send(t, 1)
        act(X("BT", 32, 48), X("key"), bias=2048.0)
        mm(X("P6", 64, 80), idf, X("key"))
        for k in range(5):
            mm(X("P6", 16 * k, 16 + 16 * k), X("idM" if k < 4 else "idH"), X("farb"))
        act(X("gateb"), X("gate"))
        for k in (4, 5):
            mm(X("P6", 16 * k, 16 + 16 * k), X("idN"), X("gateb"))
        tt(X("x2"), X("P4", 0, 128), X("tm"), ALU.is_lt)
        for k in range(8):
            mm(X("P3", 288, 304), X("selg", 128 * k, 128 * k + 128), X("x2", k, 128, 8), k == 0, k == 7)
        act(X("ncb"), X("P3", 288, 304))
        for k in range(6):
            mm(X("P6", 16 * k, 16 + 16 * k), X("idN"), X("ncb"))
        tt(X("li"), X("P6", 0, 96), X("BT"), ALU.min)
        if t < NT - 1:
            act(X("clb"), X("P6", 16, 32), AF.Sign, bias=-300.0)
        ts(X("li", 32, 48), X("li", 32, 48), 2047, ALU.bitwise_and)
        cp(part(t, 2)[1], X("li", 0, 48))
        send(t, 2)
        cp(X("wrL"), X("li", 48, 96))
        selL, genL, blkL = X("wrL", 0, 16), X("wrL", 16, 32), X("wrL", 32, 48)
        ts(X("vnh"), X("li", 32, 48), -2048.0, ALU.add)
        level(4)
        act(X("sf"), by(X("SS", 0, 2304), selL))
        act(X("SS", TAB + t, 2304, 8), X("sf"))
        tt(X("old"), by(SU, vL), X("jm"), ALU.min)
        mm(X("P3", 128, 384), X("id1"), X("jm"), True)
        unwrap(X("P3", 128, 384), "selT", X("vnh"), False)
        act(X("p2"), X("P3", 128, 384), bias=-BIG)
        if not t:
            patchers()
        mm(X("P7", 256, 512), X("idV"), X("nec"), True)
        mm(X("P7", 256, 512), idb, x)
        act(X("t30"), X("P7", 256, 512))
        for bank, up, down in (("P5", "idR", "idN"), ("P6", "idQ", "idP")):
            mm(X(bank, 256, 512), X(down), X("sp"), True)
            if bank == "P5":
                mmf(X(bank, 256, 512), idf, X("verf"))
            else:
                unwrap(X(bank, 256, 512), "selT", X("vnh"), False)
            for h in range(2):
                mm(X(bank, 256 + 128 * h, 384 + 128 * h), X("mm", 128 * h, 128 * h + 128), X(up))
        act(X("mk"), X("P5", 256, 512), bias=-2048.0)
        tt(X("pr"), X("P6", 256, 512), X("mk"), ALU.max)
        for c in range(7, -1, -1):
            tt(by(X("SS", TAB, END), X("ptL", 2 * c, 2 * c + 2)), X("p2", 32 * c, 32 * c + 32), X("old", 32 * c, 32 * c + 32), ALU.max)
        act(by(X("RR", TAB, 2576), genL), X("t30"), AF.Silu)
        act(X("sb"), by(X("RR", 0, 2304), selL))
        if t < NT - 1:
            select(X("RR", TAB + t, 2304, 8), X("sb"), [[0, 256]], ALU.is_ge, 0.0, 0, 0)
        else:
            act(X("RR", TAB + t, 2304, 8), X("sb"))
        act(by(X("VL"), blkL), X("pr"), AF.Silu)
        if t < NT - 1:
            mm(X("P3", 352, 368), X("bo"), X("clb"), True, True)
            act(X("an"), X("P3", 352, 368), bias=395.5 / 16, scale=-0.5, acc=X("ac", 0, 1))
            act(X("ay", 0, 1), X("ac", 0, 1), bias=-5.5, scale=0.5)
            act(X("tha", 0, 1), X("ay", 0, 1), bias=X("ac", 0, 1), scale=-2.0)
            act(X("BT", 48, 64), X("BT", 48, 64), bias=1.0)

    urge[:] = [NT + 1, 0.5]
    for k in range(4):
        lo, hi = 512 * k, 512 * k + 512
        if k % 2:
            ts(X("G", lo, hi), sub(R, lo, hi), XO + 9, ALU.min)
            ts(X("reci", lo, hi), X("G", lo, hi), -XO, ALU.add)
        else:
            act(X("G", lo, hi), sub(R, lo, hi), bias=-1.5 * XO)
            ts(X("reci", lo, hi), X("G", lo, hi), 0.5 * XO, ALU.add, 9.0, ALU.min)
        dma("y", T.yr[:, lo:hi], X("reci", lo, hi), 131072)
    ts(X("ylo"), X("VL", 0, 512), 1.5 * 2 ** 23 - VO, ALU.add, -1.5 * 2 ** 23, ALU.add)
    dma("y", T.yl[:], X("ylo"), 262144)
    for k in range(16):
        mm(X("P0", k, 128, 16), sub(SU, 128 * k, 128 * k + 128), X("col", 24, 32), True, True)
    act(X("yso", 0, 128), X("P0", 0, 128), bias=32768.0)
    mm(X("P2", 0, 128), X("yso", 0, 128), idf, True, True)
    act(X("yso", 128, 256), X("P2", 0, 128))
    dma("s", T.ys[:], X("yso", 128, 256), 65536)
    lst = part(NT - 1, 2)[0]
    cp(X("vf"), sub(lst, 32, 48))
    x = X("xx", 256 * (NT % 2), 256 * (NT % 2) + 256)
    act(x, by(X("land", (NT - 1) * SW, NT * SW), sub(lst, 16, 32)), bias=-XO)
    dma("s", T.yx[:], x, 65536)
    unwrap(X("P1", 0, 256), "selT", X("vf"))
    cp(X("suc"), X("P1", 0, 256))
    op("y", lambda: g.sync.dma_start(T.yv[:], T.suc[0:128:16, :]), [X("suc")], [], (100.0, 2000.0), "d")
    emit(g, T, ops)
    g.wait_ge(T.sem.sent, nsent[0])
